import numpy as np
import ml_dtypes


def mxq(x, axis, fmt="e4m3"):
    dtype, down = {"e4m3": (ml_dtypes.float8_e4m3fn, 7), "e5m2": (ml_dtypes.float8_e5m2, 14)}[fmt]
    v = np.moveaxis(np.asarray(x, np.float32).astype(ml_dtypes.bfloat16).astype(np.float64), axis, -1)
    blocks = v.reshape(v.shape[:-1] + (-1, 32))
    amax = np.abs(blocks).max(-1, keepdims=True)
    byte = np.maximum(np.where(amax > 0, np.frexp(amax)[1] - 1 + 127, 0) - down, 1)
    scale = np.exp2(byte - 127.0)
    codes = (blocks / scale).astype(np.float32).astype(dtype).astype(np.float64)
    return np.moveaxis((codes * scale).reshape(v.shape), -1, axis)


WIDE = False


def mx_kscale(k):
    if not WIDE:
        return np.ones(k)
    levels = np.array([24, -24, 12, -12, 0])
    if k % 512:
        return np.exp2(np.random.permutation(np.resize(levels, k // 32))).repeat(32)
    a = np.empty((k // 512, 16))
    for p in range(k // 512):
        a[p, :8] = np.random.permutation(np.resize(levels, 8))
        for g in range(8):
            far = levels[np.abs(levels - a[p, g]) >= 10]
            a[p, g + 8] = far[np.random.randint(len(far))]
    return np.exp2(a.ravel()).repeat(32)


def f64(x):
    return np.asarray(x).astype(np.float64)


def striped8(idx):
    return np.concatenate([v.reshape(-1, 16).T for v in idx]).astype(np.uint16)


def unstriped8(offs):
    return np.stack([offs[16 * g:16 * g + 16].T.reshape(-1) for g in range(8)]).astype(np.int64)


E2M1 = np.array([0.0, 0.5, 1.0, 1.5, 2.0, 3.0, 4.0, 6.0, -0.0, -0.5, -1.0, -1.5, -2.0, -3.0, -4.0, -6.0])


def pack_weight(w, fmt):
    k, n = w.shape
    w = f64(np.asarray(w, np.float32).astype(ml_dtypes.bfloat16)).reshape(k // 32, 32, n)
    amax = np.abs(w).max(1)
    if fmt == "e4m3":
        byte = np.frexp(amax)[1] - 1 + 127 - 7
    else:
        mant, ex = np.frexp(amax / 6.0)
        byte = np.where(mant > 0.5, ex, ex - 1) + 127
    byte = np.clip(np.where(amax > 0, byte, 1), 1, 254)
    scaled = (w * np.exp2(127.0 - byte)[:, None, :]).reshape(k, n).astype(np.float32)
    by_word = np.ascontiguousarray(scaled.reshape(k // 512, 128, 4, n).transpose(0, 1, 3, 2))
    if fmt == "e4m3":
        words = by_word.astype(ml_dtypes.float8_e4m3fn).view(np.uint8)
    else:
        c = by_word.astype(ml_dtypes.float4_e2m1fn).view(np.uint8) & 0xF
        words = (c[..., 0::2] | (c[..., 1::2] << 4)).reshape(k // 512, 128, 2 * n)
    return np.ascontiguousarray(words), np.ascontiguousarray(byte.astype(np.uint8).reshape(k // 512, 16, n))


def unpack_weight(words, scales, fmt):
    g, _, n = scales.shape
    words = np.ascontiguousarray(words).reshape(g, 128, n, -1)
    if fmt == "e4m3":
        vals = words.view(ml_dtypes.float8_e4m3fn).astype(np.float64)
    else:
        nib = np.empty((g, 128, n, 4), np.uint8)
        nib[..., 0::2] = words & 0xF
        nib[..., 1::2] = words >> 4
        vals = E2M1[nib]
    vals = vals * np.repeat(np.exp2(scales.astype(np.float64) - 127.0), 8, axis=1)[..., None]
    return vals.transpose(0, 1, 3, 2).reshape(g * 512, n)


def silu(f):
    return f / (1.0 + np.exp(-np.maximum(f, -700.0)))


K, N, T, J = 1024, 512, 2048, 1024


def setup_inputs():
    n = np.random.standard_normal
    s = mx_kscale(K)[:, None]
    p_wk = pack_weight(n((K, N)) / np.sqrt(K) / s, "e4m3")
    p_wv = pack_weight(n((K, N)) / np.sqrt(K) / s, "e2m1")
    return {
        "xT": (n((K, T)) * s).astype(np.float32),
        "wgt": np.repeat(np.random.uniform(0.5, 2.0, (8, J)), 16, axis=0).astype(np.float32),
        "wk_words": p_wk[0],
        "wk_scales": p_wk[1],
        "wv_words": p_wv[0],
        "wv_scales": p_wv[1],
        "st": (n((N, J))).astype(np.float32),
        "wgo": np.repeat(np.random.uniform(0.5, 2.0, (8, J)), 16, axis=0).astype(np.float32),
        "offs": striped8(np.stack([np.random.permutation(T)[:J] for _ in range(8)])),
        "offs2": striped8(np.stack([np.random.permutation(T)[:J] for _ in range(8)])),
    }


def reference(xT, wgt, wk_words, wk_scales, wv_words, wv_scales, st, wgo, offs, offs2):
    idx = unstriped8(offs)
    idx2 = unstriped8(offs2)
    rows = np.arange(K)
    xg = f64(wgt)[rows // 4 % 128] * f64(xT)[rows[:, None], idx[rows % 512 // 64]]
    xT_ = mxq(xg, 0, "e4m3")
    wk_ = unpack_weight(wk_words, wk_scales, "e4m3")
    wv_ = unpack_weight(wv_words, wv_scales, "e2m1")
    ke = wk_.T @ xT_
    ve = wv_.T @ xT_
    gate = silu(ke * f64(st))
    out = np.zeros((N, T))
    rows = np.arange(N)
    out[rows[:, None], idx2[rows % 128 // 16]] = f64(wgo)[rows % 128] * (gate * ve)
    return out

@@ -1,0 +1,234 @@
+from contextlib import ExitStack
+
+import concourse.mybir as mybir
+from concourse.masks import make_identity
+
+K, N, T, J = 1024, 512, 2048, 1024
+FLOPS = 2 * 2 * K * N * J
+
+F32 = mybir.dt.float32
+BF16 = mybir.dt.bfloat16
+I32 = mybir.dt.int32
+U32 = mybir.dt.uint32
+U16 = mybir.dt.uint16
+U8 = mybir.dt.uint8
+FP8X4 = mybir.dt.float8_e4m3fn_x4
+FP4X4 = mybir.dt.float4_e2m1fn_x4
+MULT = mybir.AluOpType.mult
+SILU = mybir.ActivationFunctionType.Silu
+COPY = mybir.ActivationFunctionType.Copy
+
+P = 128
+PACK = 4
+PASSES = K // (P * PACK)
+HALF = 512
+HALVES = J // HALF
+ROW_TILES = N // P
+GROUPS = 8
+GROUP = P // GROUPS
+J_TILES = HALF // P
+LIST_COLS = HALF // GROUP
+DIRECT = 2
+
+
+def tile_list_siluS_kernel(
+    tc, xT, wgt, wk_words, wk_scales, wv_words, wv_scales, st, wgo, offs, offs2, out
+):
+    nc = tc.nc
+    with ExitStack() as ctx:
+        keep = ctx.enter_context(tc.tile_pool(name="keep", bufs=1))
+        ring = ctx.enter_context(tc.tile_pool(name="ring", bufs=3))
+        psum_k = ctx.enter_context(tc.psum_pool(name="psum_k", bufs=3))
+        psum_v = ctx.enter_context(tc.psum_pool(name="psum_v", bufs=3))
+        psum_t = ctx.enter_context(tc.psum_pool(name="psum_t", bufs=2))
+
+        def half_cols(h):
+            return slice(h * HALF, (h + 1) * HALF)
+
+        def list_cols(h):
+            return slice(h * LIST_COLS, (h + 1) * LIST_COLS)
+
+        pick = keep.tile([P, J // GROUP], U16, name="pick")
+        place = keep.tile([P, J // GROUP], U16, name="place")
+        wgt_sb = [keep.tile([P, HALF], F32, name=f"wgt{h}") for h in range(HALVES)]
+        planes = [keep.tile([P, T], F32, name=f"plane{q}") for q in range(PASSES * PACK)]
+        wk_codes = keep.tile([P, PASSES, N], U32, name="wk_codes", align_bytes=64)
+        wv_codes = keep.tile([P, PASSES, 2 * N], U8, name="wv_codes", align_bytes=64)
+        wk_sc = keep.tile([P, PASSES, N], U8, name="wk_sc", align_bytes=64)
+        wv_sc = keep.tile([P, PASSES, N], U8, name="wv_sc", align_bytes=64)
+        st_sb = {(h, r): keep.tile([P, HALF], F32, name=f"st{h}{r}") for h in range(HALVES) for r in range(ROW_TILES)}
+        wgo_sb = keep.tile([P, HALF], F32, name="wgo_sb")
+        wgo_rows = keep.tile([P, P], F32, name="wgo_rows")
+        wgo_t = keep.tile([P, P], F32, name="wgo_t")
+        ident = keep.tile([P, P], F32, name="ident")
+        windows = [keep.tile([P, T], F32, name=f"window{r}") for r in range(ROW_TILES)]
+        warm = keep.tile([P, 8], F32, name="warm")
+
+        nc.vector.memset(wk_sc[:].bitcast(I32), 0)
+        nc.vector.memset(wv_sc[:].bitcast(I32), 0)
+        nc.vector.memset(warm[:], 0.0)
+        nc.scalar.activation(warm[:, 1:2], warm[:, 0:1], SILU)
+        make_identity(nc, ident[:])
+        for r in range(ROW_TILES):
+            nc.gpsimd.memset(windows[r][:], 0.0)
+
+        def load_scale_rows(tile, scales, quad):
+            nc.sync.dma_start(
+                out=tile[32 * quad : 32 * quad + 4, :, :].bitcast(I32),
+                in_=scales[:, 4 * quad : 4 * quad + 4, :].rearrange("a q n -> q a n").bitcast(I32),
+            )
+
+        scale_loads = [(wk_sc, wk_scales, quad) for quad in range(4)] + [(wv_sc, wv_scales, quad) for quad in range(4)]
+        nc.sync.dma_start(pick[:], offs)
+        nc.sync.dma_start(out=wgt_sb[0][:], in_=wgt[:, half_cols(0)])
+        x_rows = xT.rearrange("(a p i) t -> p a i t", a=PASSES, i=PACK)
+        for q in range(PASSES * PACK):
+            nc.sync.dma_start(out=planes[q][:], in_=x_rows[:, q // PACK, q % PACK, :])
+            if q == 0:
+                nc.sync.dma_start(out=wgt_sb[1][:], in_=wgt[:, half_cols(1)])
+            load_scale_rows(*scale_loads[q])
+        nc.sync.dma_start(out=wk_codes[:].bitcast(I32), in_=wk_words.rearrange("a p n t -> p a (n t)").bitcast(I32))
+        nc.sync.dma_start(out=wv_codes[:].bitcast(I32), in_=wv_words.rearrange("a p b -> p a b").bitcast(I32))
+        nc.sync.dma_start(out=st_sb[0, 0][:], in_=st[0:P, half_cols(0)])
+        nc.sync.dma_start(out=wgo_sb[:], in_=wgo[:, half_cols(0)])
+        nc.sync.dma_start(place[:], offs2)
+        nc.sync.dma_start(
+            out=wgo_rows[:],
+            in_=wgo.rearrange("(g s r) j -> g s (r j)", g=GROUPS, r=2)[:, 0, :].rearrange("g (u c) -> g u c", c=P),
+        )
+        for h in range(HALVES):
+            for r in range(ROW_TILES):
+                if (h, r) != (0, 0):
+                    nc.sync.dma_start(out=st_sb[h, r][:], in_=st[r * P : (r + 1) * P, half_cols(h)])
+
+        x_codes = {}
+        x_sc = {}
+
+        def quantise_half(h):
+            for a in range(PASSES):
+                picked = keep.tile([P, PACK, HALF], F32, name=f"picked{h}{a}")
+                for i in range(PACK):
+                    nc.vector.tensor_tensor(
+                        picked[:, i, :], planes[a * PACK + i][:].indirect(pick[:, list_cols(h)]), wgt_sb[h][:], MULT
+                    )
+                grouped = keep.tile([P, HALF, PACK], BF16, name=f"grouped{h}{a}", align_bytes=64)
+                nc.scalar.copy(
+                    grouped[:].rearrange("p (c u) i -> p c i u", u=4),
+                    picked[:].rearrange("p i (c u) -> p c i u", u=4),
+                )
+                x_codes[h, a] = keep.tile([P, HALF], U32, name=f"x_codes{h}{a}", align_bytes=64)
+                x_sc[h, a] = keep.tile([P, HALF], U8, name=f"x_sc{h}{a}", align_bytes=64)
+                nc.vector.quantize_mx(
+                    out=x_codes[h, a][:].bitcast(FP8X4),
+                    scales=x_sc[h, a][:],
+                    in_=grouped[:].rearrange("p c i -> p (c i)"),
+                )
+
+        gates = {}
+        values = {}
+        scaled = {}
+
+        def make_gate(h, r):
+            rows = slice(r * P, (r + 1) * P)
+            ke = psum_k.tile([P, HALF], F32, name="ke")
+            for a in range(PASSES):
+                nc.tensor.matmul_mx(
+                    out=ke[:],
+                    lhsT=wk_codes[:, a, rows].bitcast(FP8X4),
+                    lhsT_scale=wk_sc[:, a, rows],
+                    rhs=x_codes[h, a][:].bitcast(FP8X4),
+                    rhs_scale=x_sc[h, a][:],
+                    start=(a == 0),
+                    stop=(a == PASSES - 1),
+                )
+            match = ring.tile([P, HALF], F32, name="match")
+            nc.vector.tensor_tensor(match[:], ke[:], st_sb[h, r][:], MULT)
+            gates[h, r] = ring.tile([P, HALF], F32, name="gate")
+            nc.scalar.activation(gates[h, r][:], match[:], SILU)
+
+        def values_direct(h, r):
+            rows = slice(r * P, (r + 1) * P)
+            ve = psum_v.tile([P, HALF], F32, name="ve")
+            for a in range(PASSES):
+                nc.tensor.matmul_mx(
+                    out=ve[:],
+                    lhsT=wv_codes[:, a, 2 * r * P : 2 * (r + 1) * P].bitcast(FP4X4),
+                    lhsT_scale=wv_sc[:, a, rows],
+                    rhs=x_codes[h, a][:].bitcast(FP8X4),
+                    rhs_scale=x_sc[h, a][:],
+                    start=(a == 0),
+                    stop=(a == PASSES - 1),
+                )
+            values[h, r] = ring.tile([P, HALF], F32, name="value")
+            nc.vector.tensor_tensor(values[h, r][:], ve[:], wgo_sb[:], MULT)
+
+        def transpose_wgo():
+            turned = psum_t.tile([P, HALF], F32, name="turned")
+            nc.tensor.transpose(turned[:, 0:P], wgo_rows[:], ident[:])
+            nc.scalar.copy(wgo_t[:], turned[:, 0:P])
+
+        def values_by_token(h, first):
+            width = (ROW_TILES - first) * P
+            spans = [slice(0, N)] if first == 0 else [slice(r * P, (r + 1) * P) for r in range(first, ROW_TILES)]
+            for jt in range(J_TILES):
+                tokens = slice(jt * P, (jt + 1) * P)
+                ve = psum_v.tile([P, HALF], F32, name="ve")
+                for span in spans:
+                    for step, a in enumerate(reversed(range(PASSES))):
+                        nc.tensor.matmul_mx(
+                            out=ve[:, span.start - first * P : span.stop - first * P],
+                            lhsT=x_codes[h, a][:, tokens].bitcast(FP8X4),
+                            lhsT_scale=x_sc[h, a][:, tokens],
+                            rhs=wv_codes[:, a, 2 * span.start : 2 * span.stop].bitcast(FP4X4),
+                            rhs_scale=wv_sc[:, a, span],
+                            start=(step == 0),
+                            stop=(step == PASSES - 1),
+                        )
+                scaled[h, jt] = keep.tile([P, width], F32, name=f"scaled{h}{jt}")
+                for g in range(GROUPS):
+                    col = g * GROUP + h * J_TILES + jt
+                    nc.scalar.activation(
+                        scaled[h, jt][:].rearrange("p (r g c) -> p r g c", g=GROUPS, c=GROUP)[:, :, g, :],
+                        ve[:, 0:width].rearrange("p (r g c) -> p r g c", g=GROUPS, c=GROUP)[:, :, g, :],
+                        COPY,
+                        scale=wgo_t[:, col : col + 1],
+                    )
+
+        def values_turned(h, r, first):
+            turned = psum_t.tile([P, HALF], F32, name="turned")
+            for jt in range(J_TILES):
+                nc.tensor.transpose(
+                    turned[:, jt * P : (jt + 1) * P], scaled[h, jt][:, (r - first) * P : (r - first + 1) * P], ident[:]
+                )
+            values[h, r] = ring.tile([P, HALF], F32, name="value")
+            nc.scalar.copy(values[h, r][:], turned[:])
+
+        def scatter(h, r):
+            nc.vector.tensor_tensor(
+                windows[r][:].indirect(place[:, list_cols(h)]), gates[h, r][:], values[h, r][:], MULT
+            )
+            if h == HALVES - 1:
+                nc.sync.dma_start(out=out[r * P : (r + 1) * P, :], in_=windows[r][:])
+
+        units = [(h, r) for h in range(HALVES) for r in range(ROW_TILES)]
+
+        def prepare(h, r):
+            make_gate(h, r)
+            if h == 0 and r < DIRECT:
+                values_direct(h, r)
+            else:
+                values_turned(h, r, DIRECT if h == 0 else 0)
+
+        quantise_half(0)
+        transpose_wgo()
+        prepare(*units[0])
+        for u, unit in enumerate(units):
+            if u + 1 < len(units):
+                prepare(*units[u + 1])
+            if u == 0:
+                values_by_token(0, DIRECT)
+            scatter(*unit)
+            if u == 0:
+                quantise_half(1)
+            if u == 1:
+                values_by_token(1, 0)

@@ -50,8 +50,8 @@ def tile_list_siluS_kernel(
 
         pick = keep.tile([P, J // GROUP], U16, name="pick")
         place = keep.tile([P, J // GROUP], U16, name="place")
-        wgt_sb = [keep.tile([P, HALF], F32, name=f"wgt{h}") for h in range(HALVES)]
-        planes = [keep.tile([P, T], F32, name=f"plane{q}") for q in range(PASSES * PACK)]
+        wgt_sb = [keep.tile([P, HALF], F32, name=f"wgt{h}", tag=f"wgt{h}") for h in range(HALVES)]
+        planes = [keep.tile([P, T], F32, name=f"plane{q}", tag=f"plane{q}", align_bytes=64) for q in range(PASSES * PACK)]
         wk_codes = keep.tile([P, PASSES, N], U32, name="wk_codes", align_bytes=64)
         wv_codes = keep.tile([P, PASSES, 2 * N], U8, name="wv_codes", align_bytes=64)
         wk_sc = keep.tile([P, PASSES, N], U8, name="wk_sc", align_bytes=64)
@@ -64,9 +64,9 @@ def tile_list_siluS_kernel(
         windows = [keep.tile([P, T], F32, name=f"window{r}") for r in range(ROW_TILES)]
         warm = keep.tile([P, 8], F32, name="warm")
 
-        nc.vector.memset(wk_sc[:].bitcast(I32), 0)
-        nc.vector.memset(wv_sc[:].bitcast(I32), 0)
-        nc.vector.memset(warm[:], 0.0)
+        nc.gpsimd.memset(wk_sc[:].bitcast(I32), 0)
+        nc.gpsimd.memset(wv_sc[:].bitcast(I32), 0)
+        nc.gpsimd.memset(warm[:], 0.0)
         nc.scalar.activation(warm[:, 1:2], warm[:, 0:1], SILU)
         make_identity(nc, ident[:])
         for r in range(ROW_TILES):
@@ -106,17 +106,27 @@ def tile_list_siluS_kernel(
 
         def quantise_half(h):
             for a in range(PASSES):
-                picked = keep.tile([P, PACK, HALF], F32, name=f"picked{h}{a}")
-                for i in range(PACK):
-                    nc.vector.tensor_tensor(
-                        picked[:, i, :], planes[a * PACK + i][:].indirect(pick[:, list_cols(h)]), wgt_sb[h][:], MULT
-                    )
-                grouped = keep.tile([P, HALF, PACK], BF16, name=f"grouped{h}{a}", align_bytes=64)
-                nc.scalar.copy(
-                    grouped[:].rearrange("p (c u) i -> p c i u", u=4),
-                    picked[:].rearrange("p i (c u) -> p c i u", u=4),
-                )
-                x_codes[h, a] = keep.tile([P, HALF], U32, name=f"x_codes{h}{a}", align_bytes=64)
+                last = (h, a) == (HALVES - 1, PASSES - 1)
+                runs = [(0, 2, "picked_early"), (2, 4, "wgt0")] if last else [(0, PACK, f"picked{h}{a}")]
+                grouped = keep.tile([P, HALF, PACK], BF16, name=f"grouped{h}{a}", tag=f"grouped{h}{a}", align_bytes=64)
+                for lo, hi, tag in runs:
+                    picked = keep.tile([P, hi - lo, HALF], F32, name=f"picked{h}{a}{lo}", tag=tag)
+                    for i in range(lo, hi):
+                        nc.vector.tensor_tensor(
+                            picked[:, i - lo, :],
+                            planes[a * PACK + i][:].indirect(pick[:, list_cols(h)]),
+                            wgt_sb[h][:],
+                            MULT,
+                        )
+                    if last:
+                        nc.scalar.copy(grouped[:, :, lo:hi], picked[:].rearrange("p i c -> p c i"))
+                    else:
+                        nc.scalar.copy(
+                            grouped[:].rearrange("p (c u) i -> p c i u", u=4),
+                            picked[:].rearrange("p i (c u) -> p c i u", u=4),
+                        )
+                codes_tag = {(0, 0): "plane4", (1, 0): "grouped01"}.get((h, a), f"x_codes{h}{a}")
+                x_codes[h, a] = keep.tile([P, HALF], U32, name=f"x_codes{h}{a}", tag=codes_tag, align_bytes=64)
                 x_sc[h, a] = keep.tile([P, HALF], U8, name=f"x_sc{h}{a}", align_bytes=64)
                 nc.vector.quantize_mx(
                     out=x_codes[h, a][:].bitcast(FP8X4),
@@ -128,9 +138,13 @@ def tile_list_siluS_kernel(
         values = {}
         scaled = {}
 
-        def make_gate(h, r):
+        keys = {}
+        sums = {}
+
+        def make_keys(h, r):
             rows = slice(r * P, (r + 1) * P)
             ke = psum_k.tile([P, HALF], F32, name="ke")
+            keys[h, r] = ke
             for a in range(PASSES):
                 nc.tensor.matmul_mx(
                     out=ke[:],
@@ -141,14 +155,17 @@ def tile_list_siluS_kernel(
                     start=(a == 0),
                     stop=(a == PASSES - 1),
                 )
+
+        def make_gate(h, r):
             match = ring.tile([P, HALF], F32, name="match")
-            nc.vector.tensor_tensor(match[:], ke[:], st_sb[h, r][:], MULT)
+            nc.vector.tensor_tensor(match[:], keys[h, r][:], st_sb[h, r][:], MULT)
             gates[h, r] = ring.tile([P, HALF], F32, name="gate")
             nc.scalar.activation(gates[h, r][:], match[:], SILU)
 
-        def values_direct(h, r):
+        def sums_direct(h, r):
             rows = slice(r * P, (r + 1) * P)
             ve = psum_v.tile([P, HALF], F32, name="ve")
+            sums[h, r] = ve
             for a in range(PASSES):
                 nc.tensor.matmul_mx(
                     out=ve[:],
@@ -159,8 +176,10 @@ def tile_list_siluS_kernel(
                     start=(a == 0),
                     stop=(a == PASSES - 1),
                 )
+
+        def values_direct(h, r):
             values[h, r] = ring.tile([P, HALF], F32, name="value")
-            nc.vector.tensor_tensor(values[h, r][:], ve[:], wgo_sb[:], MULT)
+            nc.vector.tensor_tensor(values[h, r][:], sums[h, r][:], wgo_sb[:], MULT)
 
         def transpose_wgo():
             turned = psum_t.tile([P, HALF], F32, name="turned")
@@ -170,29 +189,31 @@ def tile_list_siluS_kernel(
         def values_by_token(h, first):
             width = (ROW_TILES - first) * P
             spans = [slice(0, N)] if first == 0 else [slice(r * P, (r + 1) * P) for r in range(first, ROW_TILES)]
-            for jt in range(J_TILES):
-                tokens = slice(jt * P, (jt + 1) * P)
-                ve = psum_v.tile([P, HALF], F32, name="ve")
-                for span in spans:
-                    for step, a in enumerate(reversed(range(PASSES))):
-                        nc.tensor.matmul_mx(
-                            out=ve[:, span.start - first * P : span.stop - first * P],
-                            lhsT=x_codes[h, a][:, tokens].bitcast(FP8X4),
-                            lhsT_scale=x_sc[h, a][:, tokens],
-                            rhs=wv_codes[:, a, 2 * span.start : 2 * span.stop].bitcast(FP4X4),
-                            rhs_scale=wv_sc[:, a, span],
-                            start=(step == 0),
-                            stop=(step == PASSES - 1),
-                        )
-                scaled[h, jt] = keep.tile([P, width], F32, name=f"scaled{h}{jt}")
-                for g in range(GROUPS):
-                    col = g * GROUP + h * J_TILES + jt
-                    nc.scalar.activation(
-                        scaled[h, jt][:].rearrange("p (r g c) -> p r g c", g=GROUPS, c=GROUP)[:, :, g, :],
-                        ve[:, 0:width].rearrange("p (r g c) -> p r g c", g=GROUPS, c=GROUP)[:, :, g, :],
-                        COPY,
-                        scale=wgo_t[:, col : col + 1],
-                    )
+            per_bank = HALF // width
+            for jt0 in range(0, J_TILES, per_bank):
+                bank = psum_v.tile([P, HALF], F32, name="ve")
+                for slot in range(per_bank):
+                    tokens = slice((jt0 + slot) * P, (jt0 + slot + 1) * P)
+                    shift = slot * width - first * P
+                    for span in spans:
+                        for step, a in enumerate(reversed(range(PASSES))):
+                            nc.tensor.matmul_mx(
+                                out=bank[:, span.start + shift : span.stop + shift],
+                                lhsT=x_codes[h, a][:, tokens].bitcast(FP8X4),
+                                lhsT_scale=x_sc[h, a][:, tokens],
+                                rhs=wv_codes[:, a, 2 * span.start : 2 * span.stop].bitcast(FP4X4),
+                                rhs_scale=wv_sc[:, a, span],
+                                start=(step == 0),
+                                stop=(step == PASSES - 1),
+                            )
+                for slot in range(per_bank):
+                    jt = jt0 + slot
+                    scaled[h, jt] = keep.tile([P, width], F32, name=f"scaled{h}{jt}")
+                    src = bank[:, slot * width : (slot + 1) * width].rearrange("p (r g c) -> p r g c", g=GROUPS, c=GROUP)
+                    dst = scaled[h, jt][:].rearrange("p (r g c) -> p r g c", g=GROUPS, c=GROUP)
+                    for g in range(GROUPS):
+                        col = g * GROUP + h * J_TILES + jt
+                        nc.scalar.activation(dst[:, :, g, :], src[:, :, g, :], COPY, scale=wgo_t[:, col : col + 1])
 
         def values_turned(h, r, first):
             turned = psum_t.tile([P, HALF], F32, name="turned")
@@ -212,23 +233,24 @@ def tile_list_siluS_kernel(
 
         units = [(h, r) for h in range(HALVES) for r in range(ROW_TILES)]
 
-        def prepare(h, r):
-            make_gate(h, r)
-            if h == 0 and r < DIRECT:
-                values_direct(h, r)
-            else:
-                values_turned(h, r, DIRECT if h == 0 else 0)
-
         quantise_half(0)
         transpose_wgo()
-        prepare(*units[0])
+        for r in range(DIRECT):
+            make_keys(0, r)
+            sums_direct(0, r)
+        make_keys(0, DIRECT)
+        for r in range(DIRECT):
+            make_gate(0, r)
+            values_direct(0, r)
+        quantise_half(1)
+        values_by_token(0, DIRECT)
         for u, unit in enumerate(units):
-            if u + 1 < len(units):
-                prepare(*units[u + 1])
-            if u == 0:
-                values_by_token(0, DIRECT)
+            if u + 3 < len(units):
+                make_keys(*units[u + 3])
             scatter(*unit)
-            if u == 0:
-                quantise_half(1)
+            if u + 2 < len(units):
+                h, r = units[u + 2]
+                make_gate(h, r)
+                values_turned(h, r, DIRECT if h == 0 else 0)
             if u == 1:
                 values_by_token(1, 0)

@@ -70,18 +70,16 @@ def tile_list_siluS_kernel(
         nc.scalar.activation(warm[:, 1:2], warm[:, 0:1], SILU)
         make_identity(nc, ident[:])
         for r in range(ROW_TILES):
-            nc.gpsimd.memset(windows[r][:], 0.0)
+            nc.vector.memset(windows[r][:].bitcast(I32), 0)
 
-        def load_scale_rows(tile, scales, quad):
-            nc.sync.dma_start(
-                out=tile[32 * quad : 32 * quad + 4, :, :].bitcast(I32),
-                in_=scales[:, 4 * quad : 4 * quad + 4, :].rearrange("a q n -> q a n").bitcast(I32),
-            )
+        def load_scale_rows(tile, scales, r):
+            rows = scales.rearrange("a (q r) n -> r q a n", r=4)
+            nc.sync.dma_start(out=tile[r:P:32, :, :].bitcast(I32), in_=rows[r].bitcast(I32))
 
-        scale_loads = [(wk_sc, wk_scales, quad) for quad in range(4)] + [(wv_sc, wv_scales, quad) for quad in range(4)]
         nc.sync.dma_start(pick[:], offs)
         nc.sync.dma_start(out=wgt_sb[0][:], in_=wgt[:, half_cols(0)])
         x_rows = xT.rearrange("(a p i) t -> p a i t", a=PASSES, i=PACK)
+        scale_loads = [(wk_sc, wk_scales, r) for r in range(4)] + [(wv_sc, wv_scales, r) for r in range(4)]
         for q in range(PASSES * PACK):
             nc.sync.dma_start(out=planes[q][:], in_=x_rows[:, q // PACK, q % PACK, :])
             if q == 0:
@@ -91,6 +89,7 @@ def tile_list_siluS_kernel(
         nc.sync.dma_start(out=wv_codes[:].bitcast(I32), in_=wv_words.rearrange("a p b -> p a b").bitcast(I32))
         nc.sync.dma_start(out=st_sb[0, 0][:], in_=st[0:P, half_cols(0)])
         nc.sync.dma_start(out=wgo_sb[:], in_=wgo[:, half_cols(0)])
+        nc.sync.dma_start(out=st_sb[0, 1][:], in_=st[P : 2 * P, half_cols(0)])
         nc.sync.dma_start(place[:], offs2)
         nc.sync.dma_start(
             out=wgo_rows[:],
@@ -98,41 +97,50 @@ def tile_list_siluS_kernel(
         )
         for h in range(HALVES):
             for r in range(ROW_TILES):
-                if (h, r) != (0, 0):
+                if (h, r) > (0, 1):
                     nc.sync.dma_start(out=st_sb[h, r][:], in_=st[r * P : (r + 1) * P, half_cols(h)])
 
+        picked = {
+            (0, 0): keep.tile([P, PACK, HALF], F32, name="picked00"),
+            (0, 1): keep.tile([P, PACK, HALF], F32, name="picked01"),
+            (1, 0): keep.tile([P, PACK, HALF], F32, name="picked10"),
+        }
+        pairs = [
+            keep.tile([P, 2, HALF], F32, name="pair_early"),
+            keep.tile([P, 2, HALF], F32, name="pair_late", tag="wgt0"),
+        ]
+        grouped = {
+            (h, a): keep.tile([P, HALF, PACK], BF16, name=f"grouped{h}{a}", tag=f"grouped{h}{a}", align_bytes=64)
+            for h in range(HALVES)
+            for a in range(PASSES)
+        }
+        codes_tags = {(0, 0): "plane4", (0, 1): "x_codes01", (1, 0): "grouped01", (1, 1): "x_codes11"}
         x_codes = {}
         x_sc = {}
 
-        def quantise_half(h):
-            for a in range(PASSES):
-                last = (h, a) == (HALVES - 1, PASSES - 1)
-                runs = [(0, 2, "picked_early"), (2, 4, "wgt0")] if last else [(0, PACK, f"picked{h}{a}")]
-                grouped = keep.tile([P, HALF, PACK], BF16, name=f"grouped{h}{a}", tag=f"grouped{h}{a}", align_bytes=64)
-                for lo, hi, tag in runs:
-                    picked = keep.tile([P, hi - lo, HALF], F32, name=f"picked{h}{a}{lo}", tag=tag)
-                    for i in range(lo, hi):
-                        nc.vector.tensor_tensor(
-                            picked[:, i - lo, :],
-                            planes[a * PACK + i][:].indirect(pick[:, list_cols(h)]),
-                            wgt_sb[h][:],
-                            MULT,
-                        )
-                    if last:
-                        nc.scalar.copy(grouped[:, :, lo:hi], picked[:].rearrange("p i c -> p c i"))
-                    else:
-                        nc.scalar.copy(
-                            grouped[:].rearrange("p (c u) i -> p c i u", u=4),
-                            picked[:].rearrange("p i (c u) -> p c i u", u=4),
-                        )
-                codes_tag = {(0, 0): "plane4", (1, 0): "grouped01"}.get((h, a), f"x_codes{h}{a}")
-                x_codes[h, a] = keep.tile([P, HALF], U32, name=f"x_codes{h}{a}", tag=codes_tag, align_bytes=64)
-                x_sc[h, a] = keep.tile([P, HALF], U8, name=f"x_sc{h}{a}", align_bytes=64)
-                nc.vector.quantize_mx(
-                    out=x_codes[h, a][:].bitcast(FP8X4),
-                    scales=x_sc[h, a][:],
-                    in_=grouped[:].rearrange("p c i -> p (c i)"),
-                )
+        def gather(h, q, cols=slice(0, HALF)):
+            a, i = divmod(q, PACK)
+            dst = picked[h, a][:, i, cols] if (h, a) in picked else pairs[i // 2][:, i % 2, cols]
+            entries = pick[:, (h * HALF + cols.start) // GROUP : (h * HALF + cols.stop) // GROUP]
+            nc.vector.tensor_tensor(dst, planes[q][:].indirect(entries), wgt_sb[h][:, cols], MULT)
+
+        def interleave(h, a, cols=slice(0, HALF)):
+            nc.scalar.copy(
+                grouped[h, a][:, cols, :].rearrange("p (c u) i -> p c i u", u=4),
+                picked[h, a][:, :, cols].rearrange("p i (c u) -> p c i u", u=4),
+            )
+
+        def interleave_pair(n):
+            nc.scalar.copy(grouped[1, 1][:, :, 2 * n : 2 * n + 2], pairs[n][:].rearrange("p i c -> p c i"))
+
+        def quantise(h, a):
+            x_codes[h, a] = keep.tile([P, HALF], U32, name=f"x_codes{h}{a}", tag=codes_tags[h, a], align_bytes=64)
+            x_sc[h, a] = keep.tile([P, HALF], U8, name=f"x_sc{h}{a}", align_bytes=64)
+            nc.vector.quantize_mx(
+                out=x_codes[h, a][:].bitcast(FP8X4),
+                scales=x_sc[h, a][:],
+                in_=grouped[h, a][:].rearrange("p c i -> p (c i)"),
+            )
 
         gates = {}
         values = {}
@@ -141,11 +149,12 @@ def tile_list_siluS_kernel(
         keys = {}
         sums = {}
 
-        def make_keys(h, r):
+        def make_keys(h, r, passes=range(PASSES)):
             rows = slice(r * P, (r + 1) * P)
-            ke = psum_k.tile([P, HALF], F32, name="ke")
-            keys[h, r] = ke
-            for a in range(PASSES):
+            if passes[0] == 0:
+                keys[h, r] = psum_k.tile([P, HALF], F32, name="ke")
+            ke = keys[h, r]
+            for a in passes:
                 nc.tensor.matmul_mx(
                     out=ke[:],
                     lhsT=wk_codes[:, a, rows].bitcast(FP8X4),
@@ -162,11 +171,12 @@ def tile_list_siluS_kernel(
             gates[h, r] = ring.tile([P, HALF], F32, name="gate")
             nc.scalar.activation(gates[h, r][:], match[:], SILU)
 
-        def sums_direct(h, r):
+        def sums_direct(h, r, passes):
             rows = slice(r * P, (r + 1) * P)
-            ve = psum_v.tile([P, HALF], F32, name="ve")
-            sums[h, r] = ve
-            for a in range(PASSES):
+            if passes[0] == 0:
+                sums[h, r] = psum_v.tile([P, HALF], F32, name="ve")
+            ve = sums[h, r]
+            for a in passes:
                 nc.tensor.matmul_mx(
                     out=ve[:],
                     lhsT=wv_codes[:, a, 2 * r * P : 2 * (r + 1) * P].bitcast(FP4X4),
@@ -233,16 +243,36 @@ def tile_list_siluS_kernel(
 
         units = [(h, r) for h in range(HALVES) for r in range(ROW_TILES)]
 
-        quantise_half(0)
+        for q in range(PACK):
+            gather(0, q)
+            gather(1, q)
+        interleave(0, 0)
+        interleave(1, 0)
+        gather(0, 4)
+        gather(1, 4)
+        gather(0, 5)
+        quantise(0, 0)
+        gather(1, 5)
+        interleave_pair(0)
+        gather(0, 6)
+        for cols in (slice(0, HALF // 2), slice(HALF // 2, HALF)):
+            gather(0, 7, cols)
+            interleave(0, 1, cols)
+        gather(1, 6)
+        gather(1, 7)
+        quantise(0, 1)
+        quantise(1, 0)
         transpose_wgo()
-        for r in range(DIRECT):
-            make_keys(0, r)
-            sums_direct(0, r)
-        make_keys(0, DIRECT)
+        for a in range(PASSES):
+            for r in range(DIRECT):
+                make_keys(0, r, [a])
+                sums_direct(0, r, [a])
+            make_keys(0, DIRECT, [a])
         for r in range(DIRECT):
             make_gate(0, r)
             values_direct(0, r)
-        quantise_half(1)
+        interleave_pair(1)
+        quantise(1, 1)
         values_by_token(0, DIRECT)
         for u, unit in enumerate(units):
             if u + 3 < len(units):

@@ -27,8 +27,9 @@ ROW_TILES = N // P
 GROUPS = 8
 GROUP = P // GROUPS
 J_TILES = HALF // P
-LIST_COLS = HALF // GROUP
-DIRECT = 2
+UNITS = J_TILES + ROW_TILES
+ON_GPSIMD = True
+CHUNKS = (slice(0, P), slice(P, 2 * P), slice(2 * P, HALF))
 
 
 def tile_list_siluS_kernel(
@@ -45,8 +46,8 @@ def tile_list_siluS_kernel(
         def half_cols(h):
             return slice(h * HALF, (h + 1) * HALF)
 
-        def list_cols(h):
-            return slice(h * LIST_COLS, (h + 1) * LIST_COLS)
+        def block(i):
+            return slice(i * P, (i + 1) * P)
 
         pick = keep.tile([P, J // GROUP], U16, name="pick")
         place = keep.tile([P, J // GROUP], U16, name="place")
@@ -56,8 +57,8 @@ def tile_list_siluS_kernel(
         wv_codes = keep.tile([P, PASSES, 2 * N], U8, name="wv_codes", align_bytes=64)
         wk_sc = keep.tile([P, PASSES, N], U8, name="wk_sc", align_bytes=64)
         wv_sc = keep.tile([P, PASSES, N], U8, name="wv_sc", align_bytes=64)
-        st_sb = {(h, r): keep.tile([P, HALF], F32, name=f"st{h}{r}") for h in range(HALVES) for r in range(ROW_TILES)}
-        wgo_sb = keep.tile([P, HALF], F32, name="wgo_sb")
+        st_sb = [keep.tile([P, HALF], F32, name=f"st{u}", tag=f"st{u}", align_bytes=64) for u in range(UNITS)]
+        wgo_first = keep.tile([P, 1, P], F32, name="wgo_first")
         wgo_rows = keep.tile([P, P], F32, name="wgo_rows")
         wgo_t = keep.tile([P, P], F32, name="wgo_t")
         ident = keep.tile([P, P], F32, name="ident")
@@ -74,47 +75,55 @@ def tile_list_siluS_kernel(
 
         def load_scale_rows(tile, scales, r):
             rows = scales.rearrange("a (q r) n -> r q a n", r=4)
-            nc.sync.dma_start(out=tile[r:P:32, :, :].bitcast(I32), in_=rows[r].bitcast(I32))
+            nc.gpsimd.dma_start(out=tile[r:P:32, :, :].bitcast(I32), in_=rows[r].bitcast(I32))
+
+        scale_loads = [(wk_sc, wk_scales, r) for r in range(4)] + [(wv_sc, wv_scales, r) for r in range(4)]
+        for load in scale_loads:
+            load_scale_rows(*load)
 
         nc.sync.dma_start(pick[:], offs)
         nc.sync.dma_start(out=wgt_sb[0][:], in_=wgt[:, half_cols(0)])
         x_rows = xT.rearrange("(a p i) t -> p a i t", a=PASSES, i=PACK)
-        scale_loads = [(wk_sc, wk_scales, r) for r in range(4)] + [(wv_sc, wv_scales, r) for r in range(4)]
         for q in range(PASSES * PACK):
             nc.sync.dma_start(out=planes[q][:], in_=x_rows[:, q // PACK, q % PACK, :])
             if q == 0:
                 nc.sync.dma_start(out=wgt_sb[1][:], in_=wgt[:, half_cols(1)])
-            load_scale_rows(*scale_loads[q])
+            if q == 1:
+                nc.sync.dma_start(
+                    out=wgo_rows[:],
+                    in_=wgo.rearrange("(g s r) j -> g s (r j)", g=GROUPS, r=2)[:, 0, :].rearrange("g (u c) -> g u c", c=P),
+                )
         nc.sync.dma_start(out=wk_codes[:].bitcast(I32), in_=wk_words.rearrange("a p n t -> p a (n t)").bitcast(I32))
         nc.sync.dma_start(out=wv_codes[:].bitcast(I32), in_=wv_words.rearrange("a p b -> p a b").bitcast(I32))
-        nc.sync.dma_start(out=st_sb[0, 0][:], in_=st[0:P, half_cols(0)])
-        nc.sync.dma_start(out=wgo_sb[:], in_=wgo[:, half_cols(0)])
-        nc.sync.dma_start(out=st_sb[0, 1][:], in_=st[P : 2 * P, half_cols(0)])
+        st_rows = st.rearrange("(r p) j -> p r j", p=P)
+
+        def load_state(u):
+            if u < J_TILES:
+                nc.sync.dma_start(out=st_sb[u][:].rearrange("p (r j) -> p r j", j=P), in_=st_rows[:, :, block(u)])
+            else:
+                nc.sync.dma_start(out=st_sb[u][:], in_=st_rows[:, u - J_TILES, half_cols(1)])
+
+        load_state(0)
+        nc.sync.dma_start(out=wgo_first[:, 0, :], in_=wgo[:, block(0)])
         nc.sync.dma_start(place[:], offs2)
-        nc.sync.dma_start(
-            out=wgo_rows[:],
-            in_=wgo.rearrange("(g s r) j -> g s (r j)", g=GROUPS, r=2)[:, 0, :].rearrange("g (u c) -> g u c", c=P),
-        )
-        for h in range(HALVES):
-            for r in range(ROW_TILES):
-                if (h, r) > (0, 1):
-                    nc.sync.dma_start(out=st_sb[h, r][:], in_=st[r * P : (r + 1) * P, half_cols(h)])
+        for u in range(1, UNITS):
+            load_state(u)
 
         picked = {
             (0, 0): keep.tile([P, PACK, HALF], F32, name="picked00"),
             (0, 1): keep.tile([P, PACK, HALF], F32, name="picked01"),
             (1, 0): keep.tile([P, PACK, HALF], F32, name="picked10"),
         }
-        pairs = [
-            keep.tile([P, 2, HALF], F32, name="pair_early"),
-            keep.tile([P, 2, HALF], F32, name="pair_late", tag="wgt0"),
-        ]
+        pairs = [keep.tile([P, 2, HALF], F32, name=f"pair{n}") for n in range(2)]
         grouped = {
-            (h, a): keep.tile([P, HALF, PACK], BF16, name=f"grouped{h}{a}", tag=f"grouped{h}{a}", align_bytes=64)
-            for h in range(HALVES)
-            for a in range(PASSES)
+            key: keep.tile([P, HALF, PACK], BF16, name=f"grouped{key[0]}{key[1]}", align_bytes=64)
+            for key in ((0, 0), (1, 0), (1, 1))
         }
-        codes_tags = {(0, 0): "plane4", (0, 1): "x_codes01", (1, 0): "grouped01", (1, 1): "x_codes11"}
+        grouped_chunk = [
+            keep.tile([P, c.stop - c.start, PACK], BF16, name=f"grouped_chunk{n}", align_bytes=64)
+            for n, c in enumerate(CHUNKS)
+        ]
+        codes_tags = {(0, 0): "plane4", (1, 0): "plane7", (1, 1): "st0"}
         x_codes = {}
         x_sc = {}
 
@@ -124,163 +133,179 @@ def tile_list_siluS_kernel(
             entries = pick[:, (h * HALF + cols.start) // GROUP : (h * HALF + cols.stop) // GROUP]
             nc.vector.tensor_tensor(dst, planes[q][:].indirect(entries), wgt_sb[h][:, cols], MULT)
 
-        def interleave(h, a, cols=slice(0, HALF)):
-            nc.scalar.copy(
-                grouped[h, a][:, cols, :].rearrange("p (c u) i -> p c i u", u=4),
-                picked[h, a][:, :, cols].rearrange("p i (c u) -> p c i u", u=4),
-            )
+        def interleave(dst, src):
+            nc.scalar.copy(dst.rearrange("p (c u) i -> p c i u", u=4), src.rearrange("p i (c u) -> p c i u", u=4))
 
         def interleave_pair(n):
             nc.scalar.copy(grouped[1, 1][:, :, 2 * n : 2 * n + 2], pairs[n][:].rearrange("p i c -> p c i"))
 
-        def quantise(h, a):
-            x_codes[h, a] = keep.tile([P, HALF], U32, name=f"x_codes{h}{a}", tag=codes_tags[h, a], align_bytes=64)
-            x_sc[h, a] = keep.tile([P, HALF], U8, name=f"x_sc{h}{a}", align_bytes=64)
+        def quantise(key, src, tag):
+            width = src.shape[1]
+            name = "_".join(str(k) for k in key)
+            x_codes[key] = keep.tile([P, width], U32, name=f"x_codes{name}", tag=tag, align_bytes=64)
+            x_sc[key] = keep.tile([P, width], U8, name=f"x_sc{name}", align_bytes=64)
             nc.vector.quantize_mx(
-                out=x_codes[h, a][:].bitcast(FP8X4),
-                scales=x_sc[h, a][:],
-                in_=grouped[h, a][:].rearrange("p c i -> p (c i)"),
+                out=x_codes[key][:].bitcast(FP8X4), scales=x_sc[key][:], in_=src[:].rearrange("p c i -> p (c i)")
             )
 
+        def x_operand(h, a, cols):
+            if (h, a) == (0, 1):
+                n = [c.start <= cols.start < c.stop for c in CHUNKS].index(True)
+                key = (0, 1, n)
+                cols = slice(cols.start - CHUNKS[n].start, cols.stop - CHUNKS[n].start)
+            else:
+                key = (h, a)
+            return x_codes[key][:, cols].bitcast(FP8X4), x_sc[key][:, cols]
+
+        def unit_ranges(u):
+            if u < J_TILES:
+                return [(block(r), r, 0, block(u)) for r in range(ROW_TILES)]
+            return [(slice(0, HALF), u - J_TILES, 1, slice(0, HALF))]
+
+        def product(bank, u, codes, scales, bytes_per_col, fmt):
+            ranges = unit_ranges(u)
+            steps = [(a, rng) for a in range(PASSES) for rng in ranges]
+            for n, (a, (span, r, h, cols)) in enumerate(steps):
+                rhs, rhs_scale = x_operand(h, a, cols)
+                nc.tensor.matmul_mx(
+                    out=bank[:, span],
+                    lhsT=codes[:, a, bytes_per_col * r * P : bytes_per_col * (r + 1) * P].bitcast(fmt),
+                    lhsT_scale=scales[:, a, block(r)],
+                    rhs=rhs,
+                    rhs_scale=rhs_scale,
+                    start=(n == 0),
+                    stop=(n == len(steps) - 1),
+                )
+
+        keys = {}
         gates = {}
         values = {}
         scaled = {}
 
-        keys = {}
-        sums = {}
+        def make_keys(u):
+            keys[u] = psum_k.tile([P, HALF], F32, name="ke")
+            product(keys[u], u, wk_codes, wk_sc, 1, FP8X4)
 
-        def make_keys(h, r, passes=range(PASSES)):
-            rows = slice(r * P, (r + 1) * P)
-            if passes[0] == 0:
-                keys[h, r] = psum_k.tile([P, HALF], F32, name="ke")
-            ke = keys[h, r]
-            for a in passes:
-                nc.tensor.matmul_mx(
-                    out=ke[:],
-                    lhsT=wk_codes[:, a, rows].bitcast(FP8X4),
-                    lhsT_scale=wk_sc[:, a, rows],
-                    rhs=x_codes[h, a][:].bitcast(FP8X4),
-                    rhs_scale=x_sc[h, a][:],
-                    start=(a == 0),
-                    stop=(a == PASSES - 1),
-                )
+        def make_gate(u):
+            if ON_GPSIMD and u == 1:
+                match = keep.tile([P, HALF], F32, name="match1", tag="gate0")
+            else:
+                match = ring.tile([P, HALF], F32, name="match")
+            if ON_GPSIMD and u > 0:
+                key_sb = ring.tile([P, HALF], F32, name="key_sb")
+                nc.scalar.copy(key_sb[:], keys[u][:])
+                nc.gpsimd.tensor_tensor(match[:], key_sb[:], st_sb[u][:], MULT)
+            else:
+                nc.vector.tensor_tensor(match[:], keys[u][:], st_sb[u][:], MULT)
+            if u == 0:
+                gates[u] = keep.tile([P, HALF], F32, name="gate0", tag="gate0")
+            else:
+                gates[u] = ring.tile([P, HALF], F32, name="gate")
+            nc.scalar.activation(gates[u][:], match[:], SILU)
 
-        def make_gate(h, r):
-            match = ring.tile([P, HALF], F32, name="match")
-            nc.vector.tensor_tensor(match[:], keys[h, r][:], st_sb[h, r][:], MULT)
-            gates[h, r] = ring.tile([P, HALF], F32, name="gate")
-            nc.scalar.activation(gates[h, r][:], match[:], SILU)
-
-        def sums_direct(h, r, passes):
-            rows = slice(r * P, (r + 1) * P)
-            if passes[0] == 0:
-                sums[h, r] = psum_v.tile([P, HALF], F32, name="ve")
-            ve = sums[h, r]
-            for a in passes:
-                nc.tensor.matmul_mx(
-                    out=ve[:],
-                    lhsT=wv_codes[:, a, 2 * r * P : 2 * (r + 1) * P].bitcast(FP4X4),
-                    lhsT_scale=wv_sc[:, a, rows],
-                    rhs=x_codes[h, a][:].bitcast(FP8X4),
-                    rhs_scale=x_sc[h, a][:],
-                    start=(a == 0),
-                    stop=(a == PASSES - 1),
-                )
-
-        def values_direct(h, r):
-            values[h, r] = ring.tile([P, HALF], F32, name="value")
-            nc.vector.tensor_tensor(values[h, r][:], sums[h, r][:], wgo_sb[:], MULT)
+        def values_first():
+            ve = psum_t.tile([P, HALF], F32, name="turned")
+            product(ve, 0, wv_codes, wv_sc, 2, FP4X4)
+            values[0] = ring.tile([P, HALF], F32, name="value")
+            nc.vector.tensor_tensor(
+                values[0][:].rearrange("p (r j) -> p r j", j=P),
+                ve[:].rearrange("p (r j) -> p r j", j=P),
+                wgo_first[:].to_broadcast([P, ROW_TILES, P]),
+                MULT,
+            )
 
         def transpose_wgo():
             turned = psum_t.tile([P, HALF], F32, name="turned")
             nc.tensor.transpose(turned[:, 0:P], wgo_rows[:], ident[:])
             nc.scalar.copy(wgo_t[:], turned[:, 0:P])
 
-        def values_by_token(h, first):
-            width = (ROW_TILES - first) * P
-            spans = [slice(0, N)] if first == 0 else [slice(r * P, (r + 1) * P) for r in range(first, ROW_TILES)]
-            per_bank = HALF // width
-            for jt0 in range(0, J_TILES, per_bank):
-                bank = psum_v.tile([P, HALF], F32, name="ve")
-                for slot in range(per_bank):
-                    tokens = slice((jt0 + slot) * P, (jt0 + slot + 1) * P)
-                    shift = slot * width - first * P
-                    for span in spans:
-                        for step, a in enumerate(reversed(range(PASSES))):
-                            nc.tensor.matmul_mx(
-                                out=bank[:, span.start + shift : span.stop + shift],
-                                lhsT=x_codes[h, a][:, tokens].bitcast(FP8X4),
-                                lhsT_scale=x_sc[h, a][:, tokens],
-                                rhs=wv_codes[:, a, 2 * span.start : 2 * span.stop].bitcast(FP4X4),
-                                rhs_scale=wv_sc[:, a, span],
-                                start=(step == 0),
-                                stop=(step == PASSES - 1),
-                            )
-                for slot in range(per_bank):
-                    jt = jt0 + slot
-                    scaled[h, jt] = keep.tile([P, width], F32, name=f"scaled{h}{jt}")
-                    src = bank[:, slot * width : (slot + 1) * width].rearrange("p (r g c) -> p r g c", g=GROUPS, c=GROUP)
-                    dst = scaled[h, jt][:].rearrange("p (r g c) -> p r g c", g=GROUPS, c=GROUP)
-                    for g in range(GROUPS):
-                        col = g * GROUP + h * J_TILES + jt
-                        nc.scalar.activation(dst[:, :, g, :], src[:, :, g, :], COPY, scale=wgo_t[:, col : col + 1])
-
-        def values_turned(h, r, first):
-            turned = psum_t.tile([P, HALF], F32, name="turned")
-            for jt in range(J_TILES):
-                nc.tensor.transpose(
-                    turned[:, jt * P : (jt + 1) * P], scaled[h, jt][:, (r - first) * P : (r - first + 1) * P], ident[:]
+        def values_by_token(h, jt):
+            bank = psum_v.tile([P, N], F32, name="ve")
+            for a in range(PASSES):
+                lhsT, lhsT_scale = x_operand(h, a, block(jt))
+                nc.tensor.matmul_mx(
+                    out=bank[:],
+                    lhsT=lhsT,
+                    lhsT_scale=lhsT_scale,
+                    rhs=wv_codes[:, a, :].bitcast(FP4X4),
+                    rhs_scale=wv_sc[:, a, :],
+                    start=(a == 0),
+                    stop=(a == PASSES - 1),
                 )
-            values[h, r] = ring.tile([P, HALF], F32, name="value")
-            nc.scalar.copy(values[h, r][:], turned[:])
+            scaled[h, jt] = keep.tile([P, N], F32, name=f"scaled{h}{jt}")
+            src = bank[:].rearrange("p (r g c) -> p r g c", g=GROUPS, c=GROUP)
+            dst = scaled[h, jt][:].rearrange("p (r g c) -> p r g c", g=GROUPS, c=GROUP)
+            for g in range(GROUPS):
+                col = g * GROUP + h * J_TILES + jt
+                nc.scalar.activation(dst[:, :, g, :], src[:, :, g, :], COPY, scale=wgo_t[:, col : col + 1])
 
-        def scatter(h, r):
-            nc.vector.tensor_tensor(
-                windows[r][:].indirect(place[:, list_cols(h)]), gates[h, r][:], values[h, r][:], MULT
-            )
-            if h == HALVES - 1:
-                nc.sync.dma_start(out=out[r * P : (r + 1) * P, :], in_=windows[r][:])
+        def values_turned(u):
+            turned = psum_t.tile([P, HALF], F32, name="turned")
+            for n in range(HALF // P):
+                src = scaled[0, u][:, block(n)] if u < J_TILES else scaled[1, n][:, block(u - J_TILES)]
+                nc.tensor.transpose(turned[:, block(n)], src, ident[:])
+            values[u] = ring.tile([P, HALF], F32, name="value")
+            nc.scalar.copy(values[u][:], turned[:])
 
-        units = [(h, r) for h in range(HALVES) for r in range(ROW_TILES)]
+        results = {}
 
+        def combine(u):
+            if ON_GPSIMD:
+                results[u] = ring.tile([P, HALF], F32, name="result")
+                engine = nc.gpsimd if u > 0 else nc.vector
+                engine.tensor_tensor(results[u][:], gates[u][:], values[u][:], MULT)
+
+        def scatter(u):
+            for span, r, h, cols in unit_ranges(u):
+                entries = place[:, (h * HALF + cols.start) // GROUP : (h * HALF + cols.stop) // GROUP]
+                if ON_GPSIMD:
+                    nc.vector.tensor_copy(windows[r][:].indirect(entries), results[u][:, span])
+                else:
+                    nc.vector.tensor_tensor(windows[r][:].indirect(entries), gates[u][:, span], values[u][:, span], MULT)
+                if h == HALVES - 1:
+                    nc.sync.dma_start(out=out[block(r), :], in_=windows[r][:])
+
+        transpose_wgo()
         for q in range(PACK):
             gather(0, q)
             gather(1, q)
-        interleave(0, 0)
-        interleave(1, 0)
+        interleave(grouped[0, 0][:], picked[0, 0][:])
+        interleave(grouped[1, 0][:], picked[1, 0][:])
         gather(0, 4)
         gather(1, 4)
+        quantise((0, 0), grouped[0, 0], codes_tags[0, 0])
         gather(0, 5)
-        quantise(0, 0)
         gather(1, 5)
         interleave_pair(0)
         gather(0, 6)
-        for cols in (slice(0, HALF // 2), slice(HALF // 2, HALF)):
-            gather(0, 7, cols)
-            interleave(0, 1, cols)
         gather(1, 6)
+        for n, cols in enumerate(CHUNKS):
+            gather(0, 7, cols)
+            interleave(grouped_chunk[n][:], picked[0, 1][:, :, cols])
         gather(1, 7)
-        quantise(0, 1)
-        quantise(1, 0)
-        transpose_wgo()
-        for a in range(PASSES):
-            for r in range(DIRECT):
-                make_keys(0, r, [a])
-                sums_direct(0, r, [a])
-            make_keys(0, DIRECT, [a])
-        for r in range(DIRECT):
-            make_gate(0, r)
-            values_direct(0, r)
         interleave_pair(1)
-        quantise(1, 1)
-        values_by_token(0, DIRECT)
-        for u, unit in enumerate(units):
-            if u + 3 < len(units):
-                make_keys(*units[u + 3])
-            scatter(*unit)
-            if u + 2 < len(units):
-                h, r = units[u + 2]
-                make_gate(h, r)
-                values_turned(h, r, DIRECT if h == 0 else 0)
-            if u == 1:
-                values_by_token(1, 0)
+        for n in range(2):
+            quantise((0, 1, n), grouped_chunk[n], f"x_codes01{n}")
+        quantise((1, 0), grouped[1, 0], codes_tags[1, 0])
+        quantise((0, 1, 2), grouped_chunk[2], "x_codes012")
+        make_keys(0)
+        make_gate(0)
+        values_first()
+        quantise((1, 1), grouped[1, 1], codes_tags[1, 1])
+        combine(0)
+
+        def prepare(u):
+            make_keys(u)
+            if u < J_TILES:
+                values_by_token(0, u)
+            make_gate(u)
+            values_turned(u)
+            combine(u)
+            if 2 <= u < J_TILES:
+                for jt in (2 * u - 4, 2 * u - 3):
+                    values_by_token(1, jt)
+
+        for u in range(UNITS):
+            if u + 1 < UNITS:
+                prepare(u + 1)
+            scatter(u)

@@ -28,8 +28,8 @@ GROUPS = 8
 GROUP = P // GROUPS
 J_TILES = HALF // P
 UNITS = J_TILES + ROW_TILES
-ON_GPSIMD = True
-CHUNKS = (slice(0, P), slice(P, 2 * P), slice(2 * P, HALF))
+ON_VECTOR = 2
+CHUNKS = (slice(0, P), slice(P, 2 * P), slice(2 * P, HALF), slice(HALF, J))
 
 
 def tile_list_siluS_kernel(
@@ -51,7 +51,7 @@ def tile_list_siluS_kernel(
 
         pick = keep.tile([P, J // GROUP], U16, name="pick")
         place = keep.tile([P, J // GROUP], U16, name="place")
-        wgt_sb = [keep.tile([P, HALF], F32, name=f"wgt{h}", tag=f"wgt{h}") for h in range(HALVES)]
+        wgt_sb = keep.tile([P, J], F32, name="wgt_sb")
         planes = [keep.tile([P, T], F32, name=f"plane{q}", tag=f"plane{q}", align_bytes=64) for q in range(PASSES * PACK)]
         wk_codes = keep.tile([P, PASSES, N], U32, name="wk_codes", align_bytes=64)
         wv_codes = keep.tile([P, PASSES, 2 * N], U8, name="wv_codes", align_bytes=64)
@@ -70,7 +70,7 @@ def tile_list_siluS_kernel(
         nc.gpsimd.memset(warm[:], 0.0)
         nc.scalar.activation(warm[:, 1:2], warm[:, 0:1], SILU)
         make_identity(nc, ident[:])
-        for r in range(ROW_TILES):
+        for r in range(ON_VECTOR):
             nc.vector.memset(windows[r][:].bitcast(I32), 0)
 
         def load_scale_rows(tile, scales, r):
@@ -81,13 +81,16 @@ def tile_list_siluS_kernel(
         for load in scale_loads:
             load_scale_rows(*load)
 
+        for r in range(ON_VECTOR, ROW_TILES):
+            nc.gpsimd.memset(windows[r][:].bitcast(I32), 0)
+
         nc.sync.dma_start(pick[:], offs)
-        nc.sync.dma_start(out=wgt_sb[0][:], in_=wgt[:, half_cols(0)])
+        nc.sync.dma_start(out=wgt_sb[:, half_cols(0)], in_=wgt[:, half_cols(0)])
         x_rows = xT.rearrange("(a p i) t -> p a i t", a=PASSES, i=PACK)
         for q in range(PASSES * PACK):
             nc.sync.dma_start(out=planes[q][:], in_=x_rows[:, q // PACK, q % PACK, :])
             if q == 0:
-                nc.sync.dma_start(out=wgt_sb[1][:], in_=wgt[:, half_cols(1)])
+                nc.sync.dma_start(out=wgt_sb[:, half_cols(1)], in_=wgt[:, half_cols(1)])
             if q == 1:
                 nc.sync.dma_start(
                     out=wgo_rows[:],
@@ -109,35 +112,29 @@ def tile_list_siluS_kernel(
         for u in range(1, UNITS):
             load_state(u)
 
-        picked = {
-            (0, 0): keep.tile([P, PACK, HALF], F32, name="picked00"),
-            (0, 1): keep.tile([P, PACK, HALF], F32, name="picked01"),
-            (1, 0): keep.tile([P, PACK, HALF], F32, name="picked10"),
-        }
-        pairs = [keep.tile([P, 2, HALF], F32, name=f"pair{n}") for n in range(2)]
-        grouped = {
-            key: keep.tile([P, HALF, PACK], BF16, name=f"grouped{key[0]}{key[1]}", align_bytes=64)
-            for key in ((0, 0), (1, 0), (1, 1))
-        }
+        picked = keep.tile([P, PACK, J], F32, name="picked")
+        pairs = [keep.tile([P, 2, J], F32, name=f"pair{n}") for n in range(2)]
+        grouped_first = keep.tile([P, J, PACK], BF16, name="grouped_first", align_bytes=64)
         grouped_chunk = [
             keep.tile([P, c.stop - c.start, PACK], BF16, name=f"grouped_chunk{n}", align_bytes=64)
             for n, c in enumerate(CHUNKS)
         ]
-        codes_tags = {(0, 0): "plane4", (1, 0): "plane7", (1, 1): "st0"}
         x_codes = {}
         x_sc = {}
 
-        def gather(h, q, cols=slice(0, HALF)):
+        def gather(q, cols=slice(0, J)):
             a, i = divmod(q, PACK)
-            dst = picked[h, a][:, i, cols] if (h, a) in picked else pairs[i // 2][:, i % 2, cols]
-            entries = pick[:, (h * HALF + cols.start) // GROUP : (h * HALF + cols.stop) // GROUP]
-            nc.vector.tensor_tensor(dst, planes[q][:].indirect(entries), wgt_sb[h][:, cols], MULT)
+            dst = picked[:, i, cols] if a == 0 else pairs[i // 2][:, i % 2, cols]
+            entries = pick[:, cols.start // GROUP : cols.stop // GROUP]
+            nc.vector.tensor_tensor(dst, planes[q][:].indirect(entries), wgt_sb[:, cols], MULT)
 
         def interleave(dst, src):
             nc.scalar.copy(dst.rearrange("p (c u) i -> p c i u", u=4), src.rearrange("p i (c u) -> p c i u", u=4))
 
-        def interleave_pair(n):
-            nc.scalar.copy(grouped[1, 1][:, :, 2 * n : 2 * n + 2], pairs[n][:].rearrange("p i c -> p c i"))
+        def interleave_pair(n, chunk):
+            nc.scalar.copy(
+                grouped_chunk[chunk][:, :, 2 * n : 2 * n + 2], pairs[n][:, :, CHUNKS[chunk]].rearrange("p i c -> p c i")
+            )
 
         def quantise(key, src, tag):
             width = src.shape[1]
@@ -149,12 +146,13 @@ def tile_list_siluS_kernel(
             )
 
         def x_operand(h, a, cols):
-            if (h, a) == (0, 1):
+            cols = slice(h * HALF + cols.start, h * HALF + cols.stop)
+            if a == 1:
                 n = [c.start <= cols.start < c.stop for c in CHUNKS].index(True)
-                key = (0, 1, n)
+                key = (1, n)
                 cols = slice(cols.start - CHUNKS[n].start, cols.stop - CHUNKS[n].start)
             else:
-                key = (h, a)
+                key = (0,)
             return x_codes[key][:, cols].bitcast(FP8X4), x_sc[key][:, cols]
 
         def unit_ranges(u):
@@ -186,27 +184,34 @@ def tile_list_siluS_kernel(
             keys[u] = psum_k.tile([P, HALF], F32, name="ke")
             product(keys[u], u, wk_codes, wk_sc, 1, FP8X4)
 
+        matches = {}
+        key_sb = {}
+
+        def copy_keys(u):
+            key_sb[u] = ring.tile([P, HALF], F32, name="key_sb")
+            nc.scalar.copy(key_sb[u][:], keys[u][:])
+
+        def make_match(u):
+            if u == 2:
+                matches[u] = keep.tile([P, HALF], F32, name="match2", tag="value0")
+            else:
+                matches[u] = ring.tile([P, HALF], F32, name="match")
+            if u >= 2:
+                nc.gpsimd.tensor_tensor(matches[u][:], key_sb[u][:], st_sb[u][:], MULT)
+            else:
+                nc.vector.tensor_tensor(matches[u][:], keys[u][:], st_sb[u][:], MULT)
+
         def make_gate(u):
-            if ON_GPSIMD and u == 1:
-                match = keep.tile([P, HALF], F32, name="match1", tag="gate0")
-            else:
-                match = ring.tile([P, HALF], F32, name="match")
-            if ON_GPSIMD and u > 0:
-                key_sb = ring.tile([P, HALF], F32, name="key_sb")
-                nc.scalar.copy(key_sb[:], keys[u][:])
-                nc.gpsimd.tensor_tensor(match[:], key_sb[:], st_sb[u][:], MULT)
-            else:
-                nc.vector.tensor_tensor(match[:], keys[u][:], st_sb[u][:], MULT)
             if u == 0:
                 gates[u] = keep.tile([P, HALF], F32, name="gate0", tag="gate0")
             else:
                 gates[u] = ring.tile([P, HALF], F32, name="gate")
-            nc.scalar.activation(gates[u][:], match[:], SILU)
+            nc.scalar.activation(gates[u][:], matches[u][:], SILU)
 
         def values_first():
             ve = psum_t.tile([P, HALF], F32, name="turned")
             product(ve, 0, wv_codes, wv_sc, 2, FP4X4)
-            values[0] = ring.tile([P, HALF], F32, name="value")
+            values[0] = keep.tile([P, HALF], F32, name="value0", tag="value0")
             nc.vector.tensor_tensor(
                 values[0][:].rearrange("p (r j) -> p r j", j=P),
                 ve[:].rearrange("p (r j) -> p r j", j=P),
@@ -250,62 +255,70 @@ def tile_list_siluS_kernel(
         results = {}
 
         def combine(u):
-            if ON_GPSIMD:
+            if u == 1:
+                results[u] = keep.tile([P, HALF], F32, name="result1", tag="gate0")
+            else:
                 results[u] = ring.tile([P, HALF], F32, name="result")
-                engine = nc.gpsimd if u > 0 else nc.vector
-                engine.tensor_tensor(results[u][:], gates[u][:], values[u][:], MULT)
+            if u > 0:
+                nc.gpsimd.tensor_tensor(results[u][:], gates[u][:], values[u][:], MULT)
+            else:
+                nc.vector.tensor_tensor(results[u][:, P:], gates[u][:, P:], values[u][:, P:], MULT)
 
         def scatter(u):
             for span, r, h, cols in unit_ranges(u):
                 entries = place[:, (h * HALF + cols.start) // GROUP : (h * HALF + cols.stop) // GROUP]
-                if ON_GPSIMD:
-                    nc.vector.tensor_copy(windows[r][:].indirect(entries), results[u][:, span])
-                else:
+                if (u, r) == (0, 0):
                     nc.vector.tensor_tensor(windows[r][:].indirect(entries), gates[u][:, span], values[u][:, span], MULT)
+                else:
+                    nc.vector.tensor_copy(windows[r][:].indirect(entries), results[u][:, span])
                 if h == HALVES - 1:
                     nc.sync.dma_start(out=out[block(r), :], in_=windows[r][:])
 
         transpose_wgo()
-        for q in range(PACK):
-            gather(0, q)
-            gather(1, q)
-        interleave(grouped[0, 0][:], picked[0, 0][:])
-        interleave(grouped[1, 0][:], picked[1, 0][:])
-        gather(0, 4)
-        gather(1, 4)
-        quantise((0, 0), grouped[0, 0], codes_tags[0, 0])
-        gather(0, 5)
-        gather(1, 5)
-        interleave_pair(0)
-        gather(0, 6)
-        gather(1, 6)
+        for h in range(HALVES):
+            gather(0, half_cols(h))
+        for q in range(1, PACK):
+            gather(q)
+        for h in range(HALVES):
+            interleave(grouped_first[:, half_cols(h), :], picked[:, :, half_cols(h)])
+        gather(4)
+        gather(5)
+        quantise((0,), grouped_first, "plane5")
+        for n in range(len(CHUNKS)):
+            interleave_pair(0, n)
+        gather(6)
         for n, cols in enumerate(CHUNKS):
-            gather(0, 7, cols)
-            interleave(grouped_chunk[n][:], picked[0, 1][:, :, cols])
-        gather(1, 7)
-        interleave_pair(1)
-        for n in range(2):
-            quantise((0, 1, n), grouped_chunk[n], f"x_codes01{n}")
-        quantise((1, 0), grouped[1, 0], codes_tags[1, 0])
-        quantise((0, 1, 2), grouped_chunk[2], "x_codes012")
+            gather(7, cols)
+            interleave_pair(1, n)
+        for n in range(3):
+            quantise((1, n), grouped_chunk[n], f"x_codes1{n}")
         make_keys(0)
-        make_gate(0)
+        make_match(0)
         values_first()
-        quantise((1, 1), grouped[1, 1], codes_tags[1, 1])
+        make_keys(1)
+        make_match(1)
+        quantise((1, 3), grouped_chunk[3], "st0")
+        make_gate(0)
         combine(0)
-
-        def prepare(u):
-            make_keys(u)
-            if u < J_TILES:
-                values_by_token(0, u)
-            make_gate(u)
-            values_turned(u)
-            combine(u)
-            if 2 <= u < J_TILES:
-                for jt in (2 * u - 4, 2 * u - 3):
-                    values_by_token(1, jt)
-
+        make_gate(1)
+        values_by_token(0, 1)
+        values_turned(1)
+        make_keys(2)
+        copy_keys(2)
         for u in range(UNITS):
             if u + 1 < UNITS:
-                prepare(u + 1)
+                combine(u + 1)
+            if u + 2 < UNITS:
+                make_match(u + 2)
             scatter(u)
+            if u + 2 < J_TILES:
+                values_by_token(0, u + 2)
+            if u + 3 < UNITS:
+                make_keys(u + 3)
+                copy_keys(u + 3)
+            if u + 2 < UNITS:
+                if u + 2 == J_TILES:
+                    for jt in range(J_TILES):
+                        values_by_token(1, jt)
+                make_gate(u + 2)
+                values_turned(u + 2)

@@ -28,7 +28,7 @@ GROUPS = 8
 GROUP = P // GROUPS
 J_TILES = HALF // P
 UNITS = J_TILES + ROW_TILES
-ON_VECTOR = 2
+FIRST_CHUNKS = (slice(0, 2 * P), slice(2 * P, HALF), slice(HALF, J))
 CHUNKS = (slice(0, P), slice(P, 2 * P), slice(2 * P, HALF), slice(HALF, J))
 
 
@@ -55,23 +55,24 @@ def tile_list_siluS_kernel(
         planes = [keep.tile([P, T], F32, name=f"plane{q}", tag=f"plane{q}", align_bytes=64) for q in range(PASSES * PACK)]
         wk_codes = keep.tile([P, PASSES, N], U32, name="wk_codes", align_bytes=64)
         wv_codes = keep.tile([P, PASSES, 2 * N], U8, name="wv_codes", align_bytes=64)
-        wk_sc = keep.tile([P, PASSES, N], U8, name="wk_sc", align_bytes=64)
-        wv_sc = keep.tile([P, PASSES, N], U8, name="wv_sc", align_bytes=64)
+        w_sc = keep.tile([P, 2, PASSES, N], U8, name="w_sc", align_bytes=64)
+        wk_sc = w_sc[:, 0]
+        wv_sc = w_sc[:, 1]
         st_sb = [keep.tile([P, HALF], F32, name=f"st{u}", tag=f"st{u}", align_bytes=64) for u in range(UNITS)]
         wgo_first = keep.tile([P, 1, P], F32, name="wgo_first")
-        wgo_rows = keep.tile([P, P], F32, name="wgo_rows")
-        wgo_t = keep.tile([P, P], F32, name="wgo_t")
+        group_rows = keep.tile([P, P], F32, name="group_rows")
+        wgo_t = keep.tile([P, P // 2], F32, name="wgo_t")
+        wgt_wide = keep.tile([P, J // P, GROUPS, GROUP], F32, name="wgt_wide")
         ident = keep.tile([P, P], F32, name="ident")
         windows = [keep.tile([P, T], F32, name=f"window{r}") for r in range(ROW_TILES)]
         warm = keep.tile([P, 8], F32, name="warm")
 
-        nc.gpsimd.memset(wk_sc[:].bitcast(I32), 0)
-        nc.gpsimd.memset(wv_sc[:].bitcast(I32), 0)
         nc.gpsimd.memset(warm[:], 0.0)
         nc.scalar.activation(warm[:, 1:2], warm[:, 0:1], SILU)
         make_identity(nc, ident[:])
-        for r in range(ON_VECTOR):
+        for r in range(ROW_TILES):
             nc.vector.memset(windows[r][:].bitcast(I32), 0)
+        nc.vector.memset(w_sc[:].rearrange("p w a n -> p (w a n)").bitcast(I32), 0)
 
         def load_scale_rows(tile, scales, r):
             rows = scales.rearrange("a (q r) n -> r q a n", r=4)
@@ -81,21 +82,15 @@ def tile_list_siluS_kernel(
         for load in scale_loads:
             load_scale_rows(*load)
 
-        for r in range(ON_VECTOR, ROW_TILES):
-            nc.gpsimd.memset(windows[r][:].bitcast(I32), 0)
-
+        for n, weights in enumerate((wgt, wgo)):
+            nc.sync.dma_start(
+                out=group_rows[n * P // 2 : (n + 1) * P // 2, :],
+                in_=weights.rearrange("(g s) (u c) -> s g u c", s=GROUP, c=P)[0],
+            )
         nc.sync.dma_start(pick[:], offs)
-        nc.sync.dma_start(out=wgt_sb[:, half_cols(0)], in_=wgt[:, half_cols(0)])
         x_rows = xT.rearrange("(a p i) t -> p a i t", a=PASSES, i=PACK)
         for q in range(PASSES * PACK):
             nc.sync.dma_start(out=planes[q][:], in_=x_rows[:, q // PACK, q % PACK, :])
-            if q == 0:
-                nc.sync.dma_start(out=wgt_sb[:, half_cols(1)], in_=wgt[:, half_cols(1)])
-            if q == 1:
-                nc.sync.dma_start(
-                    out=wgo_rows[:],
-                    in_=wgo.rearrange("(g s r) j -> g s (r j)", g=GROUPS, r=2)[:, 0, :].rearrange("g (u c) -> g u c", c=P),
-                )
         nc.sync.dma_start(out=wk_codes[:].bitcast(I32), in_=wk_words.rearrange("a p n t -> p a (n t)").bitcast(I32))
         nc.sync.dma_start(out=wv_codes[:].bitcast(I32), in_=wv_words.rearrange("a p b -> p a b").bitcast(I32))
         st_rows = st.rearrange("(r p) j -> p r j", p=P)
@@ -112,8 +107,7 @@ def tile_list_siluS_kernel(
         for u in range(1, UNITS):
             load_state(u)
 
-        picked = keep.tile([P, PACK, J], F32, name="picked")
-        pairs = [keep.tile([P, 2, J], F32, name=f"pair{n}") for n in range(2)]
+        pairs = [keep.tile([P, 2, J], F32, name=f"pair{n}") for n in range(PASSES * PACK // 2)]
         grouped_first = keep.tile([P, J, PACK], BF16, name="grouped_first", align_bytes=64)
         grouped_chunk = [
             keep.tile([P, c.stop - c.start, PACK], BF16, name=f"grouped_chunk{n}", align_bytes=64)
@@ -123,18 +117,13 @@ def tile_list_siluS_kernel(
         x_sc = {}
 
         def gather(q, cols=slice(0, J)):
-            a, i = divmod(q, PACK)
-            dst = picked[:, i, cols] if a == 0 else pairs[i // 2][:, i % 2, cols]
+            dst = pairs[q // 2][:, q % 2, cols]
             entries = pick[:, cols.start // GROUP : cols.stop // GROUP]
             nc.vector.tensor_tensor(dst, planes[q][:].indirect(entries), wgt_sb[:, cols], MULT)
 
-        def interleave(dst, src):
-            nc.scalar.copy(dst.rearrange("p (c u) i -> p c i u", u=4), src.rearrange("p i (c u) -> p c i u", u=4))
-
-        def interleave_pair(n, chunk):
-            nc.scalar.copy(
-                grouped_chunk[chunk][:, :, 2 * n : 2 * n + 2], pairs[n][:, :, CHUNKS[chunk]].rearrange("p i c -> p c i")
-            )
+        def interleave_pair(dst, n, cols):
+            first = 2 * (n % 2)
+            nc.scalar.copy(dst[:, :, first : first + 2], pairs[n][:, :, cols].rearrange("p i c -> p c i"))
 
         def quantise(key, src, tag):
             width = src.shape[1]
@@ -219,10 +208,20 @@ def tile_list_siluS_kernel(
                 MULT,
             )
 
-        def transpose_wgo():
-            turned = psum_t.tile([P, HALF], F32, name="turned")
-            nc.tensor.transpose(turned[:, 0:P], wgo_rows[:], ident[:])
-            nc.scalar.copy(wgo_t[:], turned[:, 0:P])
+        def spread_group_weights():
+            by_place = psum_k.tile([P, HALF], F32, name="ke")
+            nc.tensor.transpose(by_place[:, 0:P], group_rows[:], ident[:])
+            wgt_t = by_place[:, 0 : P // 2].rearrange("p (g u o) -> p u g o", g=GROUPS, o=1)
+            for cols in FIRST_CHUNKS:
+                tiles = slice(cols.start // P, cols.stop // P)
+                count = tiles.stop - tiles.start
+                nc.scalar.copy(wgt_wide[:, tiles], wgt_t[:, tiles].to_broadcast([P, count, GROUPS, GROUP]))
+                turned = psum_v.tile([P, HALF], F32, name="ve")
+                for n in range(count):
+                    src = wgt_wide[:, tiles.start + n].rearrange("p g s -> p (g s)")
+                    nc.tensor.transpose(turned[:, block(n)], src, ident[:])
+                nc.scalar.copy(wgt_sb[:, cols], turned[:, 0 : count * P])
+            nc.scalar.copy(wgo_t[:], by_place[:, P // 2 : P])
 
         def values_by_token(h, jt):
             bank = psum_v.tile([P, N], F32, name="ve")
@@ -241,7 +240,7 @@ def tile_list_siluS_kernel(
             src = bank[:].rearrange("p (r g c) -> p r g c", g=GROUPS, c=GROUP)
             dst = scaled[h, jt][:].rearrange("p (r g c) -> p r g c", g=GROUPS, c=GROUP)
             for g in range(GROUPS):
-                col = g * GROUP + h * J_TILES + jt
+                col = g * (J // P) + h * J_TILES + jt
                 nc.scalar.activation(dst[:, :, g, :], src[:, :, g, :], COPY, scale=wgo_t[:, col : col + 1])
 
         def values_turned(u):
@@ -274,22 +273,23 @@ def tile_list_siluS_kernel(
                 if h == HALVES - 1:
                     nc.sync.dma_start(out=out[block(r), :], in_=windows[r][:])
 
-        transpose_wgo()
-        for h in range(HALVES):
-            gather(0, half_cols(h))
-        for q in range(1, PACK):
-            gather(q)
-        for h in range(HALVES):
-            interleave(grouped_first[:, half_cols(h), :], picked[:, :, half_cols(h)])
+        spread_group_weights()
+        for cols in FIRST_CHUNKS:
+            gather(0, cols)
+        gather(1)
+        interleave_pair(grouped_first, 0, slice(0, J))
+        gather(2)
+        gather(3)
+        interleave_pair(grouped_first, 1, slice(0, J))
         gather(4)
         gather(5)
         quantise((0,), grouped_first, "plane5")
-        for n in range(len(CHUNKS)):
-            interleave_pair(0, n)
+        for n, cols in enumerate(CHUNKS):
+            interleave_pair(grouped_chunk[n], 2, cols)
         gather(6)
         for n, cols in enumerate(CHUNKS):
             gather(7, cols)
-            interleave_pair(1, n)
+            interleave_pair(grouped_chunk[n], 3, cols)
         for n in range(3):
             quantise((1, n), grouped_chunk[n], f"x_codes1{n}")
         make_keys(0)

@@ -1,7 +1,6 @@
 from contextlib import ExitStack
 
 import concourse.mybir as mybir
-from concourse.masks import make_identity
 
 K, N, T, J = 1024, 512, 2048, 1024
 FLOPS = 2 * 2 * K * N * J
@@ -21,15 +20,21 @@ COPY = mybir.ActivationFunctionType.Copy
 P = 128
 PACK = 4
 PASSES = K // (P * PACK)
+PLANES = PASSES * PACK
 HALF = 512
 HALVES = J // HALF
 ROW_TILES = N // P
 GROUPS = 8
 GROUP = P // GROUPS
-J_TILES = HALF // P
-UNITS = J_TILES + ROW_TILES
-FIRST_CHUNKS = (slice(0, 2 * P), slice(2 * P, HALF), slice(HALF, J))
-CHUNKS = (slice(0, P), slice(P, 2 * P), slice(2 * P, HALF), slice(HALF, J))
+PLACE_TILES = HALF // P
+UNITS = N * J // (P * HALF)
+NARROW_UNITS = 2
+FIRST_HALF_UNITS = UNITS // HALVES
+MATCH_ON_VECTOR = 3
+SCALE_ROWS = 4
+F32_BYTES = 4
+FIRST_PLANE_PIECES = (slice(0, 2 * P), slice(2 * P, HALF), slice(HALF, J))
+LAST_PLANE_PIECES = (slice(0, P), slice(P, 2 * P), slice(2 * P, HALF), slice(HALF, J))
 
 
 def tile_list_siluS_kernel(
@@ -38,6 +43,7 @@ def tile_list_siluS_kernel(
     nc = tc.nc
     with ExitStack() as ctx:
         keep = ctx.enter_context(tc.tile_pool(name="keep", bufs=1))
+        pages = ctx.enter_context(tc.tile_pool(name="pages", bufs=1))
         ring = ctx.enter_context(tc.tile_pool(name="ring", bufs=3))
         psum_k = ctx.enter_context(tc.psum_pool(name="psum_k", bufs=3))
         psum_v = ctx.enter_context(tc.psum_pool(name="psum_v", bufs=3))
@@ -52,9 +58,9 @@ def tile_list_siluS_kernel(
         pick = keep.tile([P, J // GROUP], U16, name="pick")
         place = keep.tile([P, J // GROUP], U16, name="place")
         wgt_sb = keep.tile([P, J], F32, name="wgt_sb")
-        planes = [keep.tile([P, T], F32, name=f"plane{q}", tag=f"plane{q}", align_bytes=64) for q in range(PASSES * PACK)]
-        wk_codes = keep.tile([P, PASSES, N], U32, name="wk_codes", align_bytes=64)
-        wv_codes = keep.tile([P, PASSES, 2 * N], U8, name="wv_codes", align_bytes=64)
+        planes = [keep.tile([P, T], F32, name=f"plane{q}", tag=f"plane{q}", align_bytes=64) for q in range(PLANES)]
+        wk_codes = [keep.tile([P, N], U32, name=f"wk_codes{a}", align_bytes=64) for a in range(PASSES)]
+        wv_codes = [keep.tile([P, 2 * N], U8, name=f"wv_codes{a}", align_bytes=64) for a in range(PASSES)]
         w_sc = keep.tile([P, 2, PASSES, N], U8, name="w_sc", align_bytes=64)
         wk_sc = w_sc[:, 0]
         wv_sc = w_sc[:, 1]
@@ -62,133 +68,161 @@ def tile_list_siluS_kernel(
         wgo_first = keep.tile([P, 1, P], F32, name="wgo_first")
         group_rows = keep.tile([P, P], F32, name="group_rows")
         wgo_t = keep.tile([P, P // 2], F32, name="wgo_t")
-        wgt_wide = keep.tile([P, J // P, GROUPS, GROUP], F32, name="wgt_wide")
+        wgt_wide = [
+            keep.tile([P, PLACE_TILES, GROUPS, GROUP], F32, name=f"wgt_wide{h}", tag=f"window{2 + h}")
+            for h in range(HALVES)
+        ]
         ident = keep.tile([P, P], F32, name="ident")
-        windows = [keep.tile([P, T], F32, name=f"window{r}") for r in range(ROW_TILES)]
+        zeros = pages.tile([P, P], F32, name="zeros", offset=F32_BYTES * (T - P // 2))
+        windows = []
         warm = keep.tile([P, 8], F32, name="warm")
 
-        nc.gpsimd.memset(warm[:], 0.0)
+        nc.vector.memset(zeros[:], 0.0)
+        nc.vector.memset(warm[:], 0.0)
         nc.scalar.activation(warm[:, 1:2], warm[:, 0:1], SILU)
-        make_identity(nc, ident[:])
-        for r in range(ROW_TILES):
-            nc.vector.memset(windows[r][:].bitcast(I32), 0)
+        nc.gpsimd.affine_select(
+            out=ident[:],
+            in_=zeros[:],
+            compare_op=mybir.AluOpType.not_equal,
+            fill=1.0,
+            base=0,
+            pattern=[[-1, P]],
+            channel_multiplier=1,
+        )
         nc.vector.memset(w_sc[:].rearrange("p w a n -> p (w a n)").bitcast(I32), 0)
+        for r in range(2):
+            windows.append(pages.tile([P, T], F32, name=f"window{r}", offset=F32_BYTES * T * r))
+            nc.vector.memset(windows[r][:].bitcast(I32), 0)
 
-        def load_scale_rows(tile, scales, r):
-            rows = scales.rearrange("a (q r) n -> r q a n", r=4)
-            nc.gpsimd.dma_start(out=tile[r:P:32, :, :].bitcast(I32), in_=rows[r].bitcast(I32))
-
-        scale_loads = [(wk_sc, wk_scales, r) for r in range(4)] + [(wv_sc, wv_scales, r) for r in range(4)]
-        for load in scale_loads:
-            load_scale_rows(*load)
+        for tile, scales in ((wk_sc, wk_scales), (wv_sc, wv_scales)):
+            rows = scales.rearrange("a (q r) n -> r q a n", r=SCALE_ROWS)
+            for r in range(SCALE_ROWS):
+                nc.gpsimd.dma_start(out=tile[r:P:32, :, :].bitcast(I32), in_=rows[r].bitcast(I32))
 
         for n, weights in enumerate((wgt, wgo)):
             nc.sync.dma_start(
                 out=group_rows[n * P // 2 : (n + 1) * P // 2, :],
-                in_=weights.rearrange("(g s) (u c) -> s g u c", s=GROUP, c=P)[0],
+                in_=weights.rearrange("(g s) (t c) -> s g t c", s=GROUP, c=P)[0],
             )
         nc.sync.dma_start(pick[:], offs)
         x_rows = xT.rearrange("(a p i) t -> p a i t", a=PASSES, i=PACK)
-        for q in range(PASSES * PACK):
+        for q in range(PLANES):
             nc.sync.dma_start(out=planes[q][:], in_=x_rows[:, q // PACK, q % PACK, :])
-        nc.sync.dma_start(out=wk_codes[:].bitcast(I32), in_=wk_words.rearrange("a p n t -> p a (n t)").bitcast(I32))
-        nc.sync.dma_start(out=wv_codes[:].bitcast(I32), in_=wv_words.rearrange("a p b -> p a b").bitcast(I32))
+
+        def load_weights(a):
+            words = wk_words[a].rearrange("p n i -> p (n i)")
+            nc.sync.dma_start(out=wk_codes[a][:].bitcast(I32), in_=words.bitcast(I32))
+            nc.sync.dma_start(out=wv_codes[a][:].bitcast(I32), in_=wv_words[a].bitcast(I32))
+
+        def unit_ranges(u):
+            if u < NARROW_UNITS:
+                return [(block(r), r, 0, block(u)) for r in range(ROW_TILES)]
+            if u < FIRST_HALF_UNITS:
+                first = 2 * (u - NARROW_UNITS)
+                return [(slice(n * 2 * P, (n + 1) * 2 * P), first + n, 0, LAST_PLANE_PIECES[2]) for n in range(2)]
+            return [(slice(0, HALF), u - FIRST_HALF_UNITS, 1, slice(0, HALF))]
+
         st_rows = st.rearrange("(r p) j -> p r j", p=P)
 
         def load_state(u):
-            if u < J_TILES:
-                nc.sync.dma_start(out=st_sb[u][:].rearrange("p (r j) -> p r j", j=P), in_=st_rows[:, :, block(u)])
+            ranges = unit_ranges(u)
+            span, first, h, cols = ranges[0]
+            places = slice(h * HALF + cols.start, h * HALF + cols.stop)
+            if len(ranges) == 1:
+                nc.sync.dma_start(out=st_sb[u][:], in_=st_rows[:, first, places])
             else:
-                nc.sync.dma_start(out=st_sb[u][:], in_=st_rows[:, u - J_TILES, half_cols(1)])
+                nc.sync.dma_start(
+                    out=st_sb[u][:].rearrange("p (r j) -> p r j", r=len(ranges)),
+                    in_=st_rows[:, first : first + len(ranges), places],
+                )
 
+        load_weights(0)
         load_state(0)
         nc.sync.dma_start(out=wgo_first[:, 0, :], in_=wgo[:, block(0)])
+        load_state(1)
+        load_weights(1)
         nc.sync.dma_start(place[:], offs2)
-        for u in range(1, UNITS):
+        for u in range(NARROW_UNITS, UNITS):
             load_state(u)
 
-        pairs = [keep.tile([P, 2, J], F32, name=f"pair{n}") for n in range(PASSES * PACK // 2)]
+        picked = keep.tile([P, PACK, J], F32, name="picked")
+        pairs = [keep.tile([P, 2, J], F32, name=f"pair{n}") for n in range(PACK // 2)]
         grouped_first = keep.tile([P, J, PACK], BF16, name="grouped_first", align_bytes=64)
-        grouped_chunk = [
-            keep.tile([P, c.stop - c.start, PACK], BF16, name=f"grouped_chunk{n}", align_bytes=64)
-            for n, c in enumerate(CHUNKS)
+        grouped_piece = [
+            keep.tile([P, c.stop - c.start, PACK], BF16, name=f"grouped_piece{n}", align_bytes=64)
+            for n, c in enumerate(LAST_PLANE_PIECES)
         ]
         x_codes = {}
         x_sc = {}
 
         def gather(q, cols=slice(0, J)):
-            dst = pairs[q // 2][:, q % 2, cols]
+            a, i = divmod(q, PACK)
+            dst = picked[:, i, cols] if a == 0 else pairs[i // 2][:, i % 2, cols]
             entries = pick[:, cols.start // GROUP : cols.stop // GROUP]
             nc.vector.tensor_tensor(dst, planes[q][:].indirect(entries), wgt_sb[:, cols], MULT)
 
+        def interleave(dst, src):
+            nc.scalar.copy(dst.rearrange("p (c u) i -> p c i u", u=4), src.rearrange("p i (c u) -> p c i u", u=4))
+
         def interleave_pair(dst, n, cols):
-            first = 2 * (n % 2)
-            nc.scalar.copy(dst[:, :, first : first + 2], pairs[n][:, :, cols].rearrange("p i c -> p c i"))
+            nc.scalar.copy(dst[:, :, 2 * n : 2 * n + 2], pairs[n][:, :, cols].rearrange("p i c -> p c i"))
 
         def quantise(key, src, tag):
             width = src.shape[1]
-            name = "_".join(str(k) for k in key)
-            x_codes[key] = keep.tile([P, width], U32, name=f"x_codes{name}", tag=tag, align_bytes=64)
-            x_sc[key] = keep.tile([P, width], U8, name=f"x_sc{name}", align_bytes=64)
+            x_codes[key] = keep.tile([P, width], U32, name=f"x_codes_{key}", tag=tag, align_bytes=64)
+            x_sc[key] = keep.tile([P, width], U8, name=f"x_sc_{key}", align_bytes=64)
             nc.vector.quantize_mx(
                 out=x_codes[key][:].bitcast(FP8X4), scales=x_sc[key][:], in_=src[:].rearrange("p c i -> p (c i)")
             )
 
         def x_operand(h, a, cols):
             cols = slice(h * HALF + cols.start, h * HALF + cols.stop)
+            key = "first"
             if a == 1:
-                n = [c.start <= cols.start < c.stop for c in CHUNKS].index(True)
-                key = (1, n)
-                cols = slice(cols.start - CHUNKS[n].start, cols.stop - CHUNKS[n].start)
-            else:
-                key = (0,)
+                key = [c.start <= cols.start < c.stop for c in LAST_PLANE_PIECES].index(True)
+                cols = slice(cols.start - LAST_PLANE_PIECES[key].start, cols.stop - LAST_PLANE_PIECES[key].start)
             return x_codes[key][:, cols].bitcast(FP8X4), x_sc[key][:, cols]
 
-        def unit_ranges(u):
-            if u < J_TILES:
-                return [(block(r), r, 0, block(u)) for r in range(ROW_TILES)]
-            return [(slice(0, HALF), u - J_TILES, 1, slice(0, HALF))]
-
-        def product(bank, u, codes, scales, bytes_per_col, fmt):
-            ranges = unit_ranges(u)
-            steps = [(a, rng) for a in range(PASSES) for rng in ranges]
+        def product(bank, u, codes, scales, units_per_col, fmt, passes):
+            steps = [(a, part) for a in range(PASSES) for part in unit_ranges(u)]
             for n, (a, (span, r, h, cols)) in enumerate(steps):
-                rhs, rhs_scale = x_operand(h, a, cols)
-                nc.tensor.matmul_mx(
-                    out=bank[:, span],
-                    lhsT=codes[:, a, bytes_per_col * r * P : bytes_per_col * (r + 1) * P].bitcast(fmt),
-                    lhsT_scale=scales[:, a, block(r)],
-                    rhs=rhs,
-                    rhs_scale=rhs_scale,
-                    start=(n == 0),
-                    stop=(n == len(steps) - 1),
-                )
+                if a in passes:
+                    rhs, rhs_scale = x_operand(h, a, cols)
+                    nc.tensor.matmul_mx(
+                        out=bank[:, span],
+                        lhsT=codes[a][:, units_per_col * r * P : units_per_col * (r + 1) * P].bitcast(fmt),
+                        lhsT_scale=scales[:, a, block(r)],
+                        rhs=rhs,
+                        rhs_scale=rhs_scale,
+                        start=(n == 0),
+                        stop=(n == len(steps) - 1),
+                    )
 
         keys = {}
-        gates = {}
-        values = {}
-        scaled = {}
-
-        def make_keys(u):
-            keys[u] = psum_k.tile([P, HALF], F32, name="ke")
-            product(keys[u], u, wk_codes, wk_sc, 1, FP8X4)
-
-        matches = {}
         key_sb = {}
+        matches = {}
+        gates = {}
+        sums = {}
+        scaled = {}
+        values = {}
+        results = {}
+
+        def make_keys(u, passes=range(PASSES)):
+            if passes[0] == 0:
+                keys[u] = psum_k.tile([P, HALF], F32, name="ke")
+            product(keys[u], u, wk_codes, wk_sc, 1, FP8X4, passes)
 
         def copy_keys(u):
             key_sb[u] = ring.tile([P, HALF], F32, name="key_sb")
             nc.scalar.copy(key_sb[u][:], keys[u][:])
 
         def make_match(u):
-            if u == 2:
-                matches[u] = keep.tile([P, HALF], F32, name="match2", tag="value0")
-            else:
+            if u < MATCH_ON_VECTOR:
                 matches[u] = ring.tile([P, HALF], F32, name="match")
-            if u >= 2:
-                nc.gpsimd.tensor_tensor(matches[u][:], key_sb[u][:], st_sb[u][:], MULT)
-            else:
                 nc.vector.tensor_tensor(matches[u][:], keys[u][:], st_sb[u][:], MULT)
+            else:
+                matches[u] = keep.tile([P, HALF], F32, name=f"match{u}", tag=f"value{u - 2}")
+                nc.gpsimd.tensor_tensor(matches[u][:], key_sb[u][:], st_sb[u][:], MULT)
 
         def make_gate(u):
             if u == 0:
@@ -197,13 +231,16 @@ def tile_list_siluS_kernel(
                 gates[u] = ring.tile([P, HALF], F32, name="gate")
             nc.scalar.activation(gates[u][:], matches[u][:], SILU)
 
+        def sums_first(passes):
+            if passes[0] == 0:
+                sums["first"] = psum_t.tile([P, HALF], F32, name="turned")
+            product(sums["first"], 0, wv_codes, wv_sc, 2, FP4X4, passes)
+
         def values_first():
-            ve = psum_t.tile([P, HALF], F32, name="turned")
-            product(ve, 0, wv_codes, wv_sc, 2, FP4X4)
             values[0] = keep.tile([P, HALF], F32, name="value0", tag="value0")
             nc.vector.tensor_tensor(
                 values[0][:].rearrange("p (r j) -> p r j", j=P),
-                ve[:].rearrange("p (r j) -> p r j", j=P),
+                sums["first"][:].rearrange("p (r j) -> p r j", j=P),
                 wgo_first[:].to_broadcast([P, ROW_TILES, P]),
                 MULT,
             )
@@ -211,57 +248,68 @@ def tile_list_siluS_kernel(
         def spread_group_weights():
             by_place = psum_k.tile([P, HALF], F32, name="ke")
             nc.tensor.transpose(by_place[:, 0:P], group_rows[:], ident[:])
-            wgt_t = by_place[:, 0 : P // 2].rearrange("p (g u o) -> p u g o", g=GROUPS, o=1)
-            for cols in FIRST_CHUNKS:
+            wgt_t = by_place[:, 0 : P // 2].rearrange("p (g t o) -> p t g o", g=GROUPS, o=1)
+            for cols in FIRST_PLANE_PIECES:
                 tiles = slice(cols.start // P, cols.stop // P)
                 count = tiles.stop - tiles.start
-                nc.scalar.copy(wgt_wide[:, tiles], wgt_t[:, tiles].to_broadcast([P, count, GROUPS, GROUP]))
+                first = tiles.start % PLACE_TILES
+                wide = wgt_wide[cols.start // HALF][:, first : first + count]
+                nc.scalar.copy(wide, wgt_t[:, tiles].to_broadcast([P, count, GROUPS, GROUP]))
                 turned = psum_v.tile([P, HALF], F32, name="ve")
                 for n in range(count):
-                    src = wgt_wide[:, tiles.start + n].rearrange("p g s -> p (g s)")
-                    nc.tensor.transpose(turned[:, block(n)], src, ident[:])
+                    nc.tensor.transpose(turned[:, block(n)], wide[:, n].rearrange("p g s -> p (g s)"), ident[:])
                 nc.scalar.copy(wgt_sb[:, cols], turned[:, 0 : count * P])
             nc.scalar.copy(wgo_t[:], by_place[:, P // 2 : P])
 
-        def values_by_token(h, jt):
-            bank = psum_v.tile([P, N], F32, name="ve")
-            for a in range(PASSES):
-                lhsT, lhsT_scale = x_operand(h, a, block(jt))
-                nc.tensor.matmul_mx(
-                    out=bank[:],
-                    lhsT=lhsT,
-                    lhsT_scale=lhsT_scale,
-                    rhs=wv_codes[:, a, :].bitcast(FP4X4),
-                    rhs_scale=wv_sc[:, a, :],
-                    start=(a == 0),
-                    stop=(a == PASSES - 1),
-                )
-            scaled[h, jt] = keep.tile([P, N], F32, name=f"scaled{h}{jt}")
-            src = bank[:].rearrange("p (r g c) -> p r g c", g=GROUPS, c=GROUP)
-            dst = scaled[h, jt][:].rearrange("p (r g c) -> p r g c", g=GROUPS, c=GROUP)
+        def sums_by_place(h, t, rows, passes=range(PASSES)):
+            if passes[0] == 0:
+                sums[h, t, rows[0]] = psum_v.tile([P, N], F32, name="ve")
+            spans = [slice(0, N)] if len(rows) == ROW_TILES else [block(r) for r in rows]
+            steps = [(a, span) for a in range(PASSES) for span in spans]
+            for n, (a, span) in enumerate(steps):
+                if a in passes:
+                    lhsT, lhsT_scale = x_operand(h, a, block(t))
+                    nc.tensor.matmul_mx(
+                        out=sums[h, t, rows[0]][:, span],
+                        lhsT=lhsT,
+                        lhsT_scale=lhsT_scale,
+                        rhs=wv_codes[a][:, 2 * span.start : 2 * span.stop].bitcast(FP4X4),
+                        rhs_scale=wv_sc[:, a, span],
+                        start=(n == 0),
+                        stop=(n == len(steps) - 1),
+                    )
+
+        def scale_by_place(h, t, rows=range(ROW_TILES)):
+            if (h, t, rows[0]) not in sums:
+                sums_by_place(h, t, rows)
+            if rows[0] == 0:
+                scaled[h, t] = keep.tile([P, N], F32, name=f"scaled{h}{t}")
+            row_tiles = slice(rows[0], rows[-1] + 1)
+            src = sums[h, t, rows[0]][:].rearrange("p (r g c) -> p r g c", g=GROUPS, c=GROUP)[:, row_tiles]
+            dst = scaled[h, t][:].rearrange("p (r g c) -> p r g c", g=GROUPS, c=GROUP)[:, row_tiles]
             for g in range(GROUPS):
-                col = g * (J // P) + h * J_TILES + jt
+                col = g * (J // P) + h * PLACE_TILES + t
                 nc.scalar.activation(dst[:, :, g, :], src[:, :, g, :], COPY, scale=wgo_t[:, col : col + 1])
 
         def values_turned(u):
             turned = psum_t.tile([P, HALF], F32, name="turned")
-            for n in range(HALF // P):
-                src = scaled[0, u][:, block(n)] if u < J_TILES else scaled[1, n][:, block(u - J_TILES)]
-                nc.tensor.transpose(turned[:, block(n)], src, ident[:])
-            values[u] = ring.tile([P, HALF], F32, name="value")
+            for span, r, h, cols in unit_ranges(u):
+                for n in range((cols.stop - cols.start) // P):
+                    src = scaled[h, cols.start // P + n][:, block(r)]
+                    nc.tensor.transpose(turned[:, block(span.start // P + n)], src, ident[:])
+            values[u] = keep.tile([P, HALF], F32, name=f"value{u}", tag=f"value{u}")
             nc.scalar.copy(values[u][:], turned[:])
 
-        results = {}
-
         def combine(u):
+            if u == 0:
+                results[u] = ring.tile([P, HALF], F32, name="result")
+                nc.vector.tensor_tensor(results[u][:, P:], gates[u][:, P:], values[u][:, P:], MULT)
+                return
             if u == 1:
                 results[u] = keep.tile([P, HALF], F32, name="result1", tag="gate0")
             else:
                 results[u] = ring.tile([P, HALF], F32, name="result")
-            if u > 0:
-                nc.gpsimd.tensor_tensor(results[u][:], gates[u][:], values[u][:], MULT)
-            else:
-                nc.vector.tensor_tensor(results[u][:, P:], gates[u][:, P:], values[u][:, P:], MULT)
+            nc.gpsimd.tensor_tensor(results[u][:], gates[u][:], values[u][:], MULT)
 
         def scatter(u):
             for span, r, h, cols in unit_ranges(u):
@@ -274,51 +322,70 @@ def tile_list_siluS_kernel(
                     nc.sync.dma_start(out=out[block(r), :], in_=windows[r][:])
 
         spread_group_weights()
-        for cols in FIRST_CHUNKS:
+        for r in range(2, ROW_TILES):
+            windows.append(keep.tile([P, T], F32, name=f"window{r}", tag=f"window{r}"))
+            nc.gpsimd.memset(windows[r][:].bitcast(I32), 0)
+
+        for cols in FIRST_PLANE_PIECES:
             gather(0, cols)
-        gather(1)
-        interleave_pair(grouped_first, 0, slice(0, J))
-        gather(2)
-        gather(3)
-        interleave_pair(grouped_first, 1, slice(0, J))
-        gather(4)
-        gather(5)
-        quantise((0,), grouped_first, "plane5")
-        for n, cols in enumerate(CHUNKS):
-            interleave_pair(grouped_chunk[n], 2, cols)
-        gather(6)
-        for n, cols in enumerate(CHUNKS):
-            gather(7, cols)
-            interleave_pair(grouped_chunk[n], 3, cols)
-        for n in range(3):
-            quantise((1, n), grouped_chunk[n], f"x_codes1{n}")
-        make_keys(0)
+        for q in range(1, PACK - 1):
+            gather(q)
+        for h in range(HALVES):
+            gather(PACK - 1, half_cols(h))
+            interleave(grouped_first[:, half_cols(h), :], picked[:, :, half_cols(h)])
+
+        gather(PACK)
+        gather(PACK + 1)
+        quantise("first", grouped_first, f"plane{PACK + 1}")
+        for n, cols in enumerate(LAST_PLANE_PIECES):
+            interleave_pair(grouped_piece[n], 0, cols)
+        gather(PACK + 2)
+        for n, cols in enumerate(LAST_PLANE_PIECES):
+            gather(PACK + 3, cols)
+            interleave_pair(grouped_piece[n], 1, cols)
+        second_half = len(LAST_PLANE_PIECES) - 1
+        for n in range(second_half):
+            quantise(n, grouped_piece[n], f"x_codes_{n}")
+
+        for a in range(PASSES):
+            make_keys(0, [a])
+            sums_first([a])
+            sums_by_place(0, 1, range(ROW_TILES), [a])
+            make_keys(1, [a])
+            make_keys(2, [a])
         make_match(0)
         values_first()
-        make_keys(1)
+        quantise(second_half, grouped_piece[second_half], "st0")
         make_match(1)
-        quantise((1, 3), grouped_chunk[3], "st0")
+        make_match(2)
         make_gate(0)
         combine(0)
-        make_gate(1)
-        values_by_token(0, 1)
+        scale_by_place(0, 1)
         values_turned(1)
-        make_keys(2)
-        copy_keys(2)
+        make_gate(1)
+
         for u in range(UNITS):
-            if u + 1 < UNITS:
+            if u + 1 == FIRST_HALF_UNITS:
                 combine(u + 1)
-            if u + 2 < UNITS:
+            if MATCH_ON_VECTOR <= u + 2 < UNITS:
                 make_match(u + 2)
+            if u + 1 < UNITS and u + 1 != FIRST_HALF_UNITS:
+                combine(u + 1)
             scatter(u)
-            if u + 2 < J_TILES:
-                values_by_token(0, u + 2)
+            if u + 2 == NARROW_UNITS:
+                for t in range(NARROW_UNITS, PLACE_TILES):
+                    scale_by_place(0, t)
+            if u + 2 == FIRST_HALF_UNITS:
+                for t in range(PLACE_TILES):
+                    scale_by_place(1, t, range(0, ROW_TILES // 2))
+                make_gate(u + 2)
+                values_turned(u + 2)
+            if u + 2 == FIRST_HALF_UNITS + ROW_TILES // 2:
+                for t in range(PLACE_TILES):
+                    scale_by_place(1, t, range(ROW_TILES // 2, ROW_TILES))
             if u + 3 < UNITS:
                 make_keys(u + 3)
                 copy_keys(u + 3)
-            if u + 2 < UNITS:
-                if u + 2 == J_TILES:
-                    for jt in range(J_TILES):
-                        values_by_token(1, jt)
+            if u + 2 < UNITS and u + 2 != FIRST_HALF_UNITS:
                 make_gate(u + 2)
                 values_turned(u + 2)

@@ -27,14 +27,13 @@ ROW_TILES = N // P
 GROUPS = 8
 GROUP = P // GROUPS
 PLACE_TILES = HALF // P
-UNITS = N * J // (P * HALF)
-NARROW_UNITS = 2
-FIRST_HALF_UNITS = UNITS // HALVES
-MATCH_ON_VECTOR = 3
+PLACE_UNITS = 5
+UNITS = PLACE_UNITS + ROW_TILES
 SCALE_ROWS = 4
 F32_BYTES = 4
 FIRST_PLANE_PIECES = (slice(0, 2 * P), slice(2 * P, HALF), slice(HALF, J))
-LAST_PLANE_PIECES = (slice(0, P), slice(P, 2 * P), slice(2 * P, HALF), slice(HALF, J))
+PIECES = (slice(0, P), slice(P, 2 * P), slice(2 * P, HALF), slice(HALF, HALF + 2 * P), slice(HALF + 2 * P, J))
+PAIR_STEP = HALF + 2 * P
 
 
 def tile_list_siluS_kernel(
@@ -45,9 +44,8 @@ def tile_list_siluS_kernel(
         keep = ctx.enter_context(tc.tile_pool(name="keep", bufs=1))
         pages = ctx.enter_context(tc.tile_pool(name="pages", bufs=1))
         ring = ctx.enter_context(tc.tile_pool(name="ring", bufs=3))
-        psum_k = ctx.enter_context(tc.psum_pool(name="psum_k", bufs=3))
+        psum_k = ctx.enter_context(tc.psum_pool(name="psum_k", bufs=1))
         psum_v = ctx.enter_context(tc.psum_pool(name="psum_v", bufs=3))
-        psum_t = ctx.enter_context(tc.psum_pool(name="psum_t", bufs=2))
 
         def half_cols(h):
             return slice(h * HALF, (h + 1) * HALF)
@@ -64,8 +62,12 @@ def tile_list_siluS_kernel(
         w_sc = keep.tile([P, 2, PASSES, N], U8, name="w_sc", align_bytes=64)
         wk_sc = w_sc[:, 0]
         wv_sc = w_sc[:, 1]
-        st_sb = [keep.tile([P, HALF], F32, name=f"st{u}", tag=f"st{u}", align_bytes=64) for u in range(UNITS)]
-        wgo_first = keep.tile([P, 1, P], F32, name="wgo_first")
+        pair_late = keep.tile([P, HALF + 2 * PAIR_STEP], F32, name="pair_late", tag="pair_late", align_bytes=64)
+        late_half = [
+            pair_late[:, h * HALF : h * HALF + 2 * PAIR_STEP].rearrange("p (i c) -> p i c", i=2) for h in range(HALVES)
+        ]
+        st_sb = [keep.tile([P, HALF], F32, name=f"st{u}", tag=f"st{u}", align_bytes=64)[:] for u in range(UNITS)]
+        wgo_head = late_half[1][:, 1, 2 * P - 1 : 2 * P + 1]
         group_rows = keep.tile([P, P], F32, name="group_rows")
         wgo_t = keep.tile([P, P // 2], F32, name="wgo_t")
         wgt_wide = [
@@ -109,94 +111,85 @@ def tile_list_siluS_kernel(
         for q in range(PLANES):
             nc.sync.dma_start(out=planes[q][:], in_=x_rows[:, q // PACK, q % PACK, :])
 
-        def load_weights(a):
-            words = wk_words[a].rearrange("p n i -> p (n i)")
-            nc.sync.dma_start(out=wk_codes[a][:].bitcast(I32), in_=words.bitcast(I32))
+        def load_values_weight(a):
             nc.sync.dma_start(out=wv_codes[a][:].bitcast(I32), in_=wv_words[a].bitcast(I32))
 
-        def unit_ranges(u):
-            if u < NARROW_UNITS:
-                return [(block(r), r, 0, block(u)) for r in range(ROW_TILES)]
-            if u < FIRST_HALF_UNITS:
-                first = 2 * (u - NARROW_UNITS)
-                return [(slice(n * 2 * P, (n + 1) * 2 * P), first + n, 0, LAST_PLANE_PIECES[2]) for n in range(2)]
-            return [(slice(0, HALF), u - FIRST_HALF_UNITS, 1, slice(0, HALF))]
+        def load_keys_weight(a):
+            words = wk_words[a].rearrange("p n i -> p (n i)")
+            nc.sync.dma_start(out=wk_codes[a][:].bitcast(I32), in_=words.bitcast(I32))
+
+        def unit_parts(u):
+            if u < PLACE_UNITS:
+                return [(block(r), r, block(u)) for r in range(ROW_TILES)]
+            return [(slice(0, J - PLACE_UNITS * P), u - PLACE_UNITS, slice(PLACE_UNITS * P, J))]
+
+        def unit_cols(u):
+            return slice(0, unit_parts(u)[-1][0].stop)
 
         st_rows = st.rearrange("(r p) j -> p r j", p=P)
 
         def load_state(u):
-            ranges = unit_ranges(u)
-            span, first, h, cols = ranges[0]
-            places = slice(h * HALF + cols.start, h * HALF + cols.stop)
-            if len(ranges) == 1:
-                nc.sync.dma_start(out=st_sb[u][:], in_=st_rows[:, first, places])
+            parts = unit_parts(u)
+            span, first, places = parts[0]
+            if len(parts) == 1:
+                nc.sync.dma_start(out=st_sb[u][:, span], in_=st_rows[:, first, places])
             else:
                 nc.sync.dma_start(
-                    out=st_sb[u][:].rearrange("p (r j) -> p r j", r=len(ranges)),
-                    in_=st_rows[:, first : first + len(ranges), places],
+                    out=st_sb[u].rearrange("p (r j) -> p r j", r=len(parts)),
+                    in_=st_rows[:, first : first + len(parts), places],
                 )
 
-        load_weights(0)
         load_state(0)
-        nc.sync.dma_start(out=wgo_first[:, 0, :], in_=wgo[:, block(0)])
+        for a in range(PASSES):
+            load_values_weight(a)
+            load_keys_weight(a)
         load_state(1)
-        load_weights(1)
         nc.sync.dma_start(place[:], offs2)
-        for u in range(NARROW_UNITS, UNITS):
+        for u in range(2, UNITS):
             load_state(u)
 
-        picked = keep.tile([P, PACK, J], F32, name="picked")
-        pairs = [keep.tile([P, 2, J], F32, name=f"pair{n}") for n in range(PACK // 2)]
-        grouped_first = keep.tile([P, J, PACK], BF16, name="grouped_first", align_bytes=64)
+        picked = keep.tile([P, PACK, J], F32, name="picked", tag="picked", align_bytes=64)
+        pair_early = keep.tile([P, 2, J], F32, name="pair_early")
+        grouped_first = [keep.tile([P, HALF, PACK], BF16, name=f"grouped_first{h}", align_bytes=64) for h in range(HALVES)]
         grouped_piece = [
-            keep.tile([P, c.stop - c.start, PACK], BF16, name=f"grouped_piece{n}", align_bytes=64)
-            for n, c in enumerate(LAST_PLANE_PIECES)
+            keep.tile([P, c.stop - c.start, PACK], BF16, name=f"grouped_piece{n}", tag=f"grouped{n}", align_bytes=64)
+            for n, c in enumerate(PIECES)
         ]
         x_codes = {}
         x_sc = {}
 
+        def pair_view(n, cols):
+            if n == 0:
+                return pair_early[:, :, cols]
+            h = cols.start // HALF
+            return late_half[h][:, :, cols.start - h * HALF : cols.stop - h * HALF]
+
         def gather(q, cols=slice(0, J)):
             a, i = divmod(q, PACK)
-            dst = picked[:, i, cols] if a == 0 else pairs[i // 2][:, i % 2, cols]
+            dst = picked[:, i, cols] if a == 0 else pair_view(i // 2, cols)[:, i % 2, :]
             entries = pick[:, cols.start // GROUP : cols.stop // GROUP]
             nc.vector.tensor_tensor(dst, planes[q][:].indirect(entries), wgt_sb[:, cols], MULT)
 
         def interleave(dst, src):
             nc.scalar.copy(dst.rearrange("p (c u) i -> p c i u", u=4), src.rearrange("p i (c u) -> p c i u", u=4))
 
-        def interleave_pair(dst, n, cols):
-            nc.scalar.copy(dst[:, :, 2 * n : 2 * n + 2], pairs[n][:, :, cols].rearrange("p i c -> p c i"))
+        def interleave_pair(n, piece):
+            src = pair_view(n, PIECES[piece]).rearrange("p i c -> p c i")
+            nc.scalar.copy(grouped_piece[piece][:, :, 2 * n : 2 * n + 2], src)
 
-        def quantise(key, src, tag):
+        def quantise(key, src, codes_tag, scales_tag):
             width = src.shape[1]
-            x_codes[key] = keep.tile([P, width], U32, name=f"x_codes_{key}", tag=tag, align_bytes=64)
-            x_sc[key] = keep.tile([P, width], U8, name=f"x_sc_{key}", align_bytes=64)
+            x_codes[key] = keep.tile([P, width], U32, name=f"x_codes_{key[0]}_{key[1]}", tag=codes_tag, align_bytes=64)
+            x_sc[key] = keep.tile([P, width], U8, name=f"x_sc_{key[0]}_{key[1]}", tag=scales_tag, align_bytes=64)
             nc.vector.quantize_mx(
                 out=x_codes[key][:].bitcast(FP8X4), scales=x_sc[key][:], in_=src[:].rearrange("p c i -> p (c i)")
             )
 
-        def x_operand(h, a, cols):
-            cols = slice(h * HALF + cols.start, h * HALF + cols.stop)
-            key = "first"
-            if a == 1:
-                key = [c.start <= cols.start < c.stop for c in LAST_PLANE_PIECES].index(True)
-                cols = slice(cols.start - LAST_PLANE_PIECES[key].start, cols.stop - LAST_PLANE_PIECES[key].start)
-            return x_codes[key][:, cols].bitcast(FP8X4), x_sc[key][:, cols]
-
-        def product(bank, u, codes, scales, units_per_col, fmt, passes):
-            steps = [(a, part) for a in range(PASSES) for part in unit_ranges(u)]
-            for n, (a, (span, r, h, cols)) in enumerate(steps):
-                if a in passes:
-                    rhs, rhs_scale = x_operand(h, a, cols)
-                    nc.tensor.matmul_mx(
-                        out=bank[:, span],
-                        lhsT=codes[a][:, units_per_col * r * P : units_per_col * (r + 1) * P].bitcast(fmt),
-                        lhsT_scale=scales[:, a, block(r)],
-                        rhs=rhs,
-                        rhs_scale=rhs_scale,
-                        start=(n == 0),
-                        stop=(n == len(steps) - 1),
-                    )
+        def x_operand(a, places):
+            pieces = [half_cols(h) for h in range(HALVES)] if a == 0 else PIECES
+            n = [c.start <= places.start < c.stop for c in pieces].index(True)
+            cols = slice(places.start - pieces[n].start, places.stop - pieces[n].start)
+            return x_codes[a, n][:, cols].bitcast(FP8X4), x_sc[a, n][:, cols]
 
         keys = {}
         key_sb = {}
@@ -204,49 +197,65 @@ def tile_list_siluS_kernel(
         gates = {}
         sums = {}
         scaled = {}
+        turned = {}
         values = {}
         results = {}
 
+        taken = []
+
+        def next_bank(name, first=None):
+            if first is None:
+                first = len(taken) % 5
+                taken.append(name)
+            return psum_k.tile([P, HALF], F32, name=name, tag=f"bank{first}")
+
         def make_keys(u, passes=range(PASSES)):
             if passes[0] == 0:
-                keys[u] = psum_k.tile([P, HALF], F32, name="ke")
-            product(keys[u], u, wk_codes, wk_sc, 1, FP8X4, passes)
+                keys[u] = next_bank("ke", {0: 1, 1: 4}.get(u))
+            runs = []
+            for span, r, places in unit_parts(u):
+                for c in PIECES:
+                    start, stop = max(c.start, places.start), min(c.stop, places.stop)
+                    if start < stop:
+                        first = span.start + start - places.start
+                        runs.append((slice(first, first + stop - start), r, slice(start, stop)))
+            steps = [(a, run) for a in range(PASSES) for run in runs]
+            for n, (a, (span, r, places)) in enumerate(steps):
+                if a in passes:
+                    rhs, rhs_scale = x_operand(a, places)
+                    nc.tensor.matmul_mx(
+                        out=keys[u][:, span],
+                        lhsT=wk_codes[a][:, block(r)].bitcast(FP8X4),
+                        lhsT_scale=wk_sc[:, a, block(r)],
+                        rhs=rhs,
+                        rhs_scale=rhs_scale,
+                        start=(n == 0),
+                        stop=(n == len(steps) - 1),
+                    )
 
         def copy_keys(u):
-            key_sb[u] = ring.tile([P, HALF], F32, name="key_sb")
-            nc.scalar.copy(key_sb[u][:], keys[u][:])
+            key_sb[u] = keep.tile([P, HALF], F32, name=f"key{u}", tag="st0" if u % 2 else "key_even", align_bytes=64)
+            nc.scalar.copy(key_sb[u][:, unit_cols(u)], keys[u][:, unit_cols(u)])
 
         def make_match(u):
-            if u < MATCH_ON_VECTOR:
-                matches[u] = ring.tile([P, HALF], F32, name="match")
-                nc.vector.tensor_tensor(matches[u][:], keys[u][:], st_sb[u][:], MULT)
-            else:
-                matches[u] = keep.tile([P, HALF], F32, name=f"match{u}", tag=f"value{u - 2}")
-                nc.gpsimd.tensor_tensor(matches[u][:], key_sb[u][:], st_sb[u][:], MULT)
+            cols = unit_cols(u)
+            if u == 0:
+                matches[u] = keep.tile([P, HALF], F32, name="match0", tag="match0", align_bytes=64)
+                nc.vector.tensor_tensor(matches[u][:], keys[u][:], st_sb[u], MULT)
+                return
+            tag = {1: f"grouped{len(PIECES) - 1}", 2: "gate0"}.get(u, f"value{u - 2}")
+            matches[u] = keep.tile([P, HALF], F32, name=f"match{u}", tag=tag, align_bytes=64)
+            nc.gpsimd.tensor_tensor(matches[u][:, cols], key_sb[u][:, cols], st_sb[u][:, cols], MULT)
 
         def make_gate(u):
-            if u == 0:
-                gates[u] = keep.tile([P, HALF], F32, name="gate0", tag="gate0")
+            if u in (0, 2, 3):
+                gates[u] = keep.tile([P, HALF], F32, name=f"gate{u}", tag=f"gate{u}", align_bytes=64)
             else:
                 gates[u] = ring.tile([P, HALF], F32, name="gate")
-            nc.scalar.activation(gates[u][:], matches[u][:], SILU)
-
-        def sums_first(passes):
-            if passes[0] == 0:
-                sums["first"] = psum_t.tile([P, HALF], F32, name="turned")
-            product(sums["first"], 0, wv_codes, wv_sc, 2, FP4X4, passes)
-
-        def values_first():
-            values[0] = keep.tile([P, HALF], F32, name="value0", tag="value0")
-            nc.vector.tensor_tensor(
-                values[0][:].rearrange("p (r j) -> p r j", j=P),
-                sums["first"][:].rearrange("p (r j) -> p r j", j=P),
-                wgo_first[:].to_broadcast([P, ROW_TILES, P]),
-                MULT,
-            )
+            nc.scalar.activation(gates[u][:, unit_cols(u)], matches[u][:, unit_cols(u)], SILU)
 
         def spread_group_weights():
-            by_place = psum_k.tile([P, HALF], F32, name="ke")
+            by_place = next_bank("by_place", 0)
             nc.tensor.transpose(by_place[:, 0:P], group_rows[:], ident[:])
             wgt_t = by_place[:, 0 : P // 2].rearrange("p (g t o) -> p t g o", g=GROUPS, o=1)
             for cols in FIRST_PLANE_PIECES:
@@ -255,70 +264,66 @@ def tile_list_siluS_kernel(
                 first = tiles.start % PLACE_TILES
                 wide = wgt_wide[cols.start // HALF][:, first : first + count]
                 nc.scalar.copy(wide, wgt_t[:, tiles].to_broadcast([P, count, GROUPS, GROUP]))
-                turned = psum_v.tile([P, HALF], F32, name="ve")
+                back = psum_v.tile([P, HALF], F32, name="ve")
                 for n in range(count):
-                    nc.tensor.transpose(turned[:, block(n)], wide[:, n].rearrange("p g s -> p (g s)"), ident[:])
-                nc.scalar.copy(wgt_sb[:, cols], turned[:, 0 : count * P])
+                    nc.tensor.transpose(back[:, block(n)], wide[:, n].rearrange("p g s -> p (g s)"), ident[:])
+                nc.scalar.copy(wgt_sb[:, cols], back[:, 0 : count * P])
+            nc.scalar.copy(wgo_head, by_place[:, P // 2 : P // 2 + 2 * GROUPS : GROUPS])
             nc.scalar.copy(wgo_t[:], by_place[:, P // 2 : P])
 
-        def sums_by_place(h, t, rows, passes=range(PASSES)):
+        def sums_by_place(t, passes=range(PASSES)):
             if passes[0] == 0:
-                sums[h, t, rows[0]] = psum_v.tile([P, N], F32, name="ve")
-            spans = [slice(0, N)] if len(rows) == ROW_TILES else [block(r) for r in rows]
-            steps = [(a, span) for a in range(PASSES) for span in spans]
-            for n, (a, span) in enumerate(steps):
-                if a in passes:
-                    lhsT, lhsT_scale = x_operand(h, a, block(t))
-                    nc.tensor.matmul_mx(
-                        out=sums[h, t, rows[0]][:, span],
-                        lhsT=lhsT,
-                        lhsT_scale=lhsT_scale,
-                        rhs=wv_codes[a][:, 2 * span.start : 2 * span.stop].bitcast(FP4X4),
-                        rhs_scale=wv_sc[:, a, span],
-                        start=(n == 0),
-                        stop=(n == len(steps) - 1),
-                    )
+                sums[t] = next_bank("ve", {0: 2, 1: 3}.get(t))
+            for a in passes:
+                lhsT, lhsT_scale = x_operand(a, block(t))
+                nc.tensor.matmul_mx(
+                    out=sums[t][:],
+                    lhsT=lhsT,
+                    lhsT_scale=lhsT_scale,
+                    rhs=wv_codes[a][:].bitcast(FP4X4),
+                    rhs_scale=wv_sc[:, a, :],
+                    start=(a == 0),
+                    stop=(a == PASSES - 1),
+                )
 
-        def scale_by_place(h, t, rows=range(ROW_TILES)):
-            if (h, t, rows[0]) not in sums:
-                sums_by_place(h, t, rows)
-            if rows[0] == 0:
-                scaled[h, t] = keep.tile([P, N], F32, name=f"scaled{h}{t}")
-            row_tiles = slice(rows[0], rows[-1] + 1)
-            src = sums[h, t, rows[0]][:].rearrange("p (r g c) -> p r g c", g=GROUPS, c=GROUP)[:, row_tiles]
-            dst = scaled[h, t][:].rearrange("p (r g c) -> p r g c", g=GROUPS, c=GROUP)[:, row_tiles]
+        spent = ["plane0", "plane1", "st1", "st2", "st3", "gate2", "st4", "gate3"]
+
+        def scale_by_place(t):
+            if t not in sums:
+                sums_by_place(t)
+            scaled[t] = keep.tile([P, N], F32, name=f"scaled{t}", tag=spent[t], align_bytes=64)
+            src = sums[t][:].rearrange("p (r g c) -> p r g c", g=GROUPS, c=GROUP)
+            dst = scaled[t][:].rearrange("p (r g c) -> p r g c", g=GROUPS, c=GROUP)
             for g in range(GROUPS):
-                col = g * (J // P) + h * PLACE_TILES + t
-                nc.scalar.activation(dst[:, :, g, :], src[:, :, g, :], COPY, scale=wgo_t[:, col : col + 1])
+                col = g * (J // P) + t
+                nc.scalar.activation(dst[:, :, g, :], src[:, :, g, :], COPY, scale=wgo_head[:, g : g + 1] if t == 0 and g < 2 else wgo_t[:, col : col + 1])
 
-        def values_turned(u):
-            turned = psum_t.tile([P, HALF], F32, name="turned")
-            for span, r, h, cols in unit_ranges(u):
-                for n in range((cols.stop - cols.start) // P):
-                    src = scaled[h, cols.start // P + n][:, block(r)]
-                    nc.tensor.transpose(turned[:, block(span.start // P + n)], src, ident[:])
-            values[u] = keep.tile([P, HALF], F32, name=f"value{u}", tag=f"value{u}")
-            nc.scalar.copy(values[u][:], turned[:])
+        def turn_values(u):
+            turned[u] = next_bank("turned", {0: 1, 1: 4}.get(u))
+            for span, r, places in unit_parts(u):
+                for n in range((places.stop - places.start) // P):
+                    src = scaled[places.start // P + n][:, block(r)]
+                    nc.tensor.transpose(turned[u][:, block(span.start // P + n)], src, ident[:])
+
+        def copy_values(u):
+            values[u] = keep.tile([P, HALF], F32, name=f"value{u}", tag=f"value{u}", align_bytes=64)
+            nc.scalar.copy(values[u][:, unit_cols(u)], turned[u][:, unit_cols(u)])
 
         def combine(u):
+            cols = unit_cols(u)
             if u == 0:
-                results[u] = ring.tile([P, HALF], F32, name="result")
-                nc.vector.tensor_tensor(results[u][:, P:], gates[u][:, P:], values[u][:, P:], MULT)
+                results[u] = keep.tile([P, HALF], F32, name="result0", tag="pair_late", align_bytes=64)
+                nc.vector.tensor_tensor(results[u][:], turned[u][:], gates[u][:], MULT)
                 return
-            if u == 1:
-                results[u] = keep.tile([P, HALF], F32, name="result1", tag="gate0")
-            else:
-                results[u] = ring.tile([P, HALF], F32, name="result")
-            nc.gpsimd.tensor_tensor(results[u][:], gates[u][:], values[u][:], MULT)
+            results[u] = ring.tile([P, HALF], F32, name="result")
+            for part in (slice(0, 2 * P), slice(2 * P, HALF)) if u == 1 else (cols,):
+                nc.gpsimd.tensor_tensor(results[u][:, part], gates[u][:, part], values[u][:, part], MULT)
 
         def scatter(u):
-            for span, r, h, cols in unit_ranges(u):
-                entries = place[:, (h * HALF + cols.start) // GROUP : (h * HALF + cols.stop) // GROUP]
-                if (u, r) == (0, 0):
-                    nc.vector.tensor_tensor(windows[r][:].indirect(entries), gates[u][:, span], values[u][:, span], MULT)
-                else:
-                    nc.vector.tensor_copy(windows[r][:].indirect(entries), results[u][:, span])
-                if h == HALVES - 1:
+            for span, r, places in unit_parts(u):
+                entries = place[:, places.start // GROUP : places.stop // GROUP]
+                nc.vector.tensor_copy(windows[r][:].indirect(entries), results[u][:, span])
+                if places.stop == J:
                     nc.sync.dma_start(out=out[block(r), :], in_=windows[r][:])
 
         spread_group_weights()
@@ -332,60 +337,64 @@ def tile_list_siluS_kernel(
             gather(q)
         for h in range(HALVES):
             gather(PACK - 1, half_cols(h))
-            interleave(grouped_first[:, half_cols(h), :], picked[:, :, half_cols(h)])
+            interleave(grouped_first[h][:], picked[:, :, half_cols(h)])
 
-        gather(PACK)
-        gather(PACK + 1)
-        quantise("first", grouped_first, f"plane{PACK + 1}")
-        for n, cols in enumerate(LAST_PLANE_PIECES):
-            interleave_pair(grouped_piece[n], 0, cols)
-        gather(PACK + 2)
-        for n, cols in enumerate(LAST_PLANE_PIECES):
-            gather(PACK + 3, cols)
-            interleave_pair(grouped_piece[n], 1, cols)
-        second_half = len(LAST_PLANE_PIECES) - 1
-        for n in range(second_half):
-            quantise(n, grouped_piece[n], f"x_codes_{n}")
-
-        for a in range(PASSES):
-            make_keys(0, [a])
-            sums_first([a])
-            sums_by_place(0, 1, range(ROW_TILES), [a])
-            make_keys(1, [a])
-            make_keys(2, [a])
+        gather(4)
+        gather(5, half_cols(0))
+        for n in range(3):
+            interleave_pair(0, n)
+        gather(5, half_cols(1))
+        for n in range(3, 5):
+            interleave_pair(0, n)
+        quantise((0, 0), grouped_first[0], "plane5", "x_sc00")
+        gather(6, half_cols(0))
+        gather(7, slice(0, 2 * P))
+        interleave_pair(1, 0)
+        interleave_pair(1, 1)
+        gather(7, PIECES[2])
+        quantise((1, 0), grouped_piece[0], "codes_a", "scales_a")
+        quantise((1, 1), grouped_piece[1], "codes_b", "scales_b")
+        gather(6, half_cols(1))
+        interleave_pair(1, 2)
+        sums_by_place(0)
+        make_keys(0)
+        scale_by_place(0)
+        make_keys(1)
+        sums_by_place(1)
+        for n in range(3, 5):
+            gather(7, PIECES[n])
+            interleave_pair(1, n)
         make_match(0)
-        values_first()
-        quantise(second_half, grouped_piece[second_half], "st0")
-        make_match(1)
-        make_match(2)
         make_gate(0)
+        turn_values(0)
+        copy_keys(1)
+        quantise((0, 1), grouped_first[1], "codes_a", "x_sc01")
+        quantise((1, 2), grouped_piece[2], "codes_b", "scales_c")
+        quantise((1, 3), grouped_piece[3], "codes_d", "scales_a")
+        quantise((1, 4), grouped_piece[4], "codes_e", "scales_b")
         combine(0)
-        scale_by_place(0, 1)
-        values_turned(1)
+        make_match(1)
+        scale_by_place(1)
+        turn_values(1)
+        make_keys(2)
+        copy_keys(2)
+        copy_values(1)
         make_gate(1)
 
         for u in range(UNITS):
-            if u + 1 == FIRST_HALF_UNITS:
-                combine(u + 1)
-            if MATCH_ON_VECTOR <= u + 2 < UNITS:
+            if u + 2 < UNITS:
                 make_match(u + 2)
-            if u + 1 < UNITS and u + 1 != FIRST_HALF_UNITS:
+            if u + 1 < UNITS:
                 combine(u + 1)
             scatter(u)
-            if u + 2 == NARROW_UNITS:
-                for t in range(NARROW_UNITS, PLACE_TILES):
-                    scale_by_place(0, t)
-            if u + 2 == FIRST_HALF_UNITS:
-                for t in range(PLACE_TILES):
-                    scale_by_place(1, t, range(0, ROW_TILES // 2))
-                make_gate(u + 2)
-                values_turned(u + 2)
-            if u + 2 == FIRST_HALF_UNITS + ROW_TILES // 2:
-                for t in range(PLACE_TILES):
-                    scale_by_place(1, t, range(ROW_TILES // 2, ROW_TILES))
             if u + 3 < UNITS:
                 make_keys(u + 3)
                 copy_keys(u + 3)
-            if u + 2 < UNITS and u + 2 != FIRST_HALF_UNITS:
+            if u + 2 < UNITS:
+                places = unit_parts(u + 2)[0][2]
+                for t in range(places.start // P, places.stop // P):
+                    if t not in scaled:
+                        scale_by_place(t)
                 make_gate(u + 2)
-                values_turned(u + 2)
+                turn_values(u + 2)
+                copy_values(u + 2)

@@ -33,6 +33,7 @@ SCALE_ROWS = 4
 F32_BYTES = 4
 FIRST_PLANE_PIECES = (slice(0, 2 * P), slice(2 * P, HALF), slice(HALF, J))
 PIECES = (slice(0, P), slice(P, 2 * P), slice(2 * P, HALF), slice(HALF, HALF + 2 * P), slice(HALF + 2 * P, J))
+QUANTISED = PIECES[:3] + (slice(HALF, J),)
 PAIR_STEP = HALF + 2 * P
 
 
@@ -71,11 +72,11 @@ def tile_list_siluS_kernel(
         group_rows = keep.tile([P, P], F32, name="group_rows")
         wgo_t = keep.tile([P, P // 2], F32, name="wgo_t")
         wgt_wide = [
-            keep.tile([P, PLACE_TILES, GROUPS, GROUP], F32, name=f"wgt_wide{h}", tag=f"window{2 + h}")
-            for h in range(HALVES)
+            keep.tile([P, (c.stop - c.start) // P, GROUPS, GROUP], F32, name=f"wgt_wide{n}", tag=f"window{1 + n}")
+            for n, c in enumerate(FIRST_PLANE_PIECES)
         ]
         ident = keep.tile([P, P], F32, name="ident")
-        zeros = pages.tile([P, P], F32, name="zeros", offset=F32_BYTES * (T - P // 2))
+        zeros = pages.tile([P, P], F32, name="zeros", offset=0)
         windows = []
         warm = keep.tile([P, 8], F32, name="warm")
 
@@ -92,9 +93,8 @@ def tile_list_siluS_kernel(
             channel_multiplier=1,
         )
         nc.vector.memset(w_sc[:].rearrange("p w a n -> p (w a n)").bitcast(I32), 0)
-        for r in range(2):
-            windows.append(pages.tile([P, T], F32, name=f"window{r}", offset=F32_BYTES * T * r))
-            nc.vector.memset(windows[r][:].bitcast(I32), 0)
+        windows.append(pages.tile([P, T], F32, name="window0", offset=0))
+        nc.vector.memset(windows[0][:].bitcast(I32), 0)
 
         for tile, scales in ((wk_sc, wk_scales), (wv_sc, wv_scales)):
             rows = scales.rearrange("a (q r) n -> r q a n", r=SCALE_ROWS)
@@ -106,10 +106,11 @@ def tile_list_siluS_kernel(
                 out=group_rows[n * P // 2 : (n + 1) * P // 2, :],
                 in_=weights.rearrange("(g s) (t c) -> s g t c", s=GROUP, c=P)[0],
             )
-        nc.sync.dma_start(pick[:], offs)
         x_rows = xT.rearrange("(a p i) t -> p a i t", a=PASSES, i=PACK)
         for q in range(PLANES):
             nc.sync.dma_start(out=planes[q][:], in_=x_rows[:, q // PACK, q % PACK, :])
+            if q == 0:
+                nc.sync.dma_start(pick[:], offs)
 
         def load_values_weight(a):
             nc.sync.dma_start(out=wv_codes[a][:].bitcast(I32), in_=wv_words[a].bitcast(I32))
@@ -153,7 +154,7 @@ def tile_list_siluS_kernel(
         grouped_first = [keep.tile([P, HALF, PACK], BF16, name=f"grouped_first{h}", align_bytes=64) for h in range(HALVES)]
         grouped_piece = [
             keep.tile([P, c.stop - c.start, PACK], BF16, name=f"grouped_piece{n}", tag=f"grouped{n}", align_bytes=64)
-            for n, c in enumerate(PIECES)
+            for n, c in enumerate(QUANTISED)
         ]
         x_codes = {}
         x_sc = {}
@@ -175,7 +176,10 @@ def tile_list_siluS_kernel(
 
         def interleave_pair(n, piece):
             src = pair_view(n, PIECES[piece]).rearrange("p i c -> p c i")
-            nc.scalar.copy(grouped_piece[piece][:, :, 2 * n : 2 * n + 2], src)
+            cols = PIECES[piece]
+            whole = min(piece, len(QUANTISED) - 1)
+            first = QUANTISED[whole].start
+            nc.scalar.copy(grouped_piece[whole][:, cols.start - first : cols.stop - first, 2 * n : 2 * n + 2], src)
 
         def quantise(key, src, codes_tag, scales_tag):
             width = src.shape[1]
@@ -186,7 +190,7 @@ def tile_list_siluS_kernel(
             )
 
         def x_operand(a, places):
-            pieces = [half_cols(h) for h in range(HALVES)] if a == 0 else PIECES
+            pieces = [half_cols(h) for h in range(HALVES)] if a == 0 else QUANTISED
             n = [c.start <= places.start < c.stop for c in pieces].index(True)
             cols = slice(places.start - pieces[n].start, places.stop - pieces[n].start)
             return x_codes[a, n][:, cols].bitcast(FP8X4), x_sc[a, n][:, cols]
@@ -243,7 +247,7 @@ def tile_list_siluS_kernel(
                 matches[u] = keep.tile([P, HALF], F32, name="match0", tag="match0", align_bytes=64)
                 nc.vector.tensor_tensor(matches[u][:], keys[u][:], st_sb[u], MULT)
                 return
-            tag = {1: f"grouped{len(PIECES) - 1}", 2: "gate0"}.get(u, f"value{u - 2}")
+            tag = {1: "grouped3", 2: "gate0"}.get(u, f"value{u - 2}")
             matches[u] = keep.tile([P, HALF], F32, name=f"match{u}", tag=tag, align_bytes=64)
             nc.gpsimd.tensor_tensor(matches[u][:, cols], key_sb[u][:, cols], st_sb[u][:, cols], MULT)
 
@@ -258,12 +262,10 @@ def tile_list_siluS_kernel(
             by_place = next_bank("by_place", 0)
             nc.tensor.transpose(by_place[:, 0:P], group_rows[:], ident[:])
             wgt_t = by_place[:, 0 : P // 2].rearrange("p (g t o) -> p t g o", g=GROUPS, o=1)
-            for cols in FIRST_PLANE_PIECES:
+            for wide, cols in zip(wgt_wide, FIRST_PLANE_PIECES):
                 tiles = slice(cols.start // P, cols.stop // P)
                 count = tiles.stop - tiles.start
-                first = tiles.start % PLACE_TILES
-                wide = wgt_wide[cols.start // HALF][:, first : first + count]
-                nc.scalar.copy(wide, wgt_t[:, tiles].to_broadcast([P, count, GROUPS, GROUP]))
+                nc.scalar.copy(wide[:], wgt_t[:, tiles].to_broadcast([P, count, GROUPS, GROUP]))
                 back = psum_v.tile([P, HALF], F32, name="ve")
                 for n in range(count):
                     nc.tensor.transpose(back[:, block(n)], wide[:, n].rearrange("p g s -> p (g s)"), ident[:])
@@ -327,7 +329,7 @@ def tile_list_siluS_kernel(
                     nc.sync.dma_start(out=out[block(r), :], in_=windows[r][:])
 
         spread_group_weights()
-        for r in range(2, ROW_TILES):
+        for r in range(1, ROW_TILES):
             windows.append(keep.tile([P, T], F32, name=f"window{r}", tag=f"window{r}"))
             nc.gpsimd.memset(windows[r][:].bitcast(I32), 0)
 
@@ -371,7 +373,6 @@ def tile_list_siluS_kernel(
         quantise((0, 1), grouped_first[1], "codes_a", "x_sc01")
         quantise((1, 2), grouped_piece[2], "codes_b", "scales_c")
         quantise((1, 3), grouped_piece[3], "codes_d", "scales_a")
-        quantise((1, 4), grouped_piece[4], "codes_e", "scales_b")
         combine(0)
         make_match(1)
         scale_by_place(1)

@@ -309,16 +309,18 @@ def tile_list_siluS_kernel(
 
         def copy_values(u):
             values[u] = keep.tile([P, HALF], F32, name=f"value{u}", tag=f"value{u}", align_bytes=64)
-            nc.scalar.copy(values[u][:, unit_cols(u)], turned[u][:, unit_cols(u)])
+            for part in (slice(0, P), slice(P, HALF)) if u == 1 else (unit_cols(u),):
+                nc.scalar.copy(values[u][:, part], turned[u][:, part])
 
         def combine(u):
             cols = unit_cols(u)
             if u == 0:
                 results[u] = keep.tile([P, HALF], F32, name="result0", tag="pair_late", align_bytes=64)
-                nc.vector.tensor_tensor(results[u][:], turned[u][:], gates[u][:], MULT)
+                for part in (slice(0, 2 * P), slice(2 * P, HALF)):
+                    nc.vector.tensor_tensor(results[u][:, part], turned[u][:, part], gates[u][:, part], MULT)
                 return
             results[u] = ring.tile([P, HALF], F32, name="result")
-            for part in (slice(0, 2 * P), slice(2 * P, HALF)) if u == 1 else (cols,):
+            for part in (slice(0, P), slice(P, HALF)) if u <= 3 else (cols,):
                 nc.gpsimd.tensor_tensor(results[u][:, part], gates[u][:, part], values[u][:, part], MULT)
 
         def scatter(u):

@@ -26,14 +26,17 @@ HALVES = J // HALF
 ROW_TILES = N // P
 GROUPS = 8
 GROUP = P // GROUPS
-PLACE_TILES = HALF // P
+PLACE_TILES = J // P
 PLACE_UNITS = 5
 UNITS = PLACE_UNITS + ROW_TILES
+SPLIT_RESULTS = 3
+RING_BANKS = 5
 SCALE_ROWS = 4
-F32_BYTES = 4
 FIRST_PLANE_PIECES = (slice(0, 2 * P), slice(2 * P, HALF), slice(HALF, J))
 PIECES = (slice(0, P), slice(P, 2 * P), slice(2 * P, HALF), slice(HALF, HALF + 2 * P), slice(HALF + 2 * P, J))
 QUANTISED = PIECES[:3] + (slice(HALF, J),)
+FIRST_HALF_PIECES = range(3)
+SECOND_HALF_PIECES = range(3, 5)
 PAIR_STEP = HALF + 2 * P
 
 
@@ -43,10 +46,9 @@ def tile_list_siluS_kernel(
     nc = tc.nc
     with ExitStack() as ctx:
         keep = ctx.enter_context(tc.tile_pool(name="keep", bufs=1))
-        pages = ctx.enter_context(tc.tile_pool(name="pages", bufs=1))
         ring = ctx.enter_context(tc.tile_pool(name="ring", bufs=3))
-        psum_k = ctx.enter_context(tc.psum_pool(name="psum_k", bufs=1))
-        psum_v = ctx.enter_context(tc.psum_pool(name="psum_v", bufs=3))
+        psum_ring = ctx.enter_context(tc.psum_pool(name="psum_ring", bufs=1))
+        psum_spread = ctx.enter_context(tc.psum_pool(name="psum_spread", bufs=len(FIRST_PLANE_PIECES)))
 
         def half_cols(h):
             return slice(h * HALF, (h + 1) * HALF)
@@ -76,7 +78,7 @@ def tile_list_siluS_kernel(
             for n, c in enumerate(FIRST_PLANE_PIECES)
         ]
         ident = keep.tile([P, P], F32, name="ident")
-        zeros = pages.tile([P, P], F32, name="zeros", offset=0)
+        zeros = keep.tile([P, P], F32, name="zeros", tag="window0")
         windows = []
         warm = keep.tile([P, 8], F32, name="warm")
 
@@ -93,8 +95,6 @@ def tile_list_siluS_kernel(
             channel_multiplier=1,
         )
         nc.vector.memset(w_sc[:].rearrange("p w a n -> p (w a n)").bitcast(I32), 0)
-        windows.append(pages.tile([P, T], F32, name="window0", offset=0))
-        nc.vector.memset(windows[0][:].bitcast(I32), 0)
 
         for tile, scales in ((wk_sc, wk_scales), (wv_sc, wv_scales)):
             rows = scales.rearrange("a (q r) n -> r q a n", r=SCALE_ROWS)
@@ -121,8 +121,10 @@ def tile_list_siluS_kernel(
 
         def unit_parts(u):
             if u < PLACE_UNITS:
-                return [(block(r), r, block(u)) for r in range(ROW_TILES)]
-            return [(slice(0, J - PLACE_UNITS * P), u - PLACE_UNITS, slice(PLACE_UNITS * P, J))]
+                rows = ROW_TILES - 1 if u == PLACE_UNITS - 1 else ROW_TILES
+                return [(block(r), r, block(u)) for r in range(rows)]
+            first = (PLACE_UNITS - 1 if u == UNITS - 1 else PLACE_UNITS) * P
+            return [(slice(0, J - first), u - PLACE_UNITS, slice(first, J))]
 
         def unit_cols(u):
             return slice(0, unit_parts(u)[-1][0].stop)
@@ -136,7 +138,7 @@ def tile_list_siluS_kernel(
                 nc.sync.dma_start(out=st_sb[u][:, span], in_=st_rows[:, first, places])
             else:
                 nc.sync.dma_start(
-                    out=st_sb[u].rearrange("p (r j) -> p r j", r=len(parts)),
+                    out=st_sb[u][:, unit_cols(u)].rearrange("p (r j) -> p r j", r=len(parts)),
                     in_=st_rows[:, first : first + len(parts), places],
                 )
 
@@ -149,9 +151,11 @@ def tile_list_siluS_kernel(
         for u in range(2, UNITS):
             load_state(u)
 
-        picked = keep.tile([P, PACK, J], F32, name="picked", tag="picked", align_bytes=64)
+        picked = keep.tile([P, PACK, J], F32, name="picked", align_bytes=64)
         pair_early = keep.tile([P, 2, J], F32, name="pair_early")
-        grouped_first = [keep.tile([P, HALF, PACK], BF16, name=f"grouped_first{h}", align_bytes=64) for h in range(HALVES)]
+        grouped_first = [
+            keep.tile([P, HALF, PACK], BF16, name=f"grouped_first{h}", align_bytes=64) for h in range(HALVES)
+        ]
         grouped_piece = [
             keep.tile([P, c.stop - c.start, PACK], BF16, name=f"grouped_piece{n}", tag=f"grouped{n}", align_bytes=64)
             for n, c in enumerate(QUANTISED)
@@ -207,15 +211,17 @@ def tile_list_siluS_kernel(
 
         taken = []
 
-        def next_bank(name, first=None):
-            if first is None:
-                first = len(taken) % 5
+        def next_bank(name, fixed=None):
+            if fixed is None:
+                fixed = len(taken) % RING_BANKS
                 taken.append(name)
-            return psum_k.tile([P, HALF], F32, name=name, tag=f"bank{first}")
+            return psum_ring.tile([P, HALF], F32, name=name, tag=f"bank{fixed}")
 
-        def make_keys(u, passes=range(PASSES)):
-            if passes[0] == 0:
-                keys[u] = next_bank("ke", {0: 1, 1: 4}.get(u))
+        first_key_banks = {0: 1, 1: 4}
+        first_sum_banks = {0: 2, 1: 3}
+
+        def make_keys(u):
+            keys[u] = next_bank("ke", first_key_banks.get(u))
             runs = []
             for span, r, places in unit_parts(u):
                 for c in PIECES:
@@ -225,17 +231,16 @@ def tile_list_siluS_kernel(
                         runs.append((slice(first, first + stop - start), r, slice(start, stop)))
             steps = [(a, run) for a in range(PASSES) for run in runs]
             for n, (a, (span, r, places)) in enumerate(steps):
-                if a in passes:
-                    rhs, rhs_scale = x_operand(a, places)
-                    nc.tensor.matmul_mx(
-                        out=keys[u][:, span],
-                        lhsT=wk_codes[a][:, block(r)].bitcast(FP8X4),
-                        lhsT_scale=wk_sc[:, a, block(r)],
-                        rhs=rhs,
-                        rhs_scale=rhs_scale,
-                        start=(n == 0),
-                        stop=(n == len(steps) - 1),
-                    )
+                rhs, rhs_scale = x_operand(a, places)
+                nc.tensor.matmul_mx(
+                    out=keys[u][:, span],
+                    lhsT=wk_codes[a][:, block(r)].bitcast(FP8X4),
+                    lhsT_scale=wk_sc[:, a, block(r)],
+                    rhs=rhs,
+                    rhs_scale=rhs_scale,
+                    start=(n == 0),
+                    stop=(n == len(steps) - 1),
+                )
 
         def copy_keys(u):
             key_sb[u] = keep.tile([P, HALF], F32, name=f"key{u}", tag="st0" if u % 2 else "key_even", align_bytes=64)
@@ -244,10 +249,10 @@ def tile_list_siluS_kernel(
         def make_match(u):
             cols = unit_cols(u)
             if u == 0:
-                matches[u] = keep.tile([P, HALF], F32, name="match0", tag="match0", align_bytes=64)
+                matches[u] = keep.tile([P, HALF], F32, name="match0", align_bytes=64)
                 nc.vector.tensor_tensor(matches[u][:], keys[u][:], st_sb[u], MULT)
                 return
-            tag = {1: "grouped3", 2: "gate0"}.get(u, f"value{u - 2}")
+            tag = {1: f"grouped{len(QUANTISED) - 1}", 2: "gate0"}.get(u, f"value{u - 2}")
             matches[u] = keep.tile([P, HALF], F32, name=f"match{u}", tag=tag, align_bytes=64)
             nc.gpsimd.tensor_tensor(matches[u][:, cols], key_sb[u][:, cols], st_sb[u][:, cols], MULT)
 
@@ -265,18 +270,17 @@ def tile_list_siluS_kernel(
             for wide, cols in zip(wgt_wide, FIRST_PLANE_PIECES):
                 tiles = slice(cols.start // P, cols.stop // P)
                 count = tiles.stop - tiles.start
-                nc.scalar.copy(wide[:], wgt_t[:, tiles].to_broadcast([P, count, GROUPS, GROUP]))
-                back = psum_v.tile([P, HALF], F32, name="ve")
+                nc.vector.tensor_copy(wide[:], wgt_t[:, tiles].to_broadcast([P, count, GROUPS, GROUP]))
+                back = psum_spread.tile([P, HALF], F32, name="back")
                 for n in range(count):
                     nc.tensor.transpose(back[:, block(n)], wide[:, n].rearrange("p g s -> p (g s)"), ident[:])
                 nc.scalar.copy(wgt_sb[:, cols], back[:, 0 : count * P])
-            nc.scalar.copy(wgo_head, by_place[:, P // 2 : P // 2 + 2 * GROUPS : GROUPS])
+            nc.scalar.copy(wgo_head, by_place[:, P // 2 : P // 2 + 2 * PLACE_TILES : PLACE_TILES])
             nc.scalar.copy(wgo_t[:], by_place[:, P // 2 : P])
 
-        def sums_by_place(t, passes=range(PASSES)):
-            if passes[0] == 0:
-                sums[t] = next_bank("ve", {0: 2, 1: 3}.get(t))
-            for a in passes:
+        def sums_by_place(t):
+            sums[t] = next_bank("ve", first_sum_banks.get(t))
+            for a in range(PASSES):
                 lhsT, lhsT_scale = x_operand(a, block(t))
                 nc.tensor.matmul_mx(
                     out=sums[t][:],
@@ -288,39 +292,41 @@ def tile_list_siluS_kernel(
                     stop=(a == PASSES - 1),
                 )
 
-        spent = ["plane0", "plane1", "st1", "st2", "st3", "gate2", "st4", "gate3"]
+        scaled_slots = ["plane0", "plane1", "st1", "st2", "st3", "gate2", "st4", "gate3"]
 
         def scale_by_place(t):
             if t not in sums:
                 sums_by_place(t)
-            scaled[t] = keep.tile([P, N], F32, name=f"scaled{t}", tag=spent[t], align_bytes=64)
+            scaled[t] = keep.tile([P, N], F32, name=f"scaled{t}", tag=scaled_slots[t], align_bytes=64)
             src = sums[t][:].rearrange("p (r g c) -> p r g c", g=GROUPS, c=GROUP)
             dst = scaled[t][:].rearrange("p (r g c) -> p r g c", g=GROUPS, c=GROUP)
             for g in range(GROUPS):
-                col = g * (J // P) + t
-                nc.scalar.activation(dst[:, :, g, :], src[:, :, g, :], COPY, scale=wgo_head[:, g : g + 1] if t == 0 and g < 2 else wgo_t[:, col : col + 1])
+                col = g * PLACE_TILES + t
+                scale = wgo_head[:, g : g + 1] if t == 0 and g < 2 else wgo_t[:, col : col + 1]
+                nc.scalar.activation(dst[:, :, g, :], src[:, :, g, :], COPY, scale=scale)
 
         def turn_values(u):
-            turned[u] = next_bank("turned", {0: 1, 1: 4}.get(u))
+            turned[u] = next_bank("turned", first_key_banks.get(u))
             for span, r, places in unit_parts(u):
                 for n in range((places.stop - places.start) // P):
                     src = scaled[places.start // P + n][:, block(r)]
                     nc.tensor.transpose(turned[u][:, block(span.start // P + n)], src, ident[:])
 
+        first_block_apart = (slice(0, P), slice(P, HALF))
+
         def copy_values(u):
             values[u] = keep.tile([P, HALF], F32, name=f"value{u}", tag=f"value{u}", align_bytes=64)
-            for part in (slice(0, P), slice(P, HALF)) if u == 1 else (unit_cols(u),):
+            for part in first_block_apart if u == 1 else (unit_cols(u),):
                 nc.scalar.copy(values[u][:, part], turned[u][:, part])
 
         def combine(u):
-            cols = unit_cols(u)
             if u == 0:
                 results[u] = keep.tile([P, HALF], F32, name="result0", tag="pair_late", align_bytes=64)
                 for part in (slice(0, 2 * P), slice(2 * P, HALF)):
                     nc.vector.tensor_tensor(results[u][:, part], turned[u][:, part], gates[u][:, part], MULT)
                 return
             results[u] = ring.tile([P, HALF], F32, name="result")
-            for part in (slice(0, P), slice(P, HALF)) if u <= 3 else (cols,):
+            for part in first_block_apart if u <= SPLIT_RESULTS else (unit_cols(u),):
                 nc.gpsimd.tensor_tensor(results[u][:, part], gates[u][:, part], values[u][:, part], MULT)
 
         def scatter(u):
@@ -331,7 +337,7 @@ def tile_list_siluS_kernel(
                     nc.sync.dma_start(out=out[block(r), :], in_=windows[r][:])
 
         spread_group_weights()
-        for r in range(1, ROW_TILES):
+        for r in range(ROW_TILES):
             windows.append(keep.tile([P, T], F32, name=f"window{r}", tag=f"window{r}"))
             nc.gpsimd.memset(windows[r][:].bitcast(I32), 0)
 
@@ -344,20 +350,19 @@ def tile_list_siluS_kernel(
             interleave(grouped_first[h][:], picked[:, :, half_cols(h)])
 
         gather(4)
-        gather(5, half_cols(0))
-        for n in range(3):
-            interleave_pair(0, n)
-        gather(5, half_cols(1))
-        for n in range(3, 5):
-            interleave_pair(0, n)
-        quantise((0, 0), grouped_first[0], "plane5", "x_sc00")
+        for h, pieces in enumerate((FIRST_HALF_PIECES, SECOND_HALF_PIECES)):
+            gather(5, half_cols(h))
+            for n in pieces:
+                interleave_pair(0, n)
+        quantise((0, 0), grouped_first[0], "plane5", "scales_00")
+
         gather(6, half_cols(0))
         gather(7, slice(0, 2 * P))
         interleave_pair(1, 0)
         interleave_pair(1, 1)
         gather(7, PIECES[2])
-        quantise((1, 0), grouped_piece[0], "codes_a", "scales_a")
-        quantise((1, 1), grouped_piece[1], "codes_b", "scales_b")
+        quantise((1, 0), grouped_piece[0], "codes_10", "scales_10")
+        quantise((1, 1), grouped_piece[1], "codes_11", "scales_11")
         gather(6, half_cols(1))
         interleave_pair(1, 2)
         sums_by_place(0)
@@ -365,16 +370,16 @@ def tile_list_siluS_kernel(
         scale_by_place(0)
         make_keys(1)
         sums_by_place(1)
-        for n in range(3, 5):
+        for n in SECOND_HALF_PIECES:
             gather(7, PIECES[n])
             interleave_pair(1, n)
         make_match(0)
         make_gate(0)
         turn_values(0)
         copy_keys(1)
-        quantise((0, 1), grouped_first[1], "codes_a", "x_sc01")
-        quantise((1, 2), grouped_piece[2], "codes_b", "scales_c")
-        quantise((1, 3), grouped_piece[3], "codes_d", "scales_a")
+        quantise((0, 1), grouped_first[1], "codes_10", "scales_01")
+        quantise((1, 2), grouped_piece[2], "codes_11", "scales_12")
+        quantise((1, 3), grouped_piece[3], "codes_13", "scales_10")
         combine(0)
         make_match(1)
         scale_by_place(1)

@@ -37,7 +37,8 @@ PIECES = (slice(0, P), slice(P, 2 * P), slice(2 * P, HALF), slice(HALF, HALF + 2
 QUANTISED = PIECES[:3] + (slice(HALF, J),)
 FIRST_HALF_PIECES = range(3)
 SECOND_HALF_PIECES = range(3, 5)
-PAIR_STEP = HALF + 2 * P
+LATE_STEPS = (J, J + P)
+PLANE_ORDER = (0, 1, 4, 2, 3, 5, 6, 7)
 
 
 def tile_list_siluS_kernel(
@@ -62,15 +63,14 @@ def tile_list_siluS_kernel(
         planes = [keep.tile([P, T], F32, name=f"plane{q}", tag=f"plane{q}", align_bytes=64) for q in range(PLANES)]
         wk_codes = [keep.tile([P, N], U32, name=f"wk_codes{a}", align_bytes=64) for a in range(PASSES)]
         wv_codes = [keep.tile([P, 2 * N], U8, name=f"wv_codes{a}", align_bytes=64) for a in range(PASSES)]
-        w_sc = keep.tile([P, 2, PASSES, N], U8, name="w_sc", align_bytes=64)
-        wk_sc = w_sc[:, 0]
-        wv_sc = w_sc[:, 1]
-        pair_late = keep.tile([P, HALF + 2 * PAIR_STEP], F32, name="pair_late", tag="pair_late", align_bytes=64)
+        wk_sc = keep.tile([P, PASSES, N], U8, name="wk_sc", align_bytes=64)
+        wv_sc = keep.tile([P, PASSES, N], U8, name="wv_sc", align_bytes=64)
+        late = keep.tile([P, HALF + 3 * LATE_STEPS[1]], F32, name="late", tag="pair_late", align_bytes=64)
         late_half = [
-            pair_late[:, h * HALF : h * HALF + 2 * PAIR_STEP].rearrange("p (i c) -> p i c", i=2) for h in range(HALVES)
+            late[:, h * HALF : h * HALF + 3 * LATE_STEPS[h]].rearrange("p (i c) -> p i c", i=3) for h in range(HALVES)
         ]
         st_sb = [keep.tile([P, HALF], F32, name=f"st{u}", tag=f"st{u}", align_bytes=64)[:] for u in range(UNITS)]
-        wgo_head = late_half[1][:, 1, 2 * P - 1 : 2 * P + 1]
+        wgo_head = late_half[1][:, 2, 2 * P - 1 : 2 * P + 1]
         group_rows = keep.tile([P, P], F32, name="group_rows")
         wgo_t = keep.tile([P, P // 2], F32, name="wgo_t")
         wgt_wide = [
@@ -94,9 +94,10 @@ def tile_list_siluS_kernel(
             pattern=[[-1, P]],
             channel_multiplier=1,
         )
-        nc.vector.memset(w_sc[:].rearrange("p w a n -> p (w a n)").bitcast(I32), 0)
+        for tile in (wv_sc, wk_sc):
+            nc.vector.memset(tile[:].rearrange("p a n -> p (a n)").bitcast(I32), 0)
 
-        for tile, scales in ((wk_sc, wk_scales), (wv_sc, wv_scales)):
+        for tile, scales in ((wv_sc, wv_scales), (wk_sc, wk_scales)):
             rows = scales.rearrange("a (q r) n -> r q a n", r=SCALE_ROWS)
             for r in range(SCALE_ROWS):
                 nc.gpsimd.dma_start(out=tile[r:P:32, :, :].bitcast(I32), in_=rows[r].bitcast(I32))
@@ -107,7 +108,7 @@ def tile_list_siluS_kernel(
                 in_=weights.rearrange("(g s) (t c) -> s g t c", s=GROUP, c=P)[0],
             )
         x_rows = xT.rearrange("(a p i) t -> p a i t", a=PASSES, i=PACK)
-        for q in range(PLANES):
+        for q in PLANE_ORDER:
             nc.sync.dma_start(out=planes[q][:], in_=x_rows[:, q // PACK, q % PACK, :])
             if q == 0:
                 nc.sync.dma_start(pick[:], offs)
@@ -142,17 +143,18 @@ def tile_list_siluS_kernel(
                     in_=st_rows[:, first : first + len(parts), places],
                 )
 
-        load_state(0)
         for a in range(PASSES):
             load_values_weight(a)
-            load_keys_weight(a)
+        load_keys_weight(0)
+        load_state(0)
+        load_keys_weight(1)
         load_state(1)
         nc.sync.dma_start(place[:], offs2)
         for u in range(2, UNITS):
             load_state(u)
 
         picked = keep.tile([P, PACK, J], F32, name="picked", align_bytes=64)
-        pair_early = keep.tile([P, 2, J], F32, name="pair_early")
+        single = keep.tile([P, 1, J], F32, name="single")
         grouped_first = [
             keep.tile([P, HALF, PACK], BF16, name=f"grouped_first{h}", align_bytes=64) for h in range(HALVES)
         ]
@@ -165,25 +167,27 @@ def tile_list_siluS_kernel(
 
         def pair_view(n, cols):
             if n == 0:
-                return pair_early[:, :, cols]
+                return single[:, :, cols]
             h = cols.start // HALF
             return late_half[h][:, :, cols.start - h * HALF : cols.stop - h * HALF]
 
         def gather(q, cols=slice(0, J)):
             a, i = divmod(q, PACK)
-            dst = picked[:, i, cols] if a == 0 else pair_view(i // 2, cols)[:, i % 2, :]
+            if a == 0:
+                dst = picked[:, i, cols]
+            elif i < 2:
+                dst = single[:, 0, cols] if i == 0 else late[:, cols]
+            else:
+                dst = pair_view(1, cols)[:, i - 1, :]
             entries = pick[:, cols.start // GROUP : cols.stop // GROUP]
             nc.vector.tensor_tensor(dst, planes[q][:].indirect(entries), wgt_sb[:, cols], MULT)
-
-        def interleave(dst, src):
-            nc.scalar.copy(dst.rearrange("p (c u) i -> p c i u", u=4), src.rearrange("p i (c u) -> p c i u", u=4))
 
         def interleave_pair(n, piece):
             src = pair_view(n, PIECES[piece]).rearrange("p i c -> p c i")
             cols = PIECES[piece]
             whole = min(piece, len(QUANTISED) - 1)
             first = QUANTISED[whole].start
-            nc.scalar.copy(grouped_piece[whole][:, cols.start - first : cols.stop - first, 2 * n : 2 * n + 2], src)
+            nc.scalar.copy(grouped_piece[whole][:, cols.start - first : cols.stop - first, (slice(0, 1), slice(1, PACK))[n]], src)
 
         def quantise(key, src, codes_tag, scales_tag):
             width = src.shape[1]
@@ -343,18 +347,18 @@ def tile_list_siluS_kernel(
 
         for cols in FIRST_PLANE_PIECES:
             gather(0, cols)
-        for q in range(1, PACK - 1):
+        for q in PLANE_ORDER[1:5]:
             gather(q)
-        for h in range(HALVES):
-            gather(PACK - 1, half_cols(h))
-            interleave(grouped_first[h][:], picked[:, :, half_cols(h)])
+            if q == 4:
+                for n in range(len(PIECES)):
+                    interleave_pair(0, n)
+            if q % 2:
+                for h in range(HALVES):
+                    src = picked[:, q - 1 : q + 1, half_cols(h)].rearrange("p i c -> p c i")
+                    nc.scalar.copy(grouped_first[h][:, :, q - 1 : q + 1], src)
 
-        gather(4)
-        for h, pieces in enumerate((FIRST_HALF_PIECES, SECOND_HALF_PIECES)):
-            gather(5, half_cols(h))
-            for n in pieces:
-                interleave_pair(0, n)
-        quantise((0, 0), grouped_first[0], "plane5", "scales_00")
+        gather(5)
+        quantise((0, 0), grouped_first[0], "codes_00", "scales_00")
 
         gather(6, half_cols(0))
         gather(7, slice(0, 2 * P))
@@ -362,8 +366,8 @@ def tile_list_siluS_kernel(
         interleave_pair(1, 1)
         gather(7, PIECES[2])
         quantise((1, 0), grouped_piece[0], "codes_10", "scales_10")
-        quantise((1, 1), grouped_piece[1], "codes_11", "scales_11")
         gather(6, half_cols(1))
+        quantise((1, 1), grouped_piece[1], "codes_11", "scales_11")
         interleave_pair(1, 2)
         sums_by_place(0)
         make_keys(0)

@@ -62,8 +62,8 @@ def tile_list_siluS_kernel(
         wgt_sb = keep.tile([P, J], F32, name="wgt_sb")
         planes = [keep.tile([P, T], F32, name=f"plane{q}", tag=f"plane{q}", align_bytes=64) for q in range(PLANES)]
         wk_codes = [keep.tile([P, N], U32, name=f"wk_codes{a}", align_bytes=64) for a in range(PASSES)]
-        wv_codes = [keep.tile([P, 2 * N], U8, name=f"wv_codes{a}", align_bytes=64) for a in range(PASSES)]
-        wk_sc = keep.tile([P, PASSES, N], U8, name="wk_sc", align_bytes=64)
+        wv_codes = keep.tile([P, PASSES, 2 * N], U8, name="wv_codes", align_bytes=64)
+        wk_sc = keep.tile([P, N], U8, name="wk_sc", align_bytes=64)
         wv_sc = keep.tile([P, PASSES, N], U8, name="wv_sc", align_bytes=64)
         late = keep.tile([P, HALF + 3 * LATE_STEPS[1]], F32, name="late", tag="pair_late", align_bytes=64)
         late_half = [
@@ -71,7 +71,7 @@ def tile_list_siluS_kernel(
         ]
         st_sb = [keep.tile([P, HALF], F32, name=f"st{u}", tag=f"st{u}", align_bytes=64)[:] for u in range(UNITS)]
         wgo_head = late_half[1][:, 2, 2 * P - 1 : 2 * P + 1]
-        group_rows = keep.tile([P, P], F32, name="group_rows")
+        group_rows = [keep.tile([P, P], F32, name=f"group_rows{n}") for n in range(2)]
         wgo_t = keep.tile([P, P // 2], F32, name="wgo_t")
         wgt_wide = [
             keep.tile([P, (c.stop - c.start) // P, GROUPS, GROUP], F32, name=f"wgt_wide{n}", tag=f"window{1 + n}")
@@ -83,6 +83,8 @@ def tile_list_siluS_kernel(
         warm = keep.tile([P, 8], F32, name="warm")
 
         nc.vector.memset(zeros[:], 0.0)
+        for rows in group_rows:
+            nc.vector.memset(rows[P // 2 : P, :], 0.0)
         nc.vector.memset(warm[:], 0.0)
         nc.scalar.activation(warm[:, 1:2], warm[:, 0:1], SILU)
         nc.gpsimd.affine_select(
@@ -94,31 +96,27 @@ def tile_list_siluS_kernel(
             pattern=[[-1, P]],
             channel_multiplier=1,
         )
-        for tile in (wv_sc, wk_sc):
-            nc.vector.memset(tile[:].rearrange("p a n -> p (a n)").bitcast(I32), 0)
+        nc.vector.memset(wk_sc[:].bitcast(I32), 0)
+        nc.vector.memset(wv_sc[:].rearrange("p a n -> p (a n)").bitcast(I32), 0)
 
-        for tile, scales in ((wv_sc, wv_scales), (wk_sc, wk_scales)):
-            rows = scales.rearrange("a (q r) n -> r q a n", r=SCALE_ROWS)
-            for r in range(SCALE_ROWS):
-                nc.gpsimd.dma_start(out=tile[r:P:32, :, :].bitcast(I32), in_=rows[r].bitcast(I32))
+        for q in range(P // 32):
+            rows = wk_scales[:, q * SCALE_ROWS : (q + 1) * SCALE_ROWS, :]
+            first = 32 * q + SCALE_ROWS
+            nc.gpsimd.dma_start(out=wk_sc[first : first + PASSES * SCALE_ROWS, :].bitcast(I32), in_=rows.bitcast(I32))
 
-        for n, weights in enumerate((wgt, wgo)):
-            nc.sync.dma_start(
-                out=group_rows[n * P // 2 : (n + 1) * P // 2, :],
-                in_=weights.rearrange("(g s) (t c) -> s g t c", s=GROUP, c=P)[0],
-            )
+        def load_group_rows(n, weights):
+            rows = weights.rearrange("(g s) (t c) -> s g t c", s=GROUP, c=P)[0]
+            nc.sync.dma_start(out=group_rows[n][0 : P // 2, :], in_=rows)
+
+        load_group_rows(0, wgt)
         x_rows = xT.rearrange("(a p i) t -> p a i t", a=PASSES, i=PACK)
         for q in PLANE_ORDER:
             nc.sync.dma_start(out=planes[q][:], in_=x_rows[:, q // PACK, q % PACK, :])
             if q == 0:
                 nc.sync.dma_start(pick[:], offs)
+            if q == 1:
+                load_group_rows(1, wgo)
 
-        def load_values_weight(a):
-            nc.sync.dma_start(out=wv_codes[a][:].bitcast(I32), in_=wv_words[a].bitcast(I32))
-
-        def load_keys_weight(a):
-            words = wk_words[a].rearrange("p n i -> p (n i)")
-            nc.sync.dma_start(out=wk_codes[a][:].bitcast(I32), in_=words.bitcast(I32))
 
         def unit_parts(u):
             if u < PLACE_UNITS:
@@ -143,11 +141,14 @@ def tile_list_siluS_kernel(
                     in_=st_rows[:, first : first + len(parts), places],
                 )
 
+        rows = wv_scales.rearrange("a (q r) n -> r q a n", r=SCALE_ROWS)
+        for r in range(SCALE_ROWS):
+            nc.sync.dma_start(out=wv_sc[r:P:32, :, :].bitcast(I32), in_=rows[r].bitcast(I32))
+        nc.sync.dma_start(out=wv_codes[:].bitcast(I32), in_=wv_words.rearrange("a p n -> p a n").bitcast(I32))
         for a in range(PASSES):
-            load_values_weight(a)
-        load_keys_weight(0)
+            words = wk_words[a].rearrange("p n i -> p (n i)")
+            nc.sync.dma_start(out=wk_codes[a][:].bitcast(I32), in_=words.bitcast(I32))
         load_state(0)
-        load_keys_weight(1)
         load_state(1)
         nc.sync.dma_start(place[:], offs2)
         for u in range(2, UNITS):
@@ -239,7 +240,7 @@ def tile_list_siluS_kernel(
                 nc.tensor.matmul_mx(
                     out=keys[u][:, span],
                     lhsT=wk_codes[a][:, block(r)].bitcast(FP8X4),
-                    lhsT_scale=wk_sc[:, a, block(r)],
+                    lhsT_scale=wk_sc[SCALE_ROWS * (a + 1) : P, block(r)],
                     rhs=rhs,
                     rhs_scale=rhs_scale,
                     start=(n == 0),
@@ -269,7 +270,7 @@ def tile_list_siluS_kernel(
 
         def spread_group_weights():
             by_place = next_bank("by_place", 0)
-            nc.tensor.transpose(by_place[:, 0:P], group_rows[:], ident[:])
+            nc.tensor.transpose(by_place[:, 0:P], group_rows[0][:], ident[:])
             wgt_t = by_place[:, 0 : P // 2].rearrange("p (g t o) -> p t g o", g=GROUPS, o=1)
             for wide, cols in zip(wgt_wide, FIRST_PLANE_PIECES):
                 tiles = slice(cols.start // P, cols.stop // P)
@@ -279,8 +280,10 @@ def tile_list_siluS_kernel(
                 for n in range(count):
                     nc.tensor.transpose(back[:, block(n)], wide[:, n].rearrange("p g s -> p (g s)"), ident[:])
                 nc.scalar.copy(wgt_sb[:, cols], back[:, 0 : count * P])
-            nc.scalar.copy(wgo_head, by_place[:, P // 2 : P // 2 + 2 * PLACE_TILES : PLACE_TILES])
-            nc.scalar.copy(wgo_t[:], by_place[:, P // 2 : P])
+            wgo_by_place = next_bank("wgo_by_place", 0)
+            nc.tensor.transpose(wgo_by_place[:, 0:P], group_rows[1][:], ident[:])
+            nc.scalar.copy(wgo_head, wgo_by_place[:, 0 : 2 * PLACE_TILES : PLACE_TILES])
+            nc.scalar.copy(wgo_t[:], wgo_by_place[:, 0 : P // 2])
 
         def sums_by_place(t):
             sums[t] = next_bank("ve", first_sum_banks.get(t))
@@ -290,7 +293,7 @@ def tile_list_siluS_kernel(
                     out=sums[t][:],
                     lhsT=lhsT,
                     lhsT_scale=lhsT_scale,
-                    rhs=wv_codes[a][:].bitcast(FP4X4),
+                    rhs=wv_codes[:, a, :].bitcast(FP4X4),
                     rhs_scale=wv_sc[:, a, :],
                     start=(a == 0),
                     stop=(a == PASSES - 1),

@@ -114,8 +114,6 @@ def tile_list_siluS_kernel(
             nc.sync.dma_start(out=planes[q][:], in_=x_rows[:, q // PACK, q % PACK, :])
             if q == 0:
                 nc.sync.dma_start(pick[:], offs)
-            if q == 1:
-                load_group_rows(1, wgo)
 
 
         def unit_parts(u):
@@ -141,6 +139,7 @@ def tile_list_siluS_kernel(
                     in_=st_rows[:, first : first + len(parts), places],
                 )
 
+        load_group_rows(1, wgo)
         rows = wv_scales.rearrange("a (q r) n -> r q a n", r=SCALE_ROWS)
         for r in range(SCALE_ROWS):
             nc.sync.dma_start(out=wv_sc[r:P:32, :, :].bitcast(I32), in_=rows[r].bitcast(I32))
@@ -223,7 +222,7 @@ def tile_list_siluS_kernel(
             return psum_ring.tile([P, HALF], F32, name=name, tag=f"bank{fixed}")
 
         first_key_banks = {0: 1, 1: 4}
-        first_sum_banks = {0: 2, 1: 3}
+        first_sum_banks = {0: 2, 1: 2}
 
         def make_keys(u):
             keys[u] = next_bank("ke", first_key_banks.get(u))

@@ -54,6 +54,9 @@ def tile_list_siluS_kernel(
         def half_cols(h):
             return slice(h * HALF, (h + 1) * HALF)
 
+        def tile_col(t):
+            return (t + PLACE_TILES // 2) % PLACE_TILES
+
         def block(i):
             return slice(i * P, (i + 1) * P)
 
@@ -70,7 +73,6 @@ def tile_list_siluS_kernel(
             late[:, h * HALF : h * HALF + 3 * LATE_STEPS[h]].rearrange("p (i c) -> p i c", i=3) for h in range(HALVES)
         ]
         st_sb = [keep.tile([P, HALF], F32, name=f"st{u}", tag=f"st{u}", align_bytes=64)[:] for u in range(UNITS)]
-        wgo_head = late_half[1][:, 2, 2 * P - 1 : 2 * P + 1]
         group_rows = [keep.tile([P, P], F32, name=f"group_rows{n}") for n in range(2)]
         wgo_t = keep.tile([P, P // 2], F32, name="wgo_t")
         wgt_wide = [
@@ -105,7 +107,9 @@ def tile_list_siluS_kernel(
             nc.gpsimd.dma_start(out=wk_sc[first : first + PASSES * SCALE_ROWS, :].bitcast(I32), in_=rows.bitcast(I32))
 
         def load_group_rows(n, weights):
-            rows = weights.rearrange("(g s) (t c) -> s g t c", s=GROUP, c=P)[0]
+            step = GROUP // 2 * J - HALF
+            runs = weights.rearrange("p j -> (p j)")[step : step * (2 * GROUPS + 1)].rearrange("(h x) -> h x", x=step)
+            rows = runs[:, 0:HALF].rearrange("h (t c) -> h t c", c=P)
             nc.sync.dma_start(out=group_rows[n][0 : P // 2, :], in_=rows)
 
         load_group_rows(0, wgt)
@@ -114,6 +118,8 @@ def tile_list_siluS_kernel(
             nc.sync.dma_start(out=planes[q][:], in_=x_rows[:, q // PACK, q % PACK, :])
             if q == 0:
                 nc.sync.dma_start(pick[:], offs)
+            if q == 1:
+                load_group_rows(1, wgo)
 
 
         def unit_parts(u):
@@ -139,12 +145,11 @@ def tile_list_siluS_kernel(
                     in_=st_rows[:, first : first + len(parts), places],
                 )
 
-        load_group_rows(1, wgo)
         rows = wv_scales.rearrange("a (q r) n -> r q a n", r=SCALE_ROWS)
         for r in range(SCALE_ROWS):
             nc.sync.dma_start(out=wv_sc[r:P:32, :, :].bitcast(I32), in_=rows[r].bitcast(I32))
         nc.sync.dma_start(out=wv_codes[:].bitcast(I32), in_=wv_words.rearrange("a p n -> p a n").bitcast(I32))
-        for a in range(PASSES):
+        for a in reversed(range(PASSES)):
             words = wk_words[a].rearrange("p n i -> p (n i)")
             nc.sync.dma_start(out=wk_codes[a][:].bitcast(I32), in_=words.bitcast(I32))
         load_state(0)
@@ -158,10 +163,18 @@ def tile_list_siluS_kernel(
         grouped_first = [
             keep.tile([P, HALF, PACK], BF16, name=f"grouped_first{h}", align_bytes=64) for h in range(HALVES)
         ]
+        last_gathers = HALF + 2 * LATE_STEPS[1]
         grouped_piece = [
+            late[:, last_gathers + 2 * n * P : last_gathers + 2 * (n + 1) * P]
+            .bitcast(BF16)
+            .rearrange("p (c i) -> p c i", i=PACK)
+            for n in range(2)
+        ] + [
             keep.tile([P, c.stop - c.start, PACK], BF16, name=f"grouped_piece{n}", tag=f"grouped{n}", align_bytes=64)
-            for n, c in enumerate(QUANTISED)
+            for n, c in list(enumerate(QUANTISED))[2:]
         ]
+        last_words = grouped_piece[-1][:].rearrange("p c i -> p (c i)").bitcast(F32).rearrange("p (c w) -> p c w", w=2)
+        wgo_head = last_words[:, 2 * P - 1 : 2 * P + 1, 1]
         x_codes = {}
         x_sc = {}
 
@@ -272,7 +285,7 @@ def tile_list_siluS_kernel(
             nc.tensor.transpose(by_place[:, 0:P], group_rows[0][:], ident[:])
             wgt_t = by_place[:, 0 : P // 2].rearrange("p (g t o) -> p t g o", g=GROUPS, o=1)
             for wide, cols in zip(wgt_wide, FIRST_PLANE_PIECES):
-                tiles = slice(cols.start // P, cols.stop // P)
+                tiles = slice(tile_col(cols.start // P), tile_col(cols.stop // P - 1) + 1)
                 count = tiles.stop - tiles.start
                 nc.vector.tensor_copy(wide[:], wgt_t[:, tiles].to_broadcast([P, count, GROUPS, GROUP]))
                 back = psum_spread.tile([P, HALF], F32, name="back")
@@ -281,7 +294,7 @@ def tile_list_siluS_kernel(
                 nc.scalar.copy(wgt_sb[:, cols], back[:, 0 : count * P])
             wgo_by_place = next_bank("wgo_by_place", 0)
             nc.tensor.transpose(wgo_by_place[:, 0:P], group_rows[1][:], ident[:])
-            nc.scalar.copy(wgo_head, wgo_by_place[:, 0 : 2 * PLACE_TILES : PLACE_TILES])
+            nc.scalar.copy(wgo_head, wgo_by_place[:, tile_col(0) : 2 * PLACE_TILES : PLACE_TILES])
             nc.scalar.copy(wgo_t[:], wgo_by_place[:, 0 : P // 2])
 
         def sums_by_place(t):
@@ -307,7 +320,7 @@ def tile_list_siluS_kernel(
             src = sums[t][:].rearrange("p (r g c) -> p r g c", g=GROUPS, c=GROUP)
             dst = scaled[t][:].rearrange("p (r g c) -> p r g c", g=GROUPS, c=GROUP)
             for g in range(GROUPS):
-                col = g * PLACE_TILES + t
+                col = g * PLACE_TILES + tile_col(t)
                 scale = wgo_head[:, g : g + 1] if t == 0 and g < 2 else wgo_t[:, col : col + 1]
                 nc.scalar.activation(dst[:, :, g, :], src[:, :, g, :], COPY, scale=scale)
 
@@ -379,12 +392,12 @@ def tile_list_siluS_kernel(
         for n in SECOND_HALF_PIECES:
             gather(7, PIECES[n])
             interleave_pair(1, n)
+        quantise((1, 2), grouped_piece[2], "codes_12", "scales_12")
         make_match(0)
         make_gate(0)
         turn_values(0)
         copy_keys(1)
         quantise((0, 1), grouped_first[1], "codes_10", "scales_01")
-        quantise((1, 2), grouped_piece[2], "codes_11", "scales_12")
         quantise((1, 3), grouped_piece[3], "codes_13", "scales_10")
         combine(0)
         make_match(1)

@@ -31,14 +31,17 @@ PLACE_UNITS = 5
 UNITS = PLACE_UNITS + ROW_TILES
 SPLIT_RESULTS = 3
 RING_BANKS = 5
+QUADRANT = 32
 SCALE_ROWS = 4
 FIRST_PLANE_PIECES = (slice(0, 2 * P), slice(2 * P, HALF), slice(HALF, J))
 PIECES = (slice(0, P), slice(P, 2 * P), slice(2 * P, HALF), slice(HALF, HALF + 2 * P), slice(HALF + 2 * P, J))
 QUANTISED = PIECES[:3] + (slice(HALF, J),)
-FIRST_HALF_PIECES = range(3)
 SECOND_HALF_PIECES = range(3, 5)
-LATE_STEPS = (J, J + P)
 PLANE_ORDER = (0, 1, 4, 2, 3, 5, 6, 7)
+EARLY_WORD_PART = slice(0, 1)
+LATE_WORD_PART = slice(1, PACK)
+LATE_PLANES = PACK - 1
+LATE_STEPS = (J, J + P)
 
 
 def tile_list_siluS_kernel(
@@ -68,12 +71,13 @@ def tile_list_siluS_kernel(
         wv_codes = keep.tile([P, PASSES, 2 * N], U8, name="wv_codes", align_bytes=64)
         wk_sc = keep.tile([P, N], U8, name="wk_sc", align_bytes=64)
         wv_sc = keep.tile([P, PASSES, N], U8, name="wv_sc", align_bytes=64)
-        late = keep.tile([P, HALF + 3 * LATE_STEPS[1]], F32, name="late", tag="pair_late", align_bytes=64)
+        late = keep.tile([P, HALF + LATE_PLANES * LATE_STEPS[1]], F32, name="late", tag="late", align_bytes=64)
         late_half = [
-            late[:, h * HALF : h * HALF + 3 * LATE_STEPS[h]].rearrange("p (i c) -> p i c", i=3) for h in range(HALVES)
+            late[:, h * HALF : h * HALF + LATE_PLANES * LATE_STEPS[h]].rearrange("p (i c) -> p i c", i=LATE_PLANES)
+            for h in range(HALVES)
         ]
         st_sb = [keep.tile([P, HALF], F32, name=f"st{u}", tag=f"st{u}", align_bytes=64)[:] for u in range(UNITS)]
-        group_rows = [keep.tile([P, P], F32, name=f"group_rows{n}") for n in range(2)]
+        group_rows = [keep.tile([P, P], F32, name=f"group_rows_{w}") for w in ("wgt", "wgo")]
         wgo_t = keep.tile([P, P // 2], F32, name="wgo_t")
         wgt_wide = [
             keep.tile([P, (c.stop - c.start) // P, GROUPS, GROUP], F32, name=f"wgt_wide{n}", tag=f"window{1 + n}")
@@ -85,8 +89,8 @@ def tile_list_siluS_kernel(
         warm = keep.tile([P, 8], F32, name="warm")
 
         nc.vector.memset(zeros[:], 0.0)
-        for rows in group_rows:
-            nc.vector.memset(rows[P // 2 : P, :], 0.0)
+        for n, tile in enumerate(group_rows):
+            nc.vector.memset(tile[(1 - n) * P // 2 : (2 - n) * P // 2, :], 0.0)
         nc.vector.memset(warm[:], 0.0)
         nc.scalar.activation(warm[:, 1:2], warm[:, 0:1], SILU)
         nc.gpsimd.affine_select(
@@ -101,16 +105,16 @@ def tile_list_siluS_kernel(
         nc.vector.memset(wk_sc[:].bitcast(I32), 0)
         nc.vector.memset(wv_sc[:].rearrange("p a n -> p (a n)").bitcast(I32), 0)
 
-        for q in range(P // 32):
-            rows = wk_scales[:, q * SCALE_ROWS : (q + 1) * SCALE_ROWS, :]
-            first = 32 * q + SCALE_ROWS
+        for quad in range(P // QUADRANT):
+            rows = wk_scales[:, quad * SCALE_ROWS : (quad + 1) * SCALE_ROWS, :]
+            first = QUADRANT * quad + SCALE_ROWS
             nc.gpsimd.dma_start(out=wk_sc[first : first + PASSES * SCALE_ROWS, :].bitcast(I32), in_=rows.bitcast(I32))
 
         def load_group_rows(n, weights):
             step = GROUP // 2 * J - HALF
             runs = weights.rearrange("p j -> (p j)")[step : step * (2 * GROUPS + 1)].rearrange("(h x) -> h x", x=step)
             rows = runs[:, 0:HALF].rearrange("h (t c) -> h t c", c=P)
-            nc.sync.dma_start(out=group_rows[n][0 : P // 2, :], in_=rows)
+            nc.sync.dma_start(out=group_rows[n][n * P // 2 : (n + 1) * P // 2, :], in_=rows)
 
         load_group_rows(0, wgt)
         x_rows = xT.rearrange("(a p i) t -> p a i t", a=PASSES, i=PACK)
@@ -120,7 +124,6 @@ def tile_list_siluS_kernel(
                 nc.sync.dma_start(pick[:], offs)
             if q == 1:
                 load_group_rows(1, wgo)
-
 
         def unit_parts(u):
             if u < PLACE_UNITS:
@@ -145,9 +148,9 @@ def tile_list_siluS_kernel(
                     in_=st_rows[:, first : first + len(parts), places],
                 )
 
-        rows = wv_scales.rearrange("a (q r) n -> r q a n", r=SCALE_ROWS)
+        wv_rows = wv_scales.rearrange("a (q r) n -> r q a n", r=SCALE_ROWS)
         for r in range(SCALE_ROWS):
-            nc.sync.dma_start(out=wv_sc[r:P:32, :, :].bitcast(I32), in_=rows[r].bitcast(I32))
+            nc.sync.dma_start(out=wv_sc[r:P:QUADRANT, :, :].bitcast(I32), in_=wv_rows[r].bitcast(I32))
         nc.sync.dma_start(out=wv_codes[:].bitcast(I32), in_=wv_words.rearrange("a p n -> p a n").bitcast(I32))
         for a in reversed(range(PASSES)):
             words = wk_words[a].rearrange("p n i -> p (n i)")
@@ -159,11 +162,11 @@ def tile_list_siluS_kernel(
             load_state(u)
 
         picked = keep.tile([P, PACK, J], F32, name="picked", align_bytes=64)
-        single = keep.tile([P, 1, J], F32, name="single")
+        early = keep.tile([P, 1, J], F32, name="early")
         grouped_first = [
             keep.tile([P, HALF, PACK], BF16, name=f"grouped_first{h}", align_bytes=64) for h in range(HALVES)
         ]
-        last_gathers = HALF + 2 * LATE_STEPS[1]
+        last_gathers = HALF + (LATE_PLANES - 1) * LATE_STEPS[1]
         grouped_piece = [
             late[:, last_gathers + 2 * n * P : last_gathers + 2 * (n + 1) * P]
             .bitcast(BF16)
@@ -178,9 +181,7 @@ def tile_list_siluS_kernel(
         x_codes = {}
         x_sc = {}
 
-        def pair_view(n, cols):
-            if n == 0:
-                return single[:, :, cols]
+        def late_view(cols):
             h = cols.start // HALF
             return late_half[h][:, :, cols.start - h * HALF : cols.stop - h * HALF]
 
@@ -188,19 +189,22 @@ def tile_list_siluS_kernel(
             a, i = divmod(q, PACK)
             if a == 0:
                 dst = picked[:, i, cols]
-            elif i < 2:
-                dst = single[:, 0, cols] if i == 0 else late[:, cols]
+            elif i == 0:
+                dst = early[:, 0, cols]
+            elif i == 1:
+                dst = late[:, cols]
             else:
-                dst = pair_view(1, cols)[:, i - 1, :]
+                dst = late_view(cols)[:, i - 1, :]
             entries = pick[:, cols.start // GROUP : cols.stop // GROUP]
             nc.vector.tensor_tensor(dst, planes[q][:].indirect(entries), wgt_sb[:, cols], MULT)
 
-        def interleave_pair(n, piece):
-            src = pair_view(n, PIECES[piece]).rearrange("p i c -> p c i")
+        def interleave_piece(piece, word_part):
             cols = PIECES[piece]
+            src = early[:, :, cols] if word_part == EARLY_WORD_PART else late_view(cols)
             whole = min(piece, len(QUANTISED) - 1)
             first = QUANTISED[whole].start
-            nc.scalar.copy(grouped_piece[whole][:, cols.start - first : cols.stop - first, (slice(0, 1), slice(1, PACK))[n]], src)
+            dst = grouped_piece[whole][:, cols.start - first : cols.stop - first, word_part]
+            nc.scalar.copy(dst, src.rearrange("p i c -> p c i"))
 
         def quantise(key, src, codes_tag, scales_tag):
             width = src.shape[1]
@@ -294,8 +298,8 @@ def tile_list_siluS_kernel(
                 nc.scalar.copy(wgt_sb[:, cols], back[:, 0 : count * P])
             wgo_by_place = next_bank("wgo_by_place", 0)
             nc.tensor.transpose(wgo_by_place[:, 0:P], group_rows[1][:], ident[:])
-            nc.scalar.copy(wgo_head, wgo_by_place[:, tile_col(0) : 2 * PLACE_TILES : PLACE_TILES])
-            nc.scalar.copy(wgo_t[:], wgo_by_place[:, 0 : P // 2])
+            nc.scalar.copy(wgo_head, wgo_by_place[:, P // 2 + tile_col(0) : P // 2 + 2 * PLACE_TILES : PLACE_TILES])
+            nc.scalar.copy(wgo_t[:], wgo_by_place[:, P // 2 : P])
 
         def sums_by_place(t):
             sums[t] = next_bank("ve", first_sum_banks.get(t))
@@ -340,7 +344,7 @@ def tile_list_siluS_kernel(
 
         def combine(u):
             if u == 0:
-                results[u] = keep.tile([P, HALF], F32, name="result0", tag="pair_late", align_bytes=64)
+                results[u] = keep.tile([P, HALF], F32, name="result0", tag="late", align_bytes=64)
                 for part in (slice(0, 2 * P), slice(2 * P, HALF)):
                     nc.vector.tensor_tensor(results[u][:, part], turned[u][:, part], gates[u][:, part], MULT)
                 return
@@ -364,9 +368,9 @@ def tile_list_siluS_kernel(
             gather(0, cols)
         for q in PLANE_ORDER[1:5]:
             gather(q)
-            if q == 4:
+            if q == PACK:
                 for n in range(len(PIECES)):
-                    interleave_pair(0, n)
+                    interleave_piece(n, EARLY_WORD_PART)
             if q % 2:
                 for h in range(HALVES):
                     src = picked[:, q - 1 : q + 1, half_cols(h)].rearrange("p i c -> p c i")
@@ -377,13 +381,13 @@ def tile_list_siluS_kernel(
 
         gather(6, half_cols(0))
         gather(7, slice(0, 2 * P))
-        interleave_pair(1, 0)
-        interleave_pair(1, 1)
+        interleave_piece(0, LATE_WORD_PART)
+        interleave_piece(1, LATE_WORD_PART)
         gather(7, PIECES[2])
         quantise((1, 0), grouped_piece[0], "codes_10", "scales_10")
         gather(6, half_cols(1))
         quantise((1, 1), grouped_piece[1], "codes_11", "scales_11")
-        interleave_pair(1, 2)
+        interleave_piece(2, LATE_WORD_PART)
         sums_by_place(0)
         make_keys(0)
         scale_by_place(0)
@@ -391,7 +395,7 @@ def tile_list_siluS_kernel(
         sums_by_place(1)
         for n in SECOND_HALF_PIECES:
             gather(7, PIECES[n])
-            interleave_pair(1, n)
+            interleave_piece(n, LATE_WORD_PART)
         quantise((1, 2), grouped_piece[2], "codes_12", "scales_12")
         make_match(0)
         make_gate(0)

@@ -34,9 +34,10 @@ RING_BANKS = 5
 QUADRANT = 32
 SCALE_ROWS = 4
 FIRST_PLANE_PIECES = (slice(0, 2 * P), slice(2 * P, HALF), slice(HALF, J))
-PIECES = (slice(0, P), slice(P, 2 * P), slice(2 * P, HALF), slice(HALF, HALF + 2 * P), slice(HALF + 2 * P, J))
-QUANTISED = PIECES[:3] + (slice(HALF, J),)
-SECOND_HALF_PIECES = range(3, 5)
+PIECES = (slice(0, P), slice(P, HALF), slice(HALF, HALF + 2 * P), slice(HALF + 2 * P, J))
+QUANTISED = PIECES[:2] + (slice(HALF, J),)
+SECOND_HALF_PIECES = range(2, 4)
+PAIRS = [slice(n * 2 * P, (n + 1) * 2 * P) for n in range(PLACE_TILES // 2)]
 PLANE_ORDER = (0, 1, 4, 2, 3, 5, 6, 7)
 EARLY_WORD_PART = slice(0, 1)
 LATE_WORD_PART = slice(1, PACK)
@@ -168,13 +169,10 @@ def tile_list_siluS_kernel(
         ]
         last_gathers = HALF + (LATE_PLANES - 1) * LATE_STEPS[1]
         grouped_piece = [
-            late[:, last_gathers + 2 * n * P : last_gathers + 2 * (n + 1) * P]
-            .bitcast(BF16)
-            .rearrange("p (c i) -> p c i", i=PACK)
-            for n in range(2)
+            late[:, last_gathers + P : last_gathers + 3 * P].bitcast(BF16).rearrange("p (c i) -> p c i", i=PACK)
         ] + [
             keep.tile([P, c.stop - c.start, PACK], BF16, name=f"grouped_piece{n}", tag=f"grouped{n}", align_bytes=64)
-            for n, c in list(enumerate(QUANTISED))[2:]
+            for n, c in list(enumerate(QUANTISED))[1:]
         ]
         last_words = grouped_piece[-1][:].rearrange("p c i -> p (c i)").bitcast(F32).rearrange("p (c w) -> p c w", w=2)
         wgo_head = last_words[:, 2 * P - 1 : 2 * P + 1, 1]
@@ -245,7 +243,7 @@ def tile_list_siluS_kernel(
             keys[u] = next_bank("ke", first_key_banks.get(u))
             runs = []
             for span, r, places in unit_parts(u):
-                for c in PIECES:
+                for c in PAIRS:
                     start, stop = max(c.start, places.start), min(c.stop, places.stop)
                     if start < stop:
                         first = span.start + start - places.start
@@ -286,12 +284,16 @@ def tile_list_siluS_kernel(
 
         def spread_group_weights():
             by_place = next_bank("by_place", 0)
-            nc.tensor.transpose(by_place[:, 0:P], group_rows[0][:], ident[:])
-            wgt_t = by_place[:, 0 : P // 2].rearrange("p (g t o) -> p t g o", g=GROUPS, o=1)
+            again = next_bank("by_place_again", 1)
+            for bank in (by_place, again):
+                nc.tensor.transpose(bank[:, 0:P], group_rows[0][:], ident[:])
             for wide, cols in zip(wgt_wide, FIRST_PLANE_PIECES):
                 tiles = slice(tile_col(cols.start // P), tile_col(cols.stop // P - 1) + 1)
                 count = tiles.stop - tiles.start
-                nc.vector.tensor_copy(wide[:], wgt_t[:, tiles].to_broadcast([P, count, GROUPS, GROUP]))
+                last = cols.stop == J
+                wgt_t = (again if last else by_place)[:, 0 : P // 2].rearrange("p (g t o) -> p t g o", g=GROUPS, o=1)
+                repeat = nc.scalar.copy if last else nc.vector.tensor_copy
+                repeat(wide[:], wgt_t[:, tiles].to_broadcast([P, count, GROUPS, GROUP]))
                 back = psum_spread.tile([P, HALF], F32, name="back")
                 for n in range(count):
                     nc.tensor.transpose(back[:, block(n)], wide[:, n].rearrange("p g s -> p (g s)"), ident[:])
@@ -382,27 +384,25 @@ def tile_list_siluS_kernel(
         gather(6, half_cols(0))
         gather(7, slice(0, 2 * P))
         interleave_piece(0, LATE_WORD_PART)
-        interleave_piece(1, LATE_WORD_PART)
-        gather(7, PIECES[2])
+        gather(7, PAIRS[1])
         quantise((1, 0), grouped_piece[0], "codes_10", "scales_10")
         gather(6, half_cols(1))
-        quantise((1, 1), grouped_piece[1], "codes_11", "scales_11")
-        interleave_piece(2, LATE_WORD_PART)
+        interleave_piece(1, LATE_WORD_PART)
         sums_by_place(0)
         make_keys(0)
         scale_by_place(0)
-        make_keys(1)
-        sums_by_place(1)
         for n in SECOND_HALF_PIECES:
             gather(7, PIECES[n])
             interleave_piece(n, LATE_WORD_PART)
-        quantise((1, 2), grouped_piece[2], "codes_12", "scales_12")
+        quantise((1, 1), grouped_piece[1], "codes_11", "scales_11")
+        make_keys(1)
+        sums_by_place(1)
         make_match(0)
         make_gate(0)
         turn_values(0)
         copy_keys(1)
         quantise((0, 1), grouped_first[1], "codes_10", "scales_01")
-        quantise((1, 3), grouped_piece[3], "codes_13", "scales_10")
+        quantise((1, 2), grouped_piece[2], "codes_12", "scales_10")
         combine(0)
         make_match(1)
         scale_by_place(1)

@@ -18,6 +18,7 @@ SILU = mybir.ActivationFunctionType.Silu
 COPY = mybir.ActivationFunctionType.Copy
 
 P = 128
+BURST = 256
 PACK = 4
 PASSES = K // (P * PACK)
 PLANES = PASSES * PACK
@@ -67,9 +68,9 @@ def tile_list_siluS_kernel(
         pick = keep.tile([P, J // GROUP], U16, name="pick")
         place = keep.tile([P, J // GROUP], U16, name="place")
         wgt_sb = keep.tile([P, J], F32, name="wgt_sb")
-        planes = [keep.tile([P, T], F32, name=f"plane{q}", tag=f"plane{q}", align_bytes=64) for q in range(PLANES)]
-        wk_codes = [keep.tile([P, N], U32, name=f"wk_codes{a}", align_bytes=64) for a in range(PASSES)]
-        wv_codes = keep.tile([P, PASSES, 2 * N], U8, name="wv_codes", align_bytes=64)
+        planes = [keep.tile([P, T], F32, name=f"plane{q}", tag=f"plane{q}", align_bytes=BURST) for q in range(PLANES)]
+        wk_codes = [keep.tile([P, N], U32, name=f"wk_codes{a}", align_bytes=BURST) for a in range(PASSES)]
+        wv_codes = keep.tile([P, PASSES, 2 * N], U8, name="wv_codes", align_bytes=BURST)
         wk_sc = keep.tile([P, N], U8, name="wk_sc", align_bytes=64)
         wv_sc = keep.tile([P, PASSES, N], U8, name="wv_sc", align_bytes=64)
         late = keep.tile([P, HALF + LATE_PLANES * LATE_STEPS[1]], F32, name="late", tag="late", align_bytes=64)
@@ -81,11 +82,17 @@ def tile_list_siluS_kernel(
         group_rows = [keep.tile([P, P], F32, name=f"group_rows_{w}") for w in ("wgt", "wgo")]
         wgo_t = keep.tile([P, P // 2], F32, name="wgo_t")
         wgt_wide = [
-            keep.tile([P, (c.stop - c.start) // P, GROUPS, GROUP], F32, name=f"wgt_wide{n}", tag=f"window{1 + n}")
+            keep.tile(
+                [P, (c.stop - c.start) // P, GROUPS, GROUP],
+                F32,
+                name=f"wgt_wide{n}",
+                tag=f"window{1 + n}",
+                align_bytes=BURST,
+            )
             for n, c in enumerate(FIRST_PLANE_PIECES)
         ]
         ident = keep.tile([P, P], F32, name="ident")
-        zeros = keep.tile([P, P], F32, name="zeros", tag="window0")
+        zeros = keep.tile([P, P], F32, name="zeros", tag="window0", align_bytes=BURST)
         windows = []
         warm = keep.tile([P, 8], F32, name="warm")
 
@@ -322,7 +329,8 @@ def tile_list_siluS_kernel(
         def scale_by_place(t):
             if t not in sums:
                 sums_by_place(t)
-            scaled[t] = keep.tile([P, N], F32, name=f"scaled{t}", tag=scaled_slots[t], align_bytes=64)
+            align = BURST if t < 2 else 64
+            scaled[t] = keep.tile([P, N], F32, name=f"scaled{t}", tag=scaled_slots[t], align_bytes=align)
             src = sums[t][:].rearrange("p (r g c) -> p r g c", g=GROUPS, c=GROUP)
             dst = scaled[t][:].rearrange("p (r g c) -> p r g c", g=GROUPS, c=GROUP)
             for g in range(GROUPS):
@@ -363,7 +371,7 @@ def tile_list_siluS_kernel(
 
         spread_group_weights()
         for r in range(ROW_TILES):
-            windows.append(keep.tile([P, T], F32, name=f"window{r}", tag=f"window{r}"))
+            windows.append(keep.tile([P, T], F32, name=f"window{r}", tag=f"window{r}", align_bytes=BURST))
             nc.gpsimd.memset(windows[r][:].bitcast(I32), 0)
 
         for cols in FIRST_PLANE_PIECES:

@@ -78,7 +78,11 @@ def tile_list_siluS_kernel(
             late[:, h * HALF : h * HALF + LATE_PLANES * LATE_STEPS[h]].rearrange("p (i c) -> p i c", i=LATE_PLANES)
             for h in range(HALVES)
         ]
-        st_sb = [keep.tile([P, HALF], F32, name=f"st{u}", tag=f"st{u}", align_bytes=64)[:] for u in range(UNITS)]
+        st_first = [
+            keep.tile([P, ROW_TILES, P], F32, name=f"st{t}", tag=f"st{t}", align_bytes=64)
+            for t in range(PLACE_TILES // 2)
+        ]
+        st_second = keep.tile([P, ROW_TILES, HALF], F32, name="st_second", align_bytes=BURST)
         group_rows = [keep.tile([P, P], F32, name=f"group_rows_{w}") for w in ("wgt", "wgo")]
         wgo_t = keep.tile([P, P // 2], F32, name="wgo_t")
         wgt_wide = [
@@ -110,13 +114,14 @@ def tile_list_siluS_kernel(
             pattern=[[-1, P]],
             channel_multiplier=1,
         )
-        nc.vector.memset(wk_sc[:].bitcast(I32), 0)
-        nc.vector.memset(wv_sc[:].rearrange("p a n -> p (a n)").bitcast(I32), 0)
+        nc.gpsimd.memset(wk_sc[:].bitcast(I32), 0)
+        nc.gpsimd.memset(wv_sc[:].rearrange("p a n -> p (a n)").bitcast(I32), 0)
 
-        for quad in range(P // QUADRANT):
-            rows = wk_scales[:, quad * SCALE_ROWS : (quad + 1) * SCALE_ROWS, :]
-            first = QUADRANT * quad + SCALE_ROWS
-            nc.gpsimd.dma_start(out=wk_sc[first : first + PASSES * SCALE_ROWS, :].bitcast(I32), in_=rows.bitcast(I32))
+        def load_key_scales():
+            for quad in range(P // QUADRANT):
+                rows = wk_scales[:, quad * SCALE_ROWS : (quad + 1) * SCALE_ROWS, :].bitcast(I32)
+                first = QUADRANT * quad + SCALE_ROWS
+                nc.sync.dma_start(out=wk_sc[first : first + PASSES * SCALE_ROWS, :].bitcast(I32), in_=rows)
 
         def load_group_rows(n, weights):
             step = GROUP // 2 * J - HALF
@@ -132,6 +137,8 @@ def tile_list_siluS_kernel(
                 nc.sync.dma_start(pick[:], offs)
             if q == 1:
                 load_group_rows(1, wgo)
+            if q == PLANE_ORDER[2]:
+                load_key_scales()
 
         def unit_parts(u):
             if u < PLACE_UNITS:
@@ -145,16 +152,15 @@ def tile_list_siluS_kernel(
 
         st_rows = st.rearrange("(r p) j -> p r j", p=P)
 
-        def load_state(u):
+        def state(u):
             parts = unit_parts(u)
             span, first, places = parts[0]
-            if len(parts) == 1:
-                nc.sync.dma_start(out=st_sb[u][:, span], in_=st_rows[:, first, places])
-            else:
-                nc.sync.dma_start(
-                    out=st_sb[u][:, unit_cols(u)].rearrange("p (r j) -> p r j", r=len(parts)),
-                    in_=st_rows[:, first : first + len(parts), places],
-                )
+            if places.start < HALF:
+                return st_first[u][:]
+            return st_second[:, first : first + len(parts), places.start - HALF : places.stop - HALF]
+
+        def by_part(ap, u):
+            return ap[:, unit_cols(u)].rearrange("p (r j) -> p r j", r=len(unit_parts(u)))
 
         wv_rows = wv_scales.rearrange("a (q r) n -> r q a n", r=SCALE_ROWS)
         for r in range(SCALE_ROWS):
@@ -163,11 +169,11 @@ def tile_list_siluS_kernel(
         for a in reversed(range(PASSES)):
             words = wk_words[a].rearrange("p n i -> p (n i)")
             nc.sync.dma_start(out=wk_codes[a][:].bitcast(I32), in_=words.bitcast(I32))
-        load_state(0)
-        load_state(1)
-        nc.sync.dma_start(place[:], offs2)
-        for u in range(2, UNITS):
-            load_state(u)
+        for t, tile in enumerate(st_first):
+            nc.sync.dma_start(out=tile[:], in_=st_rows[:, :, block(t)])
+            if t == 1:
+                nc.sync.dma_start(place[:], offs2)
+        nc.sync.dma_start(out=st_second[:], in_=st_rows[:, :, half_cols(1)])
 
         picked = keep.tile([P, PACK, J], F32, name="picked", align_bytes=64)
         early = keep.tile([P, 1, J], F32, name="early")
@@ -273,17 +279,16 @@ def tile_list_siluS_kernel(
             nc.scalar.copy(key_sb[u][:, unit_cols(u)], keys[u][:, unit_cols(u)])
 
         def make_match(u):
-            cols = unit_cols(u)
             if u == 0:
                 matches[u] = keep.tile([P, HALF], F32, name="match0", align_bytes=64)
-                nc.vector.tensor_tensor(matches[u][:], keys[u][:], st_sb[u], MULT)
+                nc.vector.tensor_tensor(by_part(matches[u], u), by_part(keys[u], u), state(u), MULT)
                 return
             tag = {1: f"grouped{len(QUANTISED) - 1}", 2: "gate0"}.get(u, f"value{u - 2}")
             matches[u] = keep.tile([P, HALF], F32, name=f"match{u}", tag=tag, align_bytes=64)
-            nc.gpsimd.tensor_tensor(matches[u][:, cols], key_sb[u][:, cols], st_sb[u][:, cols], MULT)
+            nc.gpsimd.tensor_tensor(by_part(matches[u], u), by_part(key_sb[u], u), state(u), MULT)
 
         def make_gate(u):
-            if u in (0, 2, 3):
+            if u < 4:
                 gates[u] = keep.tile([P, HALF], F32, name=f"gate{u}", tag=f"gate{u}", align_bytes=64)
             else:
                 gates[u] = ring.tile([P, HALF], F32, name="gate")
@@ -324,7 +329,7 @@ def tile_list_siluS_kernel(
                     stop=(a == PASSES - 1),
                 )
 
-        scaled_slots = ["plane0", "plane1", "st1", "st2", "st3", "gate2", "st4", "gate3"]
+        scaled_slots = ["plane0", "plane1", "st1", "st2", "gate1", "st3", "gate2", "gate3"]
 
         def scale_by_place(t):
             if t not in sums:

@@ -34,7 +34,7 @@ SPLIT_RESULTS = 3
 RING_BANKS = 5
 QUADRANT = 32
 SCALE_ROWS = 4
-FIRST_PLANE_PIECES = (slice(0, 2 * P), slice(2 * P, HALF), slice(HALF, J))
+FIRST_PLANE_PIECES = (slice(0, P), slice(P, 2 * P), slice(2 * P, HALF), slice(HALF, J))
 PIECES = (slice(0, P), slice(P, HALF), slice(HALF, HALF + 2 * P), slice(HALF + 2 * P, J))
 QUANTISED = PIECES[:2] + (slice(HALF, J),)
 SECOND_HALF_PIECES = range(2, 4)
@@ -54,7 +54,7 @@ def tile_list_siluS_kernel(
         keep = ctx.enter_context(tc.tile_pool(name="keep", bufs=1))
         ring = ctx.enter_context(tc.tile_pool(name="ring", bufs=3))
         psum_ring = ctx.enter_context(tc.psum_pool(name="psum_ring", bufs=1))
-        psum_spread = ctx.enter_context(tc.psum_pool(name="psum_spread", bufs=len(FIRST_PLANE_PIECES)))
+        psum_spread = ctx.enter_context(tc.psum_pool(name="psum_spread", bufs=len(FIRST_PLANE_PIECES) - 1))
 
         def half_cols(h):
             return slice(h * HALF, (h + 1) * HALF)
@@ -90,17 +90,17 @@ def tile_list_siluS_kernel(
                 [P, (c.stop - c.start) // P, GROUPS, GROUP],
                 F32,
                 name=f"wgt_wide{n}",
-                tag=f"window{1 + n}",
+                tag=f"window{n}",
                 align_bytes=BURST,
             )
             for n, c in enumerate(FIRST_PLANE_PIECES)
         ]
         ident = keep.tile([P, P], F32, name="ident")
-        zeros = keep.tile([P, P], F32, name="zeros", tag="window0", align_bytes=BURST)
+        zeros = keep.tile([P, P], F32, name="zeros")
         windows = []
         warm = keep.tile([P, 8], F32, name="warm")
 
-        nc.vector.memset(zeros[:], 0.0)
+        nc.gpsimd.memset(zeros[:], 0.0)
         for n, tile in enumerate(group_rows):
             nc.vector.memset(tile[(1 - n) * P // 2 : (2 - n) * P // 2, :], 0.0)
         nc.vector.memset(warm[:], 0.0)
@@ -135,9 +135,9 @@ def tile_list_siluS_kernel(
             nc.sync.dma_start(out=planes[q][:], in_=x_rows[:, q // PACK, q % PACK, :])
             if q == 0:
                 nc.sync.dma_start(pick[:], offs)
-            if q == 1:
+            if q == PLANE_ORDER[1]:
                 load_group_rows(1, wgo)
-            if q == PLANE_ORDER[2]:
+            if q == PLANE_ORDER[5]:
                 load_key_scales()
 
         def unit_parts(u):
@@ -306,7 +306,7 @@ def tile_list_siluS_kernel(
                 wgt_t = (again if last else by_place)[:, 0 : P // 2].rearrange("p (g t o) -> p t g o", g=GROUPS, o=1)
                 repeat = nc.scalar.copy if last else nc.vector.tensor_copy
                 repeat(wide[:], wgt_t[:, tiles].to_broadcast([P, count, GROUPS, GROUP]))
-                back = psum_spread.tile([P, HALF], F32, name="back")
+                back = next_bank("back_last", 2) if last else psum_spread.tile([P, HALF], F32, name="back")
                 for n in range(count):
                     nc.tensor.transpose(back[:, block(n)], wide[:, n].rearrange("p g s -> p (g s)"), ident[:])
                 nc.scalar.copy(wgt_sb[:, cols], back[:, 0 : count * P])

@@ -34,7 +34,8 @@ SPLIT_RESULTS = 3
 RING_BANKS = 5
 QUADRANT = 32
 SCALE_ROWS = 4
-FIRST_PLANE_PIECES = (slice(0, P), slice(P, 2 * P), slice(2 * P, HALF), slice(HALF, J))
+SQUARE = 32
+SPREAD_PIECES = [slice(n * 2 * P, (n + 1) * 2 * P) for n in range(J // (2 * P))]
 PIECES = (slice(0, P), slice(P, HALF), slice(HALF, HALF + 2 * P), slice(HALF + 2 * P, J))
 QUANTISED = PIECES[:2] + (slice(HALF, J),)
 SECOND_HALF_PIECES = range(2, 4)
@@ -54,7 +55,6 @@ def tile_list_siluS_kernel(
         keep = ctx.enter_context(tc.tile_pool(name="keep", bufs=1))
         ring = ctx.enter_context(tc.tile_pool(name="ring", bufs=3))
         psum_ring = ctx.enter_context(tc.psum_pool(name="psum_ring", bufs=1))
-        psum_spread = ctx.enter_context(tc.psum_pool(name="psum_spread", bufs=len(FIRST_PLANE_PIECES) - 1))
 
         def half_cols(h):
             return slice(h * HALF, (h + 1) * HALF)
@@ -67,7 +67,7 @@ def tile_list_siluS_kernel(
 
         pick = keep.tile([P, J // GROUP], U16, name="pick")
         place = keep.tile([P, J // GROUP], U16, name="place")
-        wgt_sb = keep.tile([P, J], F32, name="wgt_sb")
+        wgt_sb = keep.tile([P, J], F32, name="wgt_sb", align_bytes=64)
         planes = [keep.tile([P, T], F32, name=f"plane{q}", tag=f"plane{q}", align_bytes=BURST) for q in range(PLANES)]
         wk_codes = [keep.tile([P, N], U32, name=f"wk_codes{a}", align_bytes=BURST) for a in range(PASSES)]
         wv_codes = keep.tile([P, PASSES, 2 * N], U8, name="wv_codes", align_bytes=BURST)
@@ -83,28 +83,24 @@ def tile_list_siluS_kernel(
             for t in range(PLACE_TILES // 2)
         ]
         st_second = keep.tile([P, ROW_TILES, HALF], F32, name="st_second", align_bytes=BURST)
-        group_rows = [keep.tile([P, P], F32, name=f"group_rows_{w}") for w in ("wgt", "wgo")]
+        wgt_rows = keep.tile([P, 2, SQUARE], F32, name="wgt_rows", align_bytes=64)
+        wgt_cols = keep.tile([P, 2, SQUARE], F32, name="wgt_cols", align_bytes=64)
+        wgt_wide = keep.tile([P, J], F32, name="wgt_wide", align_bytes=64)
+        wgo_rows = keep.tile([P, P], F32, name="wgo_rows")
         wgo_t = keep.tile([P, P // 2], F32, name="wgo_t")
-        wgt_wide = [
-            keep.tile(
-                [P, (c.stop - c.start) // P, GROUPS, GROUP],
-                F32,
-                name=f"wgt_wide{n}",
-                tag=f"window{n}",
-                align_bytes=BURST,
-            )
-            for n, c in enumerate(FIRST_PLANE_PIECES)
-        ]
         ident = keep.tile([P, P], F32, name="ident")
         zeros = keep.tile([P, P], F32, name="zeros")
-        windows = []
-        warm = keep.tile([P, 8], F32, name="warm")
+        windows = [keep.tile([P, T], F32, name=f"window{r}", align_bytes=BURST) for r in range(ROW_TILES)]
+        warm = keep.tile([P, 2], F32, name="warm")
 
-        nc.gpsimd.memset(zeros[:], 0.0)
-        for n, tile in enumerate(group_rows):
-            nc.vector.memset(tile[(1 - n) * P // 2 : (2 - n) * P // 2, :], 0.0)
-        nc.vector.memset(warm[:], 0.0)
+        nc.vector.memset(warm[:, 0:1], 0.0)
         nc.scalar.activation(warm[:, 1:2], warm[:, 0:1], SILU)
+        for window in windows[:-1]:
+            nc.gpsimd.memset(window[:].bitcast(I32), 0)
+        for part in (slice(0, T - 1), slice(T - 1, T)):
+            nc.vector.memset(windows[-1][:, part].bitcast(I32), 0)
+        nc.gpsimd.memset(zeros[:], 0.0)
+        nc.gpsimd.memset(wgo_rows[0 : P // 2, :], 0.0)
         nc.gpsimd.affine_select(
             out=ident[:],
             in_=zeros[:],
@@ -123,20 +119,22 @@ def tile_list_siluS_kernel(
                 first = QUADRANT * quad + SCALE_ROWS
                 nc.sync.dma_start(out=wk_sc[first : first + PASSES * SCALE_ROWS, :].bitcast(I32), in_=rows)
 
-        def load_group_rows(n, weights):
+        def group_runs(weights):
             step = GROUP // 2 * J - HALF
-            runs = weights.rearrange("p j -> (p j)")[step : step * (2 * GROUPS + 1)].rearrange("(h x) -> h x", x=step)
-            rows = runs[:, 0:HALF].rearrange("h (t c) -> h t c", c=P)
-            nc.sync.dma_start(out=group_rows[n][n * P // 2 : (n + 1) * P // 2, :], in_=rows)
+            runs = weights.rearrange("p j -> (p j)")[step : step * (2 * GROUPS + 1)].rearrange("(u x) -> u x", x=step)
+            return runs[:, 0:HALF]
 
-        load_group_rows(0, wgt)
+        nc.sync.dma_start(
+            out=wgt_rows[:].rearrange("p b r -> p (b r)"),
+            in_=group_runs(wgt).rearrange("u (m c) -> u m c", c=2 * SQUARE),
+        )
         x_rows = xT.rearrange("(a p i) t -> p a i t", a=PASSES, i=PACK)
         for q in PLANE_ORDER:
             nc.sync.dma_start(out=planes[q][:], in_=x_rows[:, q // PACK, q % PACK, :])
             if q == 0:
                 nc.sync.dma_start(pick[:], offs)
             if q == PLANE_ORDER[1]:
-                load_group_rows(1, wgo)
+                nc.sync.dma_start(out=wgo_rows[P // 2 : P, :], in_=group_runs(wgo).rearrange("u (t c) -> u t c", c=P))
             if q == PLANE_ORDER[5]:
                 load_key_scales()
 
@@ -295,23 +293,17 @@ def tile_list_siluS_kernel(
             nc.scalar.activation(gates[u][:, unit_cols(u)], matches[u][:, unit_cols(u)], SILU)
 
         def spread_group_weights():
-            by_place = next_bank("by_place", 0)
-            again = next_bank("by_place_again", 1)
-            for bank in (by_place, again):
-                nc.tensor.transpose(bank[:, 0:P], group_rows[0][:], ident[:])
-            for wide, cols in zip(wgt_wide, FIRST_PLANE_PIECES):
-                tiles = slice(tile_col(cols.start // P), tile_col(cols.stop // P - 1) + 1)
-                count = tiles.stop - tiles.start
-                last = cols.stop == J
-                wgt_t = (again if last else by_place)[:, 0 : P // 2].rearrange("p (g t o) -> p t g o", g=GROUPS, o=1)
-                repeat = nc.scalar.copy if last else nc.vector.tensor_copy
-                repeat(wide[:], wgt_t[:, tiles].to_broadcast([P, count, GROUPS, GROUP]))
-                back = next_bank("back_last", 2) if last else psum_spread.tile([P, HALF], F32, name="back")
-                for n in range(count):
-                    nc.tensor.transpose(back[:, block(n)], wide[:, n].rearrange("p g s -> p (g s)"), ident[:])
-                nc.scalar.copy(wgt_sb[:, cols], back[:, 0 : count * P])
+            for b in range(2):
+                nc.vector.transpose(wgt_cols[:, b, :], wgt_rows[:, b, :])
+            by_run = wgt_cols[:].rearrange("p b (h m o) -> p m b h o", h=2, o=1)
+            for cols in SPREAD_PIECES:
+                first = (cols.start // (2 * SQUARE) + GROUP // 2) % GROUP
+                count = (cols.stop - cols.start) // (2 * SQUARE)
+                dst = wgt_wide[:, cols].rearrange("p (m b h s) -> p m b h s", b=2, h=2, s=GROUP)
+                nc.scalar.copy(dst, by_run[:, first : first + count].to_broadcast([P, count, 2, 2, GROUP]))
+                nc.vector.transpose(wgt_sb[:, cols], wgt_wide[:, cols])
             wgo_by_place = next_bank("wgo_by_place", 0)
-            nc.tensor.transpose(wgo_by_place[:, 0:P], group_rows[1][:], ident[:])
+            nc.tensor.transpose(wgo_by_place[:, 0:P], wgo_rows[:], ident[:])
             nc.scalar.copy(wgo_head, wgo_by_place[:, P // 2 + tile_col(0) : P // 2 + 2 * PLACE_TILES : PLACE_TILES])
             nc.scalar.copy(wgo_t[:], wgo_by_place[:, P // 2 : P])
 
@@ -375,13 +367,8 @@ def tile_list_siluS_kernel(
                     nc.sync.dma_start(out=out[block(r), :], in_=windows[r][:])
 
         spread_group_weights()
-        for r in range(ROW_TILES):
-            windows.append(keep.tile([P, T], F32, name=f"window{r}", tag=f"window{r}", align_bytes=BURST))
-            nc.gpsimd.memset(windows[r][:].bitcast(I32), 0)
 
-        for cols in FIRST_PLANE_PIECES:
-            gather(0, cols)
-        for q in PLANE_ORDER[1:5]:
+        for q in PLANE_ORDER[0:5]:
             gather(q)
             if q == PACK:
                 for n in range(len(PIECES)):

@@ -18,6 +18,8 @@ SILU = mybir.ActivationFunctionType.Silu
 COPY = mybir.ActivationFunctionType.Copy
 
 P = 128
+WINDOW_BYTES = 4 * T
+CLEARED_EARLY = 768
 BURST = 256
 PACK = 4
 PASSES = K // (P * PACK)
@@ -54,6 +56,7 @@ def tile_list_siluS_kernel(
     with ExitStack() as ctx:
         keep = ctx.enter_context(tc.tile_pool(name="keep", bufs=1))
         ring = ctx.enter_context(tc.tile_pool(name="ring", bufs=3))
+        shared = ctx.enter_context(tc.tile_pool(name="shared", bufs=1))
         psum_ring = ctx.enter_context(tc.psum_pool(name="psum_ring", bufs=1))
 
         def half_cols(h):
@@ -71,8 +74,6 @@ def tile_list_siluS_kernel(
         planes = [keep.tile([P, T], F32, name=f"plane{q}", tag=f"plane{q}", align_bytes=BURST) for q in range(PLANES)]
         wk_codes = [keep.tile([P, N], U32, name=f"wk_codes{a}", align_bytes=BURST) for a in range(PASSES)]
         wv_codes = keep.tile([P, PASSES, 2 * N], U8, name="wv_codes", align_bytes=BURST)
-        wk_sc = keep.tile([P, N], U8, name="wk_sc", align_bytes=64)
-        wv_sc = keep.tile([P, PASSES, N], U8, name="wv_sc", align_bytes=64)
         late = keep.tile([P, HALF + LATE_PLANES * LATE_STEPS[1]], F32, name="late", tag="late", align_bytes=64)
         late_half = [
             late[:, h * HALF : h * HALF + LATE_PLANES * LATE_STEPS[h]].rearrange("p (i c) -> p i c", i=LATE_PLANES)
@@ -85,33 +86,26 @@ def tile_list_siluS_kernel(
         st_second = keep.tile([P, ROW_TILES, HALF], F32, name="st_second", align_bytes=BURST)
         wgt_rows = keep.tile([P, 2, SQUARE], F32, name="wgt_rows", align_bytes=64)
         wgt_cols = keep.tile([P, 2, SQUARE], F32, name="wgt_cols", align_bytes=64)
-        wgt_wide = keep.tile([P, J], F32, name="wgt_wide", align_bytes=64)
+        wgt_wide = shared.tile([P, J], F32, name="wgt_wide", offset=WINDOW_BYTES - 4 * BURST)
         wgo_rows = keep.tile([P, P], F32, name="wgo_rows")
         wgo_t = keep.tile([P, P // 2], F32, name="wgo_t")
-        ident = keep.tile([P, P], F32, name="ident")
+        ident = shared.tile([P, P], F32, name="ident", offset=WINDOW_BYTES)
+        wk_sc = keep.tile([P, N], U8, name="wk_sc", align_bytes=64)
+        wv_sc = shared.tile([P, PASSES, N], U8, name="wv_sc", offset=WINDOW_BYTES + 2 * BURST)
         zeros = keep.tile([P, P], F32, name="zeros")
-        windows = [keep.tile([P, T], F32, name=f"window{r}", align_bytes=BURST) for r in range(ROW_TILES)]
+        windows = [keep.tile([P, T], F32, name=f"window{r}", align_bytes=BURST) for r in range(2)] + [
+            shared.tile([P, T], F32, name=f"window{r}", align_bytes=BURST, offset=at)
+            for r, at in ((2, 0), (3, WINDOW_BYTES + 6 * BURST))
+        ]
         warm = keep.tile([P, 2], F32, name="warm")
 
         nc.vector.memset(warm[:, 0:1], 0.0)
         nc.scalar.activation(warm[:, 1:2], warm[:, 0:1], SILU)
-        for window in windows[:-1]:
-            nc.gpsimd.memset(window[:].bitcast(I32), 0)
-        for part in (slice(0, T - 1), slice(T - 1, T)):
-            nc.vector.memset(windows[-1][:, part].bitcast(I32), 0)
-        nc.gpsimd.memset(zeros[:], 0.0)
-        nc.gpsimd.memset(wgo_rows[0 : P // 2, :], 0.0)
-        nc.gpsimd.affine_select(
-            out=ident[:],
-            in_=zeros[:],
-            compare_op=mybir.AluOpType.not_equal,
-            fill=1.0,
-            base=0,
-            pattern=[[-1, P]],
-            channel_multiplier=1,
-        )
-        nc.gpsimd.memset(wk_sc[:].bitcast(I32), 0)
-        nc.gpsimd.memset(wv_sc[:].rearrange("p a n -> p (a n)").bitcast(I32), 0)
+        nc.vector.memset(zeros[:], 0.0)
+        nc.vector.memset(wgo_rows[0 : P // 2, :], 0.0)
+        nc.vector.memset(wk_sc[:].bitcast(I32), 0)
+        nc.vector.memset(windows[0][:].bitcast(I32), 0)
+        nc.vector.memset(windows[1][:, 0:CLEARED_EARLY].bitcast(I32), 0)
 
         def load_key_scales():
             for quad in range(P // QUADRANT):
@@ -128,6 +122,30 @@ def tile_list_siluS_kernel(
             out=wgt_rows[:].rearrange("p b r -> p (b r)"),
             in_=group_runs(wgt).rearrange("u (m c) -> u m c", c=2 * SQUARE),
         )
+        for b in range(2):
+            nc.vector.transpose(wgt_cols[:, b, :], wgt_rows[:, b, :])
+        nc.vector.memset(windows[1][:, CLEARED_EARLY:T].bitcast(I32), 0)
+        by_run = wgt_cols[:].rearrange("p b (h m o) -> p m b h o", h=2, o=1)
+        for cols in SPREAD_PIECES:
+            first = (cols.start // (2 * SQUARE) + GROUP // 2) % GROUP
+            count = (cols.stop - cols.start) // (2 * SQUARE)
+            dst = wgt_wide[:, cols].rearrange("p (m b h s) -> p m b h s", b=2, h=2, s=GROUP)
+            nc.scalar.copy(dst, by_run[:, first : first + count].to_broadcast([P, count, 2, 2, GROUP]))
+            nc.vector.transpose(wgt_sb[:, cols], wgt_wide[:, cols])
+
+        nc.gpsimd.affine_select(
+            out=ident[:],
+            in_=zeros[:],
+            compare_op=mybir.AluOpType.not_equal,
+            fill=1.0,
+            base=0,
+            pattern=[[-1, P]],
+            channel_multiplier=1,
+        )
+        nc.gpsimd.memset(wv_sc[:].rearrange("p a n -> p (a n)").bitcast(I32), 0)
+        for window in windows[2:]:
+            nc.gpsimd.memset(window[:].bitcast(I32), 0)
+
         x_rows = xT.rearrange("(a p i) t -> p a i t", a=PASSES, i=PACK)
         for q in PLANE_ORDER:
             nc.sync.dma_start(out=planes[q][:], in_=x_rows[:, q // PACK, q % PACK, :])
@@ -292,16 +310,7 @@ def tile_list_siluS_kernel(
                 gates[u] = ring.tile([P, HALF], F32, name="gate")
             nc.scalar.activation(gates[u][:, unit_cols(u)], matches[u][:, unit_cols(u)], SILU)
 
-        def spread_group_weights():
-            for b in range(2):
-                nc.vector.transpose(wgt_cols[:, b, :], wgt_rows[:, b, :])
-            by_run = wgt_cols[:].rearrange("p b (h m o) -> p m b h o", h=2, o=1)
-            for cols in SPREAD_PIECES:
-                first = (cols.start // (2 * SQUARE) + GROUP // 2) % GROUP
-                count = (cols.stop - cols.start) // (2 * SQUARE)
-                dst = wgt_wide[:, cols].rearrange("p (m b h s) -> p m b h s", b=2, h=2, s=GROUP)
-                nc.scalar.copy(dst, by_run[:, first : first + count].to_broadcast([P, count, 2, 2, GROUP]))
-                nc.vector.transpose(wgt_sb[:, cols], wgt_wide[:, cols])
+        def place_output_weights():
             wgo_by_place = next_bank("wgo_by_place", 0)
             nc.tensor.transpose(wgo_by_place[:, 0:P], wgo_rows[:], ident[:])
             nc.scalar.copy(wgo_head, wgo_by_place[:, P // 2 + tile_col(0) : P // 2 + 2 * PLACE_TILES : PLACE_TILES])
@@ -366,7 +375,7 @@ def tile_list_siluS_kernel(
                 if places.stop == J:
                     nc.sync.dma_start(out=out[block(r), :], in_=windows[r][:])
 
-        spread_group_weights()
+        place_output_weights()
 
         for q in PLANE_ORDER[0:5]:
             gather(q)

@@ -89,21 +89,31 @@ def tile_list_siluS_kernel(
         wgt_wide = shared.tile([P, J], F32, name="wgt_wide", offset=WINDOW_BYTES - 4 * BURST)
         wgo_rows = keep.tile([P, P], F32, name="wgo_rows")
         wgo_t = keep.tile([P, P // 2], F32, name="wgo_t")
-        ident = shared.tile([P, P], F32, name="ident", offset=WINDOW_BYTES)
+        ident = keep.tile([P, P], F32, name="ident")
         wk_sc = keep.tile([P, N], U8, name="wk_sc", align_bytes=64)
-        wv_sc = shared.tile([P, PASSES, N], U8, name="wv_sc", offset=WINDOW_BYTES + 2 * BURST)
+        wv_sc = keep.tile([P, PASSES, N], U8, name="wv_sc", align_bytes=64)
         zeros = keep.tile([P, P], F32, name="zeros")
         windows = [keep.tile([P, T], F32, name=f"window{r}", align_bytes=BURST) for r in range(2)] + [
             shared.tile([P, T], F32, name=f"window{r}", align_bytes=BURST, offset=at)
-            for r, at in ((2, 0), (3, WINDOW_BYTES + 6 * BURST))
+            for r, at in ((2, 0), (3, WINDOW_BYTES))
         ]
         warm = keep.tile([P, 2], F32, name="warm")
 
         nc.vector.memset(warm[:, 0:1], 0.0)
         nc.scalar.activation(warm[:, 1:2], warm[:, 0:1], SILU)
-        nc.vector.memset(zeros[:], 0.0)
-        nc.vector.memset(wgo_rows[0 : P // 2, :], 0.0)
-        nc.vector.memset(wk_sc[:].bitcast(I32), 0)
+        nc.gpsimd.memset(zeros[:], 0.0)
+        nc.gpsimd.memset(wgo_rows[0 : P // 2, :], 0.0)
+        nc.gpsimd.affine_select(
+            out=ident[:],
+            in_=zeros[:],
+            compare_op=mybir.AluOpType.not_equal,
+            fill=1.0,
+            base=0,
+            pattern=[[-1, P]],
+            channel_multiplier=1,
+        )
+        nc.gpsimd.memset(wk_sc[:].bitcast(I32), 0)
+        nc.gpsimd.memset(wv_sc[:].rearrange("p a n -> p (a n)").bitcast(I32), 0)
         nc.vector.memset(windows[0][:].bitcast(I32), 0)
         nc.vector.memset(windows[1][:, 0:CLEARED_EARLY].bitcast(I32), 0)
 
@@ -133,16 +143,6 @@ def tile_list_siluS_kernel(
             nc.scalar.copy(dst, by_run[:, first : first + count].to_broadcast([P, count, 2, 2, GROUP]))
             nc.vector.transpose(wgt_sb[:, cols], wgt_wide[:, cols])
 
-        nc.gpsimd.affine_select(
-            out=ident[:],
-            in_=zeros[:],
-            compare_op=mybir.AluOpType.not_equal,
-            fill=1.0,
-            base=0,
-            pattern=[[-1, P]],
-            channel_multiplier=1,
-        )
-        nc.gpsimd.memset(wv_sc[:].rearrange("p a n -> p (a n)").bitcast(I32), 0)
         for window in windows[2:]:
             nc.gpsimd.memset(window[:].bitcast(I32), 0)
 

@@ -19,7 +19,6 @@ COPY = mybir.ActivationFunctionType.Copy
 
 P = 128
 WINDOW_BYTES = 4 * T
-CLEARED_EARLY = 768
 BURST = 256
 PACK = 4
 PASSES = K // (P * PACK)
@@ -37,7 +36,7 @@ RING_BANKS = 5
 QUADRANT = 32
 SCALE_ROWS = 4
 SQUARE = 32
-SPREAD_PIECES = [slice(n * 2 * P, (n + 1) * 2 * P) for n in range(J // (2 * P))]
+SPREAD_PIECES = (slice(0, 2 * P), slice(2 * P, HALF), slice(HALF, J))
 PIECES = (slice(0, P), slice(P, HALF), slice(HALF, HALF + 2 * P), slice(HALF + 2 * P, J))
 QUANTISED = PIECES[:2] + (slice(HALF, J),)
 SECOND_HALF_PIECES = range(2, 4)
@@ -86,36 +85,25 @@ def tile_list_siluS_kernel(
         st_second = keep.tile([P, ROW_TILES, HALF], F32, name="st_second", align_bytes=BURST)
         wgt_rows = keep.tile([P, 2, SQUARE], F32, name="wgt_rows", align_bytes=64)
         wgt_cols = keep.tile([P, 2, SQUARE], F32, name="wgt_cols", align_bytes=64)
-        wgt_wide = shared.tile([P, J], F32, name="wgt_wide", offset=WINDOW_BYTES - 4 * BURST)
+        wgt_wide = shared.tile([P, T + 6 * P], F32, name="wgt_wide", offset=WINDOW_BYTES - BURST)
         wgo_rows = keep.tile([P, P], F32, name="wgo_rows")
         wgo_t = keep.tile([P, P // 2], F32, name="wgo_t")
         ident = keep.tile([P, P], F32, name="ident")
+        diagonal = keep.tile([P, P], F32, name="diagonal")
         wk_sc = keep.tile([P, N], U8, name="wk_sc", align_bytes=64)
-        wv_sc = keep.tile([P, PASSES, N], U8, name="wv_sc", align_bytes=64)
-        zeros = keep.tile([P, P], F32, name="zeros")
-        windows = [keep.tile([P, T], F32, name=f"window{r}", align_bytes=BURST) for r in range(2)] + [
+        wv_sc = shared.tile([P, PASSES, N], U8, name="wv_sc", offset=WINDOW_BYTES)
+        windows = [keep.tile([P, T], F32, name=f"window{r}", align_bytes=BURST) for r in range(1)] + [
             shared.tile([P, T], F32, name=f"window{r}", align_bytes=BURST, offset=at)
-            for r, at in ((2, 0), (3, WINDOW_BYTES))
+            for r, at in ((1, 0), (2, WINDOW_BYTES + 4 * BURST), (3, 2 * WINDOW_BYTES + 4 * BURST))
         ]
         warm = keep.tile([P, 2], F32, name="warm")
 
         nc.vector.memset(warm[:, 0:1], 0.0)
         nc.scalar.activation(warm[:, 1:2], warm[:, 0:1], SILU)
-        nc.gpsimd.memset(zeros[:], 0.0)
-        nc.gpsimd.memset(wgo_rows[0 : P // 2, :], 0.0)
-        nc.gpsimd.affine_select(
-            out=ident[:],
-            in_=zeros[:],
-            compare_op=mybir.AluOpType.not_equal,
-            fill=1.0,
-            base=0,
-            pattern=[[-1, P]],
-            channel_multiplier=1,
-        )
-        nc.gpsimd.memset(wk_sc[:].bitcast(I32), 0)
-        nc.gpsimd.memset(wv_sc[:].rearrange("p a n -> p (a n)").bitcast(I32), 0)
+        nc.gpsimd.iota(diagonal[:], [[1, P]], base=0, channel_multiplier=-1, allow_small_or_imprecise_dtypes=True)
+        nc.vector.memset(wgo_rows[0 : P // 2, :], 0.0)
+        nc.vector.memset(wk_sc[:].bitcast(I32), 0)
         nc.vector.memset(windows[0][:].bitcast(I32), 0)
-        nc.vector.memset(windows[1][:, 0:CLEARED_EARLY].bitcast(I32), 0)
 
         def load_key_scales():
             for quad in range(P // QUADRANT):
@@ -134,16 +122,19 @@ def tile_list_siluS_kernel(
         )
         for b in range(2):
             nc.vector.transpose(wgt_cols[:, b, :], wgt_rows[:, b, :])
-        nc.vector.memset(windows[1][:, CLEARED_EARLY:T].bitcast(I32), 0)
+        nc.vector.tensor_scalar(ident[:], diagonal[:], 0.0, None, mybir.AluOpType.is_equal)
         by_run = wgt_cols[:].rearrange("p b (h m o) -> p m b h o", h=2, o=1)
         for cols in SPREAD_PIECES:
+            repeat = nc.scalar.copy if cols.stop == J else nc.vector.tensor_copy
             first = (cols.start // (2 * SQUARE) + GROUP // 2) % GROUP
             count = (cols.stop - cols.start) // (2 * SQUARE)
             dst = wgt_wide[:, cols].rearrange("p (m b h s) -> p m b h s", b=2, h=2, s=GROUP)
-            nc.scalar.copy(dst, by_run[:, first : first + count].to_broadcast([P, count, 2, 2, GROUP]))
+            repeat(dst, by_run[:, first : first + count].to_broadcast([P, count, 2, 2, GROUP]))
+        for cols in SPREAD_PIECES:
             nc.vector.transpose(wgt_sb[:, cols], wgt_wide[:, cols])
 
-        for window in windows[2:]:
+        nc.gpsimd.memset(wv_sc[:].rearrange("p a n -> p (a n)").bitcast(I32), 0)
+        for window in windows[1:]:
             nc.gpsimd.memset(window[:].bitcast(I32), 0)
 
         x_rows = xT.rearrange("(a p i) t -> p a i t", a=PASSES, i=PACK)

@@ -37,16 +37,13 @@ QUADRANT = 32
 SCALE_ROWS = 4
 SQUARE = 32
 SPREAD_PIECES = (slice(0, 2 * P), slice(2 * P, HALF), slice(HALF, J))
-PIECES = (slice(0, P), slice(P, HALF), slice(HALF, HALF + 2 * P), slice(HALF + 2 * P, J))
+HELD = 3 * P
+PIECES = (slice(0, P), slice(P, HALF), slice(HALF, J - HELD), slice(J - HELD, J))
 QUANTISED = PIECES[:2] + (slice(HALF, J),)
-SECOND_HALF_PIECES = range(2, 4)
 PAIRS = [slice(n * 2 * P, (n + 1) * 2 * P) for n in range(PLACE_TILES // 2)]
-PLANE_ORDER = (0, 1, 4, 2, 3, 5, 6, 7)
-EARLY_WORD_PART = slice(0, 1)
-LATE_WORD_PART = slice(1, PACK)
-LATE_PLANES = PACK - 1
-LATE_STEPS = (J, J + P)
-
+STEP = J + HELD - P
+PLANE_AT = {4: 0, 5: J, 6: J + STEP, 7: J + 2 * STEP}
+LAST_RUNS = {6: slice(J - HELD, J), 7: slice(HALF, J)}
 
 def tile_list_siluS_kernel(
     tc, xT, wgt, wk_words, wk_scales, wv_words, wv_scales, st, wgo, offs, offs2, out
@@ -73,11 +70,7 @@ def tile_list_siluS_kernel(
         planes = [keep.tile([P, T], F32, name=f"plane{q}", tag=f"plane{q}", align_bytes=BURST) for q in range(PLANES)]
         wk_codes = [keep.tile([P, N], U32, name=f"wk_codes{a}", align_bytes=BURST) for a in range(PASSES)]
         wv_codes = keep.tile([P, PASSES, 2 * N], U8, name="wv_codes", align_bytes=BURST)
-        late = keep.tile([P, HALF + LATE_PLANES * LATE_STEPS[1]], F32, name="late", tag="late", align_bytes=64)
-        late_half = [
-            late[:, h * HALF : h * HALF + LATE_PLANES * LATE_STEPS[h]].rearrange("p (i c) -> p i c", i=LATE_PLANES)
-            for h in range(HALVES)
-        ]
+        second_pass = keep.tile([P, J + P + 3 * STEP], F32, name="second_pass", tag="second_pass", align_bytes=64)
         st_first = [
             keep.tile([P, ROW_TILES, P], F32, name=f"st{t}", tag=f"st{t}", align_bytes=64)
             for t in range(PLACE_TILES // 2)
@@ -86,7 +79,7 @@ def tile_list_siluS_kernel(
         wgt_rows = keep.tile([P, 2, SQUARE], F32, name="wgt_rows", align_bytes=64)
         wgt_cols = keep.tile([P, 2, SQUARE], F32, name="wgt_cols", align_bytes=64)
         wgt_wide = shared.tile([P, T + 6 * P], F32, name="wgt_wide", offset=WINDOW_BYTES - BURST)
-        wgo_rows = keep.tile([P, P], F32, name="wgo_rows")
+        wgo_rows = keep.tile([P, P], F32, name="wgo_rows", tag="wgo_rows", align_bytes=64)
         wgo_t = keep.tile([P, P // 2], F32, name="wgo_t")
         ident = keep.tile([P, P], F32, name="ident")
         diagonal = keep.tile([P, P], F32, name="diagonal")
@@ -138,13 +131,12 @@ def tile_list_siluS_kernel(
             nc.gpsimd.memset(window[:].bitcast(I32), 0)
 
         x_rows = xT.rearrange("(a p i) t -> p a i t", a=PASSES, i=PACK)
-        for q in PLANE_ORDER:
+        for q in range(PLANES):
             nc.sync.dma_start(out=planes[q][:], in_=x_rows[:, q // PACK, q % PACK, :])
             if q == 0:
                 nc.sync.dma_start(pick[:], offs)
-            if q == PLANE_ORDER[1]:
+            if q == 5:
                 nc.sync.dma_start(out=wgo_rows[P // 2 : P, :], in_=group_runs(wgo).rearrange("u (t c) -> u t c", c=P))
-            if q == PLANE_ORDER[5]:
                 load_key_scales()
 
         def unit_parts(u):
@@ -183,46 +175,41 @@ def tile_list_siluS_kernel(
         nc.sync.dma_start(out=st_second[:], in_=st_rows[:, :, half_cols(1)])
 
         picked = keep.tile([P, PACK, J], F32, name="picked", align_bytes=64)
-        early = keep.tile([P, 1, J], F32, name="early")
         grouped_first = [
             keep.tile([P, HALF, PACK], BF16, name=f"grouped_first{h}", align_bytes=64) for h in range(HALVES)
         ]
-        last_gathers = HALF + (LATE_PLANES - 1) * LATE_STEPS[1]
         grouped_piece = [
-            late[:, last_gathers + P : last_gathers + 3 * P].bitcast(BF16).rearrange("p (c i) -> p c i", i=PACK)
-        ] + [
             keep.tile([P, c.stop - c.start, PACK], BF16, name=f"grouped_piece{n}", tag=f"grouped{n}", align_bytes=64)
-            for n, c in list(enumerate(QUANTISED))[1:]
+            for n, c in enumerate(QUANTISED)
         ]
         last_words = grouped_piece[-1][:].rearrange("p c i -> p (c i)").bitcast(F32).rearrange("p (c w) -> p c w", w=2)
-        wgo_head = last_words[:, 2 * P - 1 : 2 * P + 1, 1]
+        wgo_head = last_words[:, HALF - HELD - 1 : HALF - HELD + 1, 1]
         x_codes = {}
         x_sc = {}
 
-        def late_view(cols):
-            h = cols.start // HALF
-            return late_half[h][:, :, cols.start - h * HALF : cols.stop - h * HALF]
+        def column(q, j):
+            last = LAST_RUNS.get(q)
+            if last and j >= last.start:
+                return PLANE_AT[q] + P - (last.stop - j)
+            return PLANE_AT[q] + j
 
         def gather(q, cols=slice(0, J)):
-            a, i = divmod(q, PACK)
-            if a == 0:
-                dst = picked[:, i, cols]
-            elif i == 0:
-                dst = early[:, 0, cols]
-            elif i == 1:
-                dst = late[:, cols]
+            if q < PACK:
+                dst = picked[:, q, cols]
             else:
-                dst = late_view(cols)[:, i - 1, :]
+                dst = second_pass[:, column(q, cols.start) : column(q, cols.start) + cols.stop - cols.start]
             entries = pick[:, cols.start // GROUP : cols.stop // GROUP]
             nc.vector.tensor_tensor(dst, planes[q][:].indirect(entries), wgt_sb[:, cols], MULT)
 
-        def interleave_piece(piece, word_part):
-            cols = PIECES[piece]
-            src = early[:, :, cols] if word_part == EARLY_WORD_PART else late_view(cols)
-            whole = min(piece, len(QUANTISED) - 1)
-            first = QUANTISED[whole].start
-            dst = grouped_piece[whole][:, cols.start - first : cols.stop - first, word_part]
-            nc.scalar.copy(dst, src.rearrange("p i c -> p c i"))
+        def interleave(first, last, cols):
+            count = last - first + 1
+            start = column(first, cols.start)
+            step = column(first + 1, cols.start) - start
+            src = second_pass[:, start : start + count * step].rearrange("p (i c) -> p c i", i=count)
+            n = [c.start <= cols.start < c.stop for c in QUANTISED].index(True)
+            at = cols.start - QUANTISED[n].start
+            width = cols.stop - cols.start
+            nc.scalar.copy(grouped_piece[n][:, at : at + width, first - PACK : last - PACK + 1], src[:, 0:width])
 
         def quantise(key, src, codes_tag, scales_tag):
             width = src.shape[1]
@@ -351,7 +338,7 @@ def tile_list_siluS_kernel(
 
         def combine(u):
             if u == 0:
-                results[u] = keep.tile([P, HALF], F32, name="result0", tag="late", align_bytes=64)
+                results[u] = keep.tile([P, HALF], F32, name="result0", tag="second_pass", align_bytes=64)
                 for part in (slice(0, 2 * P), slice(2 * P, HALF)):
                     nc.vector.tensor_tensor(results[u][:, part], turned[u][:, part], gates[u][:, part], MULT)
                 return
@@ -366,34 +353,33 @@ def tile_list_siluS_kernel(
                 if places.stop == J:
                     nc.sync.dma_start(out=out[block(r), :], in_=windows[r][:])
 
-        place_output_weights()
-
-        for q in PLANE_ORDER[0:5]:
+        for q in range(PACK):
             gather(q)
-            if q == PACK:
-                for n in range(len(PIECES)):
-                    interleave_piece(n, EARLY_WORD_PART)
             if q % 2:
                 for h in range(HALVES):
                     src = picked[:, q - 1 : q + 1, half_cols(h)].rearrange("p i c -> p c i")
                     nc.scalar.copy(grouped_first[h][:, :, q - 1 : q + 1], src)
 
+        gather(4)
+        interleave(4, 4, PIECES[1])
         gather(5)
-        quantise((0, 0), grouped_first[0], "codes_00", "scales_00")
+        place_output_weights()
+        interleave(4, 5, PIECES[0])
+        interleave(4, 5, half_cols(1))
+        quantise((0, 0), grouped_first[0], "codes_00", "wgo_rows")
 
-        gather(6, half_cols(0))
-        gather(7, slice(0, 2 * P))
-        interleave_piece(0, LATE_WORD_PART)
-        gather(7, PAIRS[1])
+        gather(6, slice(0, J - HELD))
+        gather(7, PIECES[0])
+        interleave(6, 7, PIECES[0])
+        gather(7, PIECES[1])
         quantise((1, 0), grouped_piece[0], "codes_10", "scales_10")
-        gather(6, half_cols(1))
-        interleave_piece(1, LATE_WORD_PART)
+        interleave(5, 7, PIECES[1])
         sums_by_place(0)
         make_keys(0)
         scale_by_place(0)
-        for n in SECOND_HALF_PIECES:
-            gather(7, PIECES[n])
-            interleave_piece(n, LATE_WORD_PART)
+        for q, piece in ((7, PIECES[2]), (6, PIECES[3])):
+            gather(q, LAST_RUNS[q])
+            interleave(6, 7, piece)
         quantise((1, 1), grouped_piece[1], "codes_11", "scales_11")
         make_keys(1)
         sums_by_place(1)

@@ -137,7 +137,6 @@ def tile_list_siluS_kernel(
                 nc.sync.dma_start(pick[:], offs)
             if q == 5:
                 nc.sync.dma_start(out=wgo_rows[P // 2 : P, :], in_=group_runs(wgo).rearrange("u (t c) -> u t c", c=P))
-                load_key_scales()
 
         def unit_parts(u):
             if u < PLACE_UNITS:
@@ -170,6 +169,8 @@ def tile_list_siluS_kernel(
             nc.sync.dma_start(out=wk_codes[a][:].bitcast(I32), in_=words.bitcast(I32))
         for t, tile in enumerate(st_first):
             nc.sync.dma_start(out=tile[:], in_=st_rows[:, :, block(t)])
+            if t == 0:
+                load_key_scales()
             if t == 1:
                 nc.sync.dma_start(place[:], offs2)
         nc.sync.dma_start(out=st_second[:], in_=st_rows[:, :, half_cols(1)])
@@ -296,7 +297,8 @@ def tile_list_siluS_kernel(
 
         def sums_by_place(t):
             sums[t] = next_bank("ve", first_sum_banks.get(t))
-            for a in range(PASSES):
+            order = range(PASSES) if t == 0 else range(PASSES)[::-1]
+            for a in order:
                 lhsT, lhsT_scale = x_operand(a, block(t))
                 nc.tensor.matmul_mx(
                     out=sums[t][:],
@@ -304,8 +306,8 @@ def tile_list_siluS_kernel(
                     lhsT_scale=lhsT_scale,
                     rhs=wv_codes[:, a, :].bitcast(FP4X4),
                     rhs_scale=wv_sc[:, a, :],
-                    start=(a == 0),
-                    stop=(a == PASSES - 1),
+                    start=(a == order[0]),
+                    stop=(a == order[-1]),
                 )
 
         scaled_slots = ["plane0", "plane1", "st1", "st2", "gate1", "st3", "gate2", "gate3"]
@@ -380,7 +382,7 @@ def tile_list_siluS_kernel(
         for q, piece in ((7, PIECES[2]), (6, PIECES[3])):
             gather(q, LAST_RUNS[q])
             interleave(6, 7, piece)
-        quantise((1, 1), grouped_piece[1], "codes_11", "scales_11")
+        quantise((1, 1), grouped_piece[1], "codes_11", "scales_10")
         make_keys(1)
         sums_by_place(1)
         make_match(0)
@@ -388,7 +390,7 @@ def tile_list_siluS_kernel(
         turn_values(0)
         copy_keys(1)
         quantise((0, 1), grouped_first[1], "codes_10", "scales_01")
-        quantise((1, 2), grouped_piece[2], "codes_12", "scales_10")
+        quantise((1, 2), grouped_piece[2], "codes_12", "grouped1")
         combine(0)
         make_match(1)
         scale_by_place(1)

from contextlib import ExitStack

import concourse.mybir as mybir

K, N, T, J = 1024, 512, 2048, 1024
FLOPS = 2 * 2 * K * N * J

F32 = mybir.dt.float32
BF16 = mybir.dt.bfloat16
I32 = mybir.dt.int32
U32 = mybir.dt.uint32
U16 = mybir.dt.uint16
U8 = mybir.dt.uint8
FP8X4 = mybir.dt.float8_e4m3fn_x4
FP4X4 = mybir.dt.float4_e2m1fn_x4
MULT = mybir.AluOpType.mult
SILU = mybir.ActivationFunctionType.Silu
COPY = mybir.ActivationFunctionType.Copy

P = 128
WINDOW_BYTES = 4 * T
BURST = 256
PACK = 4
PASSES = K // (P * PACK)
PLANES = PASSES * PACK
HALF = 512
HALVES = J // HALF
ROW_TILES = N // P
GROUPS = 8
GROUP = P // GROUPS
PLACE_TILES = J // P
PLACE_UNITS = 5
UNITS = PLACE_UNITS + ROW_TILES
SPLIT_RESULTS = 3
RING_BANKS = 5
QUADRANT = 32
SCALE_ROWS = 4
SQUARE = 32
SPREAD_PIECES = (slice(0, 2 * P), slice(2 * P, HALF), slice(HALF, J))
HELD = 3 * P
PIECES = (slice(0, P), slice(P, HALF), slice(HALF, J - HELD), slice(J - HELD, J))
QUANTISED = PIECES[:2] + (slice(HALF, J),)
PAIRS = [slice(n * 2 * P, (n + 1) * 2 * P) for n in range(PLACE_TILES // 2)]
STEP = J + HELD - P
PLANE_AT = {4: 0, 5: J, 6: J + STEP, 7: J + 2 * STEP}
LAST_RUNS = {6: slice(J - HELD, J), 7: slice(HALF, J)}

def tile_list_siluS_kernel(
    tc, xT, wgt, wk_words, wk_scales, wv_words, wv_scales, st, wgo, offs, offs2, out
):
    nc = tc.nc
    with ExitStack() as ctx:
        keep = ctx.enter_context(tc.tile_pool(name="keep", bufs=1))
        ring = ctx.enter_context(tc.tile_pool(name="ring", bufs=3))
        shared = ctx.enter_context(tc.tile_pool(name="shared", bufs=1))
        psum_ring = ctx.enter_context(tc.psum_pool(name="psum_ring", bufs=1))

        def half_cols(h):
            return slice(h * HALF, (h + 1) * HALF)

        def tile_col(t):
            return (t + PLACE_TILES // 2) % PLACE_TILES

        def block(i):
            return slice(i * P, (i + 1) * P)

        pick = keep.tile([P, J // GROUP], U16, name="pick")
        place = keep.tile([P, J // GROUP], U16, name="place")
        wgt_sb = keep.tile([P, J], F32, name="wgt_sb", align_bytes=64)
        planes = [keep.tile([P, T], F32, name=f"plane{q}", tag=f"plane{q}", align_bytes=BURST) for q in range(PLANES)]
        wk_codes = [keep.tile([P, N], U32, name=f"wk_codes{a}", align_bytes=BURST) for a in range(PASSES)]
        wv_codes = keep.tile([P, PASSES, 2 * N], U8, name="wv_codes", align_bytes=BURST)
        second_pass = keep.tile([P, J + P + 3 * STEP], F32, name="second_pass", tag="second_pass", align_bytes=64)
        st_first = [
            keep.tile([P, ROW_TILES, P], F32, name=f"st{t}", tag=f"st{t}", align_bytes=64)
            for t in range(PLACE_TILES // 2)
        ]
        st_second = keep.tile([P, ROW_TILES, HALF], F32, name="st_second", align_bytes=BURST)
        wgt_rows = keep.tile([P, 2, SQUARE], F32, name="wgt_rows", align_bytes=64)
        wgt_cols = keep.tile([P, 2, SQUARE], F32, name="wgt_cols", align_bytes=64)
        wgt_wide = shared.tile([P, T + 6 * P], F32, name="wgt_wide", offset=WINDOW_BYTES - BURST)
        wgo_rows = keep.tile([P, P], F32, name="wgo_rows", tag="wgo_rows", align_bytes=64)
        wgo_t = keep.tile([P, P // 2], F32, name="wgo_t")
        ident = keep.tile([P, P], F32, name="ident")
        diagonal = keep.tile([P, P], F32, name="diagonal")
        wk_sc = keep.tile([P, N], U8, name="wk_sc", align_bytes=64)
        wv_sc = shared.tile([P, PASSES, N], U8, name="wv_sc", offset=WINDOW_BYTES)
        windows = [keep.tile([P, T], F32, name=f"window{r}", align_bytes=BURST) for r in range(1)] + [
            shared.tile([P, T], F32, name=f"window{r}", align_bytes=BURST, offset=at)
            for r, at in ((1, 0), (2, WINDOW_BYTES + 4 * BURST), (3, 2 * WINDOW_BYTES + 4 * BURST))
        ]
        warm = keep.tile([P, 2], F32, name="warm")

        nc.vector.memset(warm[:, 0:1], 0.0)
        nc.scalar.activation(warm[:, 1:2], warm[:, 0:1], SILU)
        nc.gpsimd.iota(diagonal[:], [[1, P]], base=0, channel_multiplier=-1, allow_small_or_imprecise_dtypes=True)
        nc.vector.memset(wgo_rows[0 : P // 2, :], 0.0)
        nc.vector.memset(wk_sc[:].bitcast(I32), 0)
        nc.vector.memset(windows[0][:].bitcast(I32), 0)

        def load_key_scales():
            for quad in range(P // QUADRANT):
                rows = wk_scales[:, quad * SCALE_ROWS : (quad + 1) * SCALE_ROWS, :].bitcast(I32)
                first = QUADRANT * quad + SCALE_ROWS
                nc.sync.dma_start(out=wk_sc[first : first + PASSES * SCALE_ROWS, :].bitcast(I32), in_=rows)

        def group_runs(weights):
            step = GROUP // 2 * J - HALF
            runs = weights.rearrange("p j -> (p j)")[step : step * (2 * GROUPS + 1)].rearrange("(u x) -> u x", x=step)
            return runs[:, 0:HALF]

        nc.sync.dma_start(
            out=wgt_rows[:].rearrange("p b r -> p (b r)"),
            in_=group_runs(wgt).rearrange("u (m c) -> u m c", c=2 * SQUARE),
        )
        for b in range(2):
            nc.vector.transpose(wgt_cols[:, b, :], wgt_rows[:, b, :])
        nc.vector.tensor_scalar(ident[:], diagonal[:], 0.0, None, mybir.AluOpType.is_equal)
        by_run = wgt_cols[:].rearrange("p b (h m o) -> p m b h o", h=2, o=1)
        for cols in SPREAD_PIECES:
            repeat = nc.scalar.copy if cols.stop == J else nc.vector.tensor_copy
            first = (cols.start // (2 * SQUARE) + GROUP // 2) % GROUP
            count = (cols.stop - cols.start) // (2 * SQUARE)
            dst = wgt_wide[:, cols].rearrange("p (m b h s) -> p m b h s", b=2, h=2, s=GROUP)
            repeat(dst, by_run[:, first : first + count].to_broadcast([P, count, 2, 2, GROUP]))
        for cols in SPREAD_PIECES:
            nc.vector.transpose(wgt_sb[:, cols], wgt_wide[:, cols])

        nc.gpsimd.memset(wv_sc[:].rearrange("p a n -> p (a n)").bitcast(I32), 0)
        for window in windows[1:]:
            nc.gpsimd.memset(window[:].bitcast(I32), 0)

        x_rows = xT.rearrange("(a p i) t -> p a i t", a=PASSES, i=PACK)
        for q in range(PLANES):
            nc.sync.dma_start(out=planes[q][:], in_=x_rows[:, q // PACK, q % PACK, :])
            if q == 0:
                nc.sync.dma_start(pick[:], offs)
            if q == 5:
                nc.sync.dma_start(out=wgo_rows[P // 2 : P, :], in_=group_runs(wgo).rearrange("u (t c) -> u t c", c=P))

        def unit_parts(u):
            if u < PLACE_UNITS:
                rows = ROW_TILES - 1 if u == PLACE_UNITS - 1 else ROW_TILES
                return [(block(r), r, block(u)) for r in range(rows)]
            first = (PLACE_UNITS - 1 if u == UNITS - 1 else PLACE_UNITS) * P
            return [(slice(0, J - first), u - PLACE_UNITS, slice(first, J))]

        def unit_cols(u):
            return slice(0, unit_parts(u)[-1][0].stop)

        st_rows = st.rearrange("(r p) j -> p r j", p=P)

        def state(u):
            parts = unit_parts(u)
            span, first, places = parts[0]
            if places.start < HALF:
                return st_first[u][:]
            return st_second[:, first : first + len(parts), places.start - HALF : places.stop - HALF]

        def by_part(ap, u):
            return ap[:, unit_cols(u)].rearrange("p (r j) -> p r j", r=len(unit_parts(u)))

        wv_rows = wv_scales.rearrange("a (q r) n -> r q a n", r=SCALE_ROWS)
        for r in range(SCALE_ROWS):
            nc.sync.dma_start(out=wv_sc[r:P:QUADRANT, :, :].bitcast(I32), in_=wv_rows[r].bitcast(I32))
        nc.sync.dma_start(out=wv_codes[:].bitcast(I32), in_=wv_words.rearrange("a p n -> p a n").bitcast(I32))
        for a in reversed(range(PASSES)):
            words = wk_words[a].rearrange("p n i -> p (n i)")
            nc.sync.dma_start(out=wk_codes[a][:].bitcast(I32), in_=words.bitcast(I32))
        for t, tile in enumerate(st_first):
            nc.sync.dma_start(out=tile[:], in_=st_rows[:, :, block(t)])
            if t == 0:
                load_key_scales()
            if t == 1:
                nc.sync.dma_start(place[:], offs2)
        nc.sync.dma_start(out=st_second[:], in_=st_rows[:, :, half_cols(1)])

        picked = keep.tile([P, PACK, J], F32, name="picked", align_bytes=64)
        grouped_first = [
            keep.tile([P, HALF, PACK], BF16, name=f"grouped_first{h}", align_bytes=64) for h in range(HALVES)
        ]
        grouped_piece = [
            keep.tile([P, c.stop - c.start, PACK], BF16, name=f"grouped_piece{n}", tag=f"grouped{n}", align_bytes=64)
            for n, c in enumerate(QUANTISED)
        ]
        last_words = grouped_piece[-1][:].rearrange("p c i -> p (c i)").bitcast(F32).rearrange("p (c w) -> p c w", w=2)
        wgo_head = last_words[:, HALF - HELD - 1 : HALF - HELD + 1, 1]
        x_codes = {}
        x_sc = {}

        def column(q, j):
            last = LAST_RUNS.get(q)
            if last and j >= last.start:
                return PLANE_AT[q] + P - (last.stop - j)
            return PLANE_AT[q] + j

        def gather(q, cols=slice(0, J)):
            if q < PACK:
                dst = picked[:, q, cols]
            else:
                dst = second_pass[:, column(q, cols.start) : column(q, cols.start) + cols.stop - cols.start]
            entries = pick[:, cols.start // GROUP : cols.stop // GROUP]
            nc.vector.tensor_tensor(dst, planes[q][:].indirect(entries), wgt_sb[:, cols], MULT)

        def interleave(first, last, cols):
            count = last - first + 1
            start = column(first, cols.start)
            step = column(first + 1, cols.start) - start
            src = second_pass[:, start : start + count * step].rearrange("p (i c) -> p c i", i=count)
            n = [c.start <= cols.start < c.stop for c in QUANTISED].index(True)
            at = cols.start - QUANTISED[n].start
            width = cols.stop - cols.start
            nc.scalar.copy(grouped_piece[n][:, at : at + width, first - PACK : last - PACK + 1], src[:, 0:width])

        def quantise(key, src, codes_tag, scales_tag):
            width = src.shape[1]
            x_codes[key] = keep.tile([P, width], U32, name=f"x_codes_{key[0]}_{key[1]}", tag=codes_tag, align_bytes=64)
            x_sc[key] = keep.tile([P, width], U8, name=f"x_sc_{key[0]}_{key[1]}", tag=scales_tag, align_bytes=64)
            nc.vector.quantize_mx(
                out=x_codes[key][:].bitcast(FP8X4), scales=x_sc[key][:], in_=src[:].rearrange("p c i -> p (c i)")
            )

        def x_operand(a, places):
            pieces = [half_cols(h) for h in range(HALVES)] if a == 0 else QUANTISED
            n = [c.start <= places.start < c.stop for c in pieces].index(True)
            cols = slice(places.start - pieces[n].start, places.stop - pieces[n].start)
            return x_codes[a, n][:, cols].bitcast(FP8X4), x_sc[a, n][:, cols]

        keys = {}
        key_sb = {}
        matches = {}
        gates = {}
        sums = {}
        scaled = {}
        turned = {}
        values = {}
        results = {}

        taken = []

        def next_bank(name, fixed=None):
            if fixed is None:
                fixed = len(taken) % RING_BANKS
                taken.append(name)
            return psum_ring.tile([P, HALF], F32, name=name, tag=f"bank{fixed}")

        first_key_banks = {0: 1, 1: 4}
        first_sum_banks = {0: 2, 1: 2}

        def make_keys(u):
            keys[u] = next_bank("ke", first_key_banks.get(u))
            runs = []
            for span, r, places in unit_parts(u):
                for c in PAIRS:
                    start, stop = max(c.start, places.start), min(c.stop, places.stop)
                    if start < stop:
                        first = span.start + start - places.start
                        runs.append((slice(first, first + stop - start), r, slice(start, stop)))
            steps = [(a, run) for a in range(PASSES) for run in runs]
            for n, (a, (span, r, places)) in enumerate(steps):
                rhs, rhs_scale = x_operand(a, places)
                nc.tensor.matmul_mx(
                    out=keys[u][:, span],
                    lhsT=wk_codes[a][:, block(r)].bitcast(FP8X4),
                    lhsT_scale=wk_sc[SCALE_ROWS * (a + 1) : P, block(r)],
                    rhs=rhs,
                    rhs_scale=rhs_scale,
                    start=(n == 0),
                    stop=(n == len(steps) - 1),
                )

        def copy_keys(u):
            key_sb[u] = keep.tile([P, HALF], F32, name=f"key{u}", tag="st0" if u % 2 else "key_even", align_bytes=64)
            nc.scalar.copy(key_sb[u][:, unit_cols(u)], keys[u][:, unit_cols(u)])

        def make_match(u):
            if u == 0:
                matches[u] = keep.tile([P, HALF], F32, name="match0", align_bytes=64)
                nc.vector.tensor_tensor(by_part(matches[u], u), by_part(keys[u], u), state(u), MULT)
                return
            tag = {1: f"grouped{len(QUANTISED) - 1}", 2: "gate0"}.get(u, f"value{u - 2}")
            matches[u] = keep.tile([P, HALF], F32, name=f"match{u}", tag=tag, align_bytes=64)
            nc.gpsimd.tensor_tensor(by_part(matches[u], u), by_part(key_sb[u], u), state(u), MULT)

        def make_gate(u):
            if u < 4:
                gates[u] = keep.tile([P, HALF], F32, name=f"gate{u}", tag=f"gate{u}", align_bytes=64)
            else:
                gates[u] = ring.tile([P, HALF], F32, name="gate")
            nc.scalar.activation(gates[u][:, unit_cols(u)], matches[u][:, unit_cols(u)], SILU)

        def place_output_weights():
            wgo_by_place = next_bank("wgo_by_place", 0)
            nc.tensor.transpose(wgo_by_place[:, 0:P], wgo_rows[:], ident[:])
            nc.scalar.copy(wgo_head, wgo_by_place[:, P // 2 + tile_col(0) : P // 2 + 2 * PLACE_TILES : PLACE_TILES])
            nc.scalar.copy(wgo_t[:], wgo_by_place[:, P // 2 : P])

        def sums_by_place(t):
            sums[t] = next_bank("ve", first_sum_banks.get(t))
            order = range(PASSES) if t == 0 else range(PASSES)[::-1]
            for a in order:
                lhsT, lhsT_scale = x_operand(a, block(t))
                nc.tensor.matmul_mx(
                    out=sums[t][:],
                    lhsT=lhsT,
                    lhsT_scale=lhsT_scale,
                    rhs=wv_codes[:, a, :].bitcast(FP4X4),
                    rhs_scale=wv_sc[:, a, :],
                    start=(a == order[0]),
                    stop=(a == order[-1]),
                )

        scaled_slots = ["plane0", "plane1", "st1", "st2", "gate1", "st3", "gate2", "gate3"]

        def scale_by_place(t):
            if t not in sums:
                sums_by_place(t)
            align = BURST if t < 2 else 64
            scaled[t] = keep.tile([P, N], F32, name=f"scaled{t}", tag=scaled_slots[t], align_bytes=align)
            src = sums[t][:].rearrange("p (r g c) -> p r g c", g=GROUPS, c=GROUP)
            dst = scaled[t][:].rearrange("p (r g c) -> p r g c", g=GROUPS, c=GROUP)
            for g in range(GROUPS):
                col = g * PLACE_TILES + tile_col(t)
                scale = wgo_head[:, g : g + 1] if t == 0 and g < 2 else wgo_t[:, col : col + 1]
                nc.scalar.activation(dst[:, :, g, :], src[:, :, g, :], COPY, scale=scale)

        def turn_values(u):
            turned[u] = next_bank("turned", first_key_banks.get(u))
            for span, r, places in unit_parts(u):
                for n in range((places.stop - places.start) // P):
                    src = scaled[places.start // P + n][:, block(r)]
                    nc.tensor.transpose(turned[u][:, block(span.start // P + n)], src, ident[:])

        first_block_apart = (slice(0, P), slice(P, HALF))

        def copy_values(u):
            values[u] = keep.tile([P, HALF], F32, name=f"value{u}", tag=f"value{u}", align_bytes=64)
            for part in first_block_apart if u == 1 else (unit_cols(u),):
                nc.scalar.copy(values[u][:, part], turned[u][:, part])

        def combine(u):
            if u == 0:
                results[u] = keep.tile([P, HALF], F32, name="result0", tag="second_pass", align_bytes=64)
                for part in (slice(0, 2 * P), slice(2 * P, HALF)):
                    nc.vector.tensor_tensor(results[u][:, part], turned[u][:, part], gates[u][:, part], MULT)
                return
            results[u] = ring.tile([P, HALF], F32, name="result")
            for part in first_block_apart if u <= SPLIT_RESULTS else (unit_cols(u),):
                nc.gpsimd.tensor_tensor(results[u][:, part], gates[u][:, part], values[u][:, part], MULT)

        def scatter(u):
            for span, r, places in unit_parts(u):
                entries = place[:, places.start // GROUP : places.stop // GROUP]
                nc.vector.tensor_copy(windows[r][:].indirect(entries), results[u][:, span])
                if places.stop == J:
                    nc.sync.dma_start(out=out[block(r), :], in_=windows[r][:])

        for q in range(PACK):
            gather(q)
            if q % 2:
                for h in range(HALVES):
                    src = picked[:, q - 1 : q + 1, half_cols(h)].rearrange("p i c -> p c i")
                    nc.scalar.copy(grouped_first[h][:, :, q - 1 : q + 1], src)

        gather(4)
        interleave(4, 4, PIECES[1])
        gather(5)
        place_output_weights()
        interleave(4, 5, PIECES[0])
        interleave(4, 5, half_cols(1))
        quantise((0, 0), grouped_first[0], "codes_00", "wgo_rows")

        gather(6, slice(0, J - HELD))
        gather(7, PIECES[0])
        interleave(6, 7, PIECES[0])
        gather(7, PIECES[1])
        quantise((1, 0), grouped_piece[0], "codes_10", "scales_10")
        interleave(5, 7, PIECES[1])
        sums_by_place(0)
        make_keys(0)
        scale_by_place(0)
        for q, piece in ((7, PIECES[2]), (6, PIECES[3])):
            gather(q, LAST_RUNS[q])
            interleave(6, 7, piece)
        quantise((1, 1), grouped_piece[1], "codes_11", "scales_10")
        make_keys(1)
        sums_by_place(1)
        make_match(0)
        make_gate(0)
        turn_values(0)
        copy_keys(1)
        quantise((0, 1), grouped_first[1], "codes_10", "scales_01")
        quantise((1, 2), grouped_piece[2], "codes_12", "grouped1")
        combine(0)
        make_match(1)
        scale_by_place(1)
        turn_values(1)
        make_keys(2)
        copy_keys(2)
        copy_values(1)
        make_gate(1)

        for u in range(UNITS):
            if u + 2 < UNITS:
                make_match(u + 2)
            if u + 1 < UNITS:
                combine(u + 1)
            scatter(u)
            if u + 3 < UNITS:
                make_keys(u + 3)
                copy_keys(u + 3)
            if u + 2 < UNITS:
                places = unit_parts(u + 2)[0][2]
                for t in range(places.start // P, places.stop // P):
                    if t not in scaled:
                        scale_by_place(t)
                make_gate(u + 2)
                turn_values(u + 2)
                copy_values(u + 2)
